import numpy as np
import ml_dtypes


def mxq(x, axis, fmt="e4m3"):
    dtype, down = {"e4m3": (ml_dtypes.float8_e4m3fn, 7), "e5m2": (ml_dtypes.float8_e5m2, 14)}[fmt]
    v = np.moveaxis(np.asarray(x, np.float32).astype(ml_dtypes.bfloat16).astype(np.float64), axis, -1)
    blocks = v.reshape(v.shape[:-1] + (-1, 32))
    amax = np.abs(blocks).max(-1, keepdims=True)
    byte = np.maximum(np.where(amax > 0, np.frexp(amax)[1] - 1 + 127, 0) - down, 1)
    scale = np.exp2(byte - 127.0)
    codes = (blocks / scale).astype(np.float32).astype(dtype).astype(np.float64)
    return np.moveaxis((codes * scale).reshape(v.shape), -1, axis)


WIDE = False


def mx_kscale(k):
    if not WIDE:
        return np.ones(k)
    levels = np.array([10, -10, 5, -5, 0])
    if k % 512:
        return np.exp2(np.random.permutation(np.resize(levels, k // 32))).repeat(32)
    a = np.empty((k // 512, 16))
    for p in range(k // 512):
        a[p, :8] = np.random.permutation(np.resize(levels, 8))
        for g in range(8):
            far = levels[np.abs(levels - a[p, g]) >= 10]
            a[p, g + 8] = far[np.random.randint(len(far))]
    return np.exp2(a.ravel()).repeat(32)


BF16 = ml_dtypes.bfloat16


def bf(x):
    return np.asarray(x, np.float32).astype(BF16)


def f64(x):
    return np.asarray(x).astype(np.float64)

E4M3FN = np.array([(-1.0 if i & 128 else 1.0) * ((1.0 + (i & 7) / 8.0) * 2.0 ** (((i >> 3) & 15) - 7) if i & 120 else (i & 7) * 2.0 ** -9) for i in range(256)])


def e4m3fn_bytes(y):
    return np.clip(np.asarray(y, np.float64), -448.0, 448.0).astype(np.float32).astype(ml_dtypes.float8_e4m3fn).view(np.uint8)


def e4m3fn_values(b):
    return E4M3FN[b]


N, B, E = 1024, 128, 16


def setup_inputs():
    s = mx_kscale(N)
    a, c = np.random.standard_normal((2, E, N))
    P = sum(v[:, None] * v for v in a) / E * s[:, None] * s
    F = np.random.standard_normal((N, N)) / np.sqrt(N) / s
    Q = 0.3 * sum(v[:, None] * v for v in c) / E
    P_scale = (np.abs(P).reshape(N, N // B, B).max(axis=2) / 448.0).astype(np.float32)
    F_scale = (np.abs(F).reshape(N // B, B, N // B, B).max(axis=(1, 3)) / 448.0).astype(np.float32)
    return {"P_bytes": e4m3fn_bytes(P / np.repeat(f64(P_scale), B, axis=1)),
            "P_scale": P_scale,
            "F_bytes": e4m3fn_bytes(F / np.repeat(np.repeat(f64(F_scale), B, axis=0), B, axis=1)),
            "F_scale": F_scale,
            "g": bf(1 + 0.1 * np.random.standard_normal(N)),
            "Q": bf(Q)}


def reference(P_bytes, P_scale, F_bytes, F_scale, g, Q):
    P = e4m3fn_values(P_bytes) * np.repeat(f64(P_scale), B, axis=1)
    F = e4m3fn_values(F_bytes) * np.repeat(np.repeat(f64(F_scale), B, axis=0), B, axis=1)
    gain = f64(g)
    fq = mxq(F, 1, "e4m3")
    h = (mxq(P, 1, "e4m3") @ fq.T) * gain
    y = fq @ mxq(h, 0, "e4m3")
    return y * gain[:, None] + f64(Q)

@@ -1,0 +1,271 @@
+from contextlib import ExitStack
+
+import concourse.mybir as mybir
+from concourse.masks import make_identity
+
+N = 1024
+P = 128
+FLOPS = 2 * 2 * N * N * N
+
+F32 = mybir.dt.float32
+BF16 = mybir.dt.bfloat16
+U32 = mybir.dt.uint32
+U8 = mybir.dt.uint8
+FP8 = mybir.dt.float8_e4m3fn
+FP8X4 = mybir.dt.float8_e4m3fn_x4
+MULT = mybir.AluOpType.mult
+ADD = mybir.AluOpType.add
+COPY = mybir.ActivationFunctionType.Copy
+
+
+def tile_kalman_predicted_covariance_d2_kernel(tc, P_bytes, P_scale, F_bytes, F_scale, g, Q, out):
+    nc = tc.nc
+    with ExitStack() as ctx:
+        keep = ctx.enter_context(tc.tile_pool(name="keep", bufs=1))
+        psum = ctx.enter_context(tc.psum_pool(name="psum", bufs=8))
+        ctx.enter_context(tc.manual_schedule())
+
+
+        order = [("P", 0), ("P", 1), ("P", 2), ("P", 3), ("F", 0), ("F", 1), ("F", 2), ("F", 3)]
+        order += [("P", 4), ("P", 5), ("P", 6), ("P", 7), ("F", 4), ("F", 5), ("F", 6), ("F", 7)]
+        on_scalar = [("P", 1), ("F", 1), ("P", 5), ("F", 7)]
+        on_gpsimd = []
+
+        p_scale = keep.tile([P, 2, 32], F32, name="p_scale")
+        nc.scalar.dma_start(out=p_scale[:], in_=P_scale.rearrange("(g m t) c -> m g (t c)", g=2, t=4))
+        f_scale = keep.tile([P, 64], F32, name="f_scale")
+        nc.scalar.dma_start(out=f_scale[:], in_=F_scale.rearrange("b c -> (b c)").partition_broadcast(P))
+        p_rows = P_bytes.rearrange("(g m t) j -> g m t j", g=2, t=4)
+        f_rows = F_bytes.rearrange("(b p) j -> p b j", p=P)
+        raw = {}
+        scale = {}
+        for i, n in [(0, 1), (1, 1)] + [(i, 2) for i in range(2, 16, 2)]:
+            kind, b = order[i]
+            part = keep.tile([P, n, N], U8, name="bytes_%s%d" % (kind, b))
+            rows = p_rows[b // 4][:, b % 4 : b % 4 + n, :] if kind == "P" else f_rows[:, b : b + n, :]
+            nc.sync.dma_start(out=part[:], in_=rows)
+            for j in range(n):
+                raw[order[i + j]] = part[:, j, :]
+        for b in range(8):
+            scale[("P", b)] = p_scale[:, b // 4, 8 * (b % 4) : 8 * (b % 4) + 8]
+            scale[("F", b)] = f_scale[:, 8 * b : 8 * b + 8]
+        q_rows = Q.rearrange("(b p) n -> p b n", p=P)
+        q_tiles = []
+        for h in range(4):
+            qt = keep.tile([P, 2, N], BF16, name="q%d" % h)
+            nc.sync.dma_start(out=qt[:], in_=q_rows[:, 2 * h : 2 * h + 2, :])
+            q_tiles.append(qt)
+            if h == 0:
+                g_rows = keep.tile([P, N], BF16, name="g_rows")
+                nc.sync.dma_start(out=g_rows[:], in_=g.partition_broadcast(P))
+
+        ident = keep.tile([P, P], F32, name="ident")
+        make_identity(nc, ident[:])
+        first = keep.tile([P, 1], BF16, name="first")
+        nc.gpsimd.tensor_copy(out=first[:], in_=ident[:, 0:1])
+
+        codes = {}
+        c = keep.tile([P, 8, 2, P], U32, name="codes_P", align_bytes=256)
+        s = keep.tile([P, 8, 2, P], U8, name="sc_P", align_bytes=256)
+        codes["P"] = (c, s)
+        c = keep.tile([P, 2, 2, 512], U32, name="codes_F", align_bytes=256)
+        s = keep.tile([P, 2, 2, 512], U8, name="sc_F", align_bytes=256)
+        codes["F"] = (c, s)
+        h_codes = {}
+        for gi in range(2):
+            for nh in range(2):
+                hc = keep.tile([P, 512], U32, name="h_codes%d%d" % (gi, nh), align_bytes=256)
+                hs = keep.tile([P, 512], U8, name="h_sc%d%d" % (gi, nh), align_bytes=256)
+                h_codes[(gi, nh)] = (hc, hs)
+
+        wide = {}
+        banks = {}
+        grouped = {}
+        hg = {}
+        ht = {}
+
+        def widen(x):
+            w = keep.tile([P, N], BF16, name="wide_%s%d" % x, align_bytes=64)
+            wide[x] = w
+            for c in range(8):
+                src = raw[x][:, P * c : P * c + P].bitcast(FP8)
+                col = scale[x][:, c : c + 1]
+                if x in on_scalar:
+                    nc.scalar.activation(out=w[:, P * c : P * c + P], in_=src, func=COPY, scale=col)
+                else:
+                    nc.vector.tensor_scalar(out=w[:, P * c : P * c + P], in0=src, scalar1=col, scalar2=None, op0=MULT)
+
+        def turn(x):
+            words = wide[x][:].bitcast(F32)
+            bank = psum.tile([P, 2, 2, P], F32, name="bank", tag="bank")
+            banks[x] = bank
+            for k in range(2):
+                for u in range(2):
+                    w = words[:, 256 * k + u : 256 * k + 256 : 2]
+                    nc.tensor.transpose(bank[:, k, u, :], w, ident[:])
+
+        def empty(x):
+            kind, b = x
+            if kind == "P":
+                if b % 2 == 0:
+                    gr = keep.tile([P, 2, 2, 512], BF16, name="grouped_P%d" % b, align_bytes=64)
+                    grouped[("P", b // 2)] = gr
+                dst = grouped[("P", b // 2)][:, b % 2, :, :]
+            else:
+                if b % 4 == 0:
+                    gr = keep.tile([P, 2, 4, 512], BF16, name="grouped_F%d" % b, align_bytes=64)
+                    grouped[("F", b // 4)] = gr
+                dst = grouped[("F", b // 4)][:, :, b % 4, :]
+            nc.scalar.copy(
+                out=dst.bitcast(F32).rearrange("p k (r u) -> p k r u", u=2),
+                in_=banks[x][:].rearrange("p k u r -> p k r u"),
+            )
+
+        def quant_p(pair):
+            c, s = codes["P"]
+            b = 2 * pair
+            nc.vector.quantize_mx(
+                out=c[:, b : b + 2, :, :].rearrange("p b k m -> p (b k m)").bitcast(FP8X4),
+                scales=s[:, b : b + 2, :, :].rearrange("p b k m -> p (b k m)"),
+                in_=grouped[("P", pair)][:].rearrange("p b k c -> p (b k c)"),
+            )
+
+        def quant_f(nh, k):
+            c, s = codes["F"]
+            nc.vector.quantize_mx(
+                out=c[:, nh, k, :].bitcast(FP8X4),
+                scales=s[:, nh, k, :],
+                in_=grouped[("F", nh)][:, k, :, :].rearrange("p b c -> p (b c)"),
+            )
+
+        def first_product(gi, nh, t):
+            bank = psum.tile([P, 512], F32, name="bank", tag="bank")
+            banks[(gi, nh, t)] = bank
+            pc, ps = codes["P"]
+            fc, fs = codes["F"]
+            for k in range(2):
+                nc.tensor.matmul_mx(
+                    out=bank[:],
+                    lhsT=pc[:, 4 * gi + t, k, :].bitcast(FP8X4),
+                    lhsT_scale=ps[:, 4 * gi + t, k, :],
+                    rhs=fc[:, nh, k, :].bitcast(FP8X4),
+                    rhs_scale=fs[:, nh, k, :],
+                    start=(k == 0),
+                    stop=(k == 1),
+                )
+
+        def gain_h(gi, nh, t):
+            if t == 0:
+                tile_ht = keep.tile([P, 4, 512], BF16, name="ht_%d%d" % (gi, nh), align_bytes=64)
+                ht[(gi, nh)] = tile_ht
+            nc.vector.tensor_tensor(
+                out=ht[(gi, nh)][:, t, :],
+                in0=banks[(gi, nh, t)][:],
+                in1=g_rows[:, 512 * nh : 512 * nh + 512],
+                op=MULT,
+            )
+
+        def interleave_h(gi, nh, j):
+            tile_hg = keep.tile([P, 256, 4], BF16, name="hg_%d%d%d" % (gi, nh, j), align_bytes=64)
+            hg[(gi, nh, j)] = tile_hg
+            nc.scalar.copy(
+                out=tile_hg[:].rearrange("p (c i) t -> p c t i", i=4),
+                in_=ht[(gi, nh)][:, :, 256 * j : 256 * j + 256].rearrange("p t (c i) -> p c t i", i=4),
+            )
+
+        def quant_h(gi, nh, j):
+            c, s = h_codes[(gi, nh)]
+            nc.vector.quantize_mx(
+                out=c[:, 256 * j : 256 * j + 256].bitcast(FP8X4),
+                scales=s[:, 256 * j : 256 * j + 256],
+                in_=hg[(gi, nh, j)][:].rearrange("p n t -> p (n t)"),
+            )
+
+        def second_product(m, nh):
+            bank = psum.tile([P, 512], F32, name="bank", tag="bank")
+            banks[("o", m, nh)] = bank
+            fc, fs = codes["F"]
+            for gi in range(2):
+                c, s = h_codes[(gi, nh)]
+                nc.tensor.matmul_mx(
+                    out=bank[:],
+                    lhsT=fc[:, m // 4, gi, P * (m % 4) : P * (m % 4) + P].bitcast(FP8X4),
+                    lhsT_scale=fs[:, m // 4, gi, P * (m % 4) : P * (m % 4) + P],
+                    rhs=c[:].bitcast(FP8X4),
+                    rhs_scale=s[:],
+                    start=(gi == 0),
+                    stop=(gi == 1),
+                )
+
+        def finish(m, nh):
+            bank = banks[("o", m, nh)]
+            res = keep.tile([P, 512], F32, name="res_%d%d" % (m, nh))
+            q = q_tiles[m // 2][:, m % 2, 512 * nh : 512 * nh + 512]
+            if (m, nh) in on_gpsimd:
+                y = keep.tile([P, 512], F32, name="y_%d%d" % (m, nh))
+                nc.scalar.activation(out=y[:], in_=bank[:], func=COPY, scale=g_col[:, m : m + 1])
+                nc.gpsimd.tensor_tensor(out=res[:], in0=y[:], in1=q, op=ADD)
+            else:
+                nc.vector.scalar_tensor_tensor(
+                    out=res[:], in0=bank[:], scalar=g_col[:, m : m + 1], in1=q, op0=MULT, op1=ADD
+                )
+            nc.sync.dma_start(out=out[P * m : P * m + P, 512 * nh : 512 * nh + 512], in_=res[:])
+
+        on_vector = [x for x in order if x not in on_scalar]
+        for x in on_scalar[:3]:
+            widen(x)
+        for x in on_vector[:10]:
+            widen(x)
+        for x in order[:8]:
+            turn(x)
+        for x in order[:8]:
+            empty(x)
+        for x in order[8:13]:
+            turn(x)
+        for x in order[8:12]:
+            empty(x)
+        widen(on_scalar[3])
+        quant_p(0)
+        quant_p(1)
+        widen(on_vector[10])
+        quant_f(0, 0)
+        quant_f(0, 1)
+        widen(on_vector[11])
+        empty(order[12])
+        gain_bank = psum.tile([P, 512], F32, name="bank", tag="bank")
+        for m in range(8):
+            nc.tensor.matmul(gain_bank[:, m : m + 1], lhsT=g_rows[:, P * m : P * m + P], rhs=first[:], start=True, stop=True)
+        for t in range(4):
+            first_product(0, 0, t)
+        for x in order[13:]:
+            turn(x)
+        for x in order[13:]:
+            empty(x)
+        g_col = keep.tile([P, 8], F32, name="g_col")
+        nc.scalar.copy(out=g_col[:], in_=gain_bank[:, 0:8])
+
+        inputs = [(quant_p, (2,)), (quant_p, (3,)), None, None, (quant_f, (1, 0)), (quant_f, (1, 1))]
+        halves = [(gi, nh, j) for nh in range(2) for gi in range(2) for j in range(2)]
+        done = 0
+        for i in range(16):
+            gi, nh, t = (i // 4) % 2, i // 8, i % 4
+            if i >= 4:
+                first_product(gi, nh, t)
+            gain_h(gi, nh, t)
+            if t == 3:
+                interleave_h(gi, nh, 0)
+                interleave_h(gi, nh, 1)
+            if i < len(inputs) and inputs[i] is not None:
+                inputs[i][0](*inputs[i][1])
+            if i >= 7 and i % 2 == 1:
+                quant_h(*halves[done])
+                done += 1
+        n = 0
+        for nh in range(2):
+            for m in range(8):
+                second_product(m, nh)
+                finish(m, nh)
+                n += 1
+                if n >= 3 and done < 8:
+                    quant_h(*halves[done])
+                    done += 1

@@ -17,255 +17,338 @@ MULT = mybir.AluOpType.mult
 ADD = mybir.AluOpType.add
 COPY = mybir.ActivationFunctionType.Copy
 
+TURN_BANKS = 3
+LOADS = [("P", 0, (0,)), ("P", 1, (0,)), ("F", 0, (0,)), ("P", 0, (1,)), ("P", 1, (1,)), ("F", 0, (1,)), ("F", 1, (0, 1)), ("F", 2, (0, 1)), ("P", 2, (0, 1)), ("P", 3, (0, 1)), ("F", 3, (0, 1))]
+
 
 def tile_kalman_predicted_covariance_d2_kernel(tc, P_bytes, P_scale, F_bytes, F_scale, g, Q, out):
     nc = tc.nc
     with ExitStack() as ctx:
         keep = ctx.enter_context(tc.tile_pool(name="keep", bufs=1))
-        psum = ctx.enter_context(tc.psum_pool(name="psum", bufs=8))
+        psum = ctx.enter_context(tc.psum_pool(name="psum", bufs=1))
         ctx.enter_context(tc.manual_schedule())
 
+        g_rows = keep.tile([P, P], BF16, name="g_rows")
+        nc.gpsimd.memset(g_rows[:], 0.0)
+        ident = keep.tile([P, P], F32, name="ident")
+        make_identity(nc, ident[:])
 
-        order = [("P", 0), ("P", 1), ("P", 2), ("P", 3), ("F", 0), ("F", 1), ("F", 2), ("F", 3)]
-        order += [("P", 4), ("P", 5), ("P", 6), ("P", 7), ("F", 4), ("F", 5), ("F", 6), ("F", 7)]
-        on_scalar = [("P", 1), ("F", 1), ("P", 5), ("F", 7)]
-        on_gpsimd = []
-
-        p_scale = keep.tile([P, 2, 32], F32, name="p_scale")
-        nc.scalar.dma_start(out=p_scale[:], in_=P_scale.rearrange("(g m t) c -> m g (t c)", g=2, t=4))
+        p_scale = keep.tile([P, 4, 16], F32, name="p_scale")
+        nc.scalar.dma_start(out=p_scale[:], in_=P_scale.rearrange("(h m e) c -> m h (e c)", h=4, e=2))
         f_scale = keep.tile([P, 64], F32, name="f_scale")
         nc.scalar.dma_start(out=f_scale[:], in_=F_scale.rearrange("b c -> (b c)").partition_broadcast(P))
-        p_rows = P_bytes.rearrange("(g m t) j -> g m t j", g=2, t=4)
-        f_rows = F_bytes.rearrange("(b p) j -> p b j", p=P)
+        nc.scalar.dma_start(out=g_rows[0:8, :], in_=g.rearrange("(b p) -> b p", p=P))
+
+        rows = {
+            "P": P_bytes.rearrange("(h p e) j -> p h e j", h=4, e=2),
+            "F": F_bytes.rearrange("(h e p) j -> p h e j", h=4, e=2),
+        }
         raw = {}
         scale = {}
-        for i, n in [(0, 1), (1, 1)] + [(i, 2) for i in range(2, 16, 2)]:
-            kind, b = order[i]
-            part = keep.tile([P, n, N], U8, name="bytes_%s%d" % (kind, b))
-            rows = p_rows[b // 4][:, b % 4 : b % 4 + n, :] if kind == "P" else f_rows[:, b : b + n, :]
-            nc.sync.dma_start(out=part[:], in_=rows)
-            for j in range(n):
-                raw[order[i + j]] = part[:, j, :]
-        for b in range(8):
-            scale[("P", b)] = p_scale[:, b // 4, 8 * (b % 4) : 8 * (b % 4) + 8]
-            scale[("F", b)] = f_scale[:, 8 * b : 8 * b + 8]
+        for kind, pair, halves in LOADS:
+            cols = slice(512 * halves[0], 512 * halves[-1] + 512)
+            part = keep.tile([P, 2, 512 * len(halves)], U8, name="bytes_%s%d%d" % (kind, pair, halves[0]))
+            nc.sync.dma_start(out=part[:], in_=rows[kind][:, pair, :, cols])
+            for e in range(2):
+                for i, k in enumerate(halves):
+                    raw[(kind, pair, k, e)] = part[:, e, 512 * i : 512 * i + 512]
+        for pair in range(4):
+            for e in range(2):
+                scale[("P", pair, e)] = p_scale[:, pair, 8 * e : 8 * e + 8]
+                scale[("F", pair, e)] = f_scale[:, 16 * pair + 8 * e : 16 * pair + 8 * e + 8]
         q_rows = Q.rearrange("(b p) n -> p b n", p=P)
         q_tiles = []
         for h in range(4):
             qt = keep.tile([P, 2, N], BF16, name="q%d" % h)
             nc.sync.dma_start(out=qt[:], in_=q_rows[:, 2 * h : 2 * h + 2, :])
             q_tiles.append(qt)
-            if h == 0:
-                g_rows = keep.tile([P, N], BF16, name="g_rows")
-                nc.sync.dma_start(out=g_rows[:], in_=g.partition_broadcast(P))
 
-        ident = keep.tile([P, P], F32, name="ident")
-        make_identity(nc, ident[:])
-        first = keep.tile([P, 1], BF16, name="first")
-        nc.gpsimd.tensor_copy(out=first[:], in_=ident[:, 0:1])
-
-        codes = {}
-        c = keep.tile([P, 8, 2, P], U32, name="codes_P", align_bytes=256)
-        s = keep.tile([P, 8, 2, P], U8, name="sc_P", align_bytes=256)
-        codes["P"] = (c, s)
-        c = keep.tile([P, 2, 2, 512], U32, name="codes_F", align_bytes=256)
-        s = keep.tile([P, 2, 2, 512], U8, name="sc_F", align_bytes=256)
-        codes["F"] = (c, s)
-        h_codes = {}
-        for gi in range(2):
-            for nh in range(2):
-                hc = keep.tile([P, 512], U32, name="h_codes%d%d" % (gi, nh), align_bytes=256)
-                hs = keep.tile([P, 512], U8, name="h_sc%d%d" % (gi, nh), align_bytes=256)
-                h_codes[(gi, nh)] = (hc, hs)
+        pick = keep.tile([P, 8], BF16, name="pick")
+        nc.scalar.activation(out=pick[:], in_=ident[:, 0:8], func=COPY)
+        g_col = keep.tile([P, 8], F32, name="g_col")
 
         wide = {}
         banks = {}
         grouped = {}
-        hg = {}
-        ht = {}
+        codes = {}
 
-        def widen(x):
-            w = keep.tile([P, N], BF16, name="wide_%s%d" % x, align_bytes=64)
-            wide[x] = w
-            for c in range(8):
-                src = raw[x][:, P * c : P * c + P].bitcast(FP8)
-                col = scale[x][:, c : c + 1]
-                if x in on_scalar:
-                    nc.scalar.activation(out=w[:, P * c : P * c + P], in_=src, func=COPY, scale=col)
-                else:
-                    nc.vector.tensor_scalar(out=w[:, P * c : P * c + P], in0=src, scalar1=col, scalar2=None, op0=MULT)
+        def mx_tiles(key, width):
+            c = keep.tile([P, width], U32, name="codes_%s" % key, align_bytes=256)
+            s = keep.tile([P, width], U8, name="scales_%s" % key, align_bytes=256)
+            codes[key] = (c, s)
 
-        def turn(x):
-            words = wide[x][:].bitcast(F32)
-            bank = psum.tile([P, 2, 2, P], F32, name="bank", tag="bank")
-            banks[x] = bank
+        for a in range(2):
             for k in range(2):
+                mx_tiles("P%d%d" % (a, k), 512)
+                mx_tiles("F%d%d" % (a, k), 512)
+                mx_tiles("h%d%d" % (a, k), 512)
+
+        def gain_column():
+            bank = psum.tile([P, 512], F32, name="turn", tag="turn", bufs=TURN_BANKS)
+            nc.tensor.matmul(bank[:, 0:8], lhsT=g_rows[:], rhs=pick[:], start=True, stop=True)
+            nc.scalar.copy(out=g_col[:], in_=bank[:, 0:8])
+
+        def widen(kind, pair, k, e):
+            w = keep.tile([P, 512], BF16, name="wide_%s%d%d%d" % (kind, pair, k, e), align_bytes=64)
+            wide[(kind, pair, k, e)] = w
+            blocks = w[:].rearrange("p (u c q x) -> p c q u x", u=2, c=4, q=4)
+            for c in range(4):
+                nc.vector.tensor_scalar(
+                    out=blocks[:, c],
+                    in0=raw[(kind, pair, k, e)][:, P * c : P * c + P].bitcast(FP8),
+                    scalar1=scale[(kind, pair, e)][:, 4 * k + c : 4 * k + c + 1],
+                    scalar2=None,
+                    op0=MULT,
+                )
+
+        def turn(kind, pair, k):
+            bank = psum.tile([P, 2, 2, P], F32, name="turn", tag="turn", bufs=TURN_BANKS)
+            banks[(kind, pair, k)] = bank
+            for e in range(2):
+                words = wide[(kind, pair, k, e)][:].bitcast(F32)
                 for u in range(2):
-                    w = words[:, 256 * k + u : 256 * k + 256 : 2]
-                    nc.tensor.transpose(bank[:, k, u, :], w, ident[:])
+                    nc.tensor.transpose(bank[:, e, u, :], words[:, P * u : P * u + P], ident[:])
 
-        def empty(x):
-            kind, b = x
+        def empty(kind, pair, k, on_vector=False):
+            gr = keep.tile([P, N], BF16, name="grouped_%s%d%d" % (kind, pair, k), align_bytes=64)
+            grouped[(kind, pair, k)] = gr
+            words = gr[:].bitcast(F32)
+            bank = banks[(kind, pair, k)]
             if kind == "P":
-                if b % 2 == 0:
-                    gr = keep.tile([P, 2, 2, 512], BF16, name="grouped_P%d" % b, align_bytes=64)
-                    grouped[("P", b // 2)] = gr
-                dst = grouped[("P", b // 2)][:, b % 2, :, :]
+                dst = words.rearrange("p (r e u) -> p r e u", e=2, u=2)
+                src = bank[:].rearrange("p e u r -> p r e u")
             else:
-                if b % 4 == 0:
-                    gr = keep.tile([P, 2, 4, 512], BF16, name="grouped_F%d" % b, align_bytes=64)
-                    grouped[("F", b // 4)] = gr
-                dst = grouped[("F", b // 4)][:, :, b % 4, :]
-            nc.scalar.copy(
-                out=dst.bitcast(F32).rearrange("p k (r u) -> p k r u", u=2),
-                in_=banks[x][:].rearrange("p k u r -> p k r u"),
+                dst = words.rearrange("p (e r u) -> p e r u", e=2, u=2)
+                src = bank[:].rearrange("p e u r -> p e r u")
+            if on_vector:
+                nc.vector.tensor_copy(out=dst, in_=src)
+            else:
+                nc.scalar.copy(out=dst, in_=src)
+
+        def quant(kind, pair, k):
+            c, s = codes["%s%d%d" % (kind, pair // 2, k)]
+            cols = slice(256 * (pair % 2), 256 * (pair % 2) + 256)
+            nc.vector.quantize_mx(out=c[:, cols].bitcast(FP8X4), scales=s[:, cols], in_=grouped[(kind, pair, k)][:])
+
+        def product(key, b, k, moving):
+            if k == 0:
+                bank = psum.tile([P, 512], F32, name="sums", tag="sums", bufs=8 - TURN_BANKS)
+                banks[key] = bank
+            fc, fs = codes["F%d%d" % (b // 4, k)]
+            rows_m = slice(P * (b % 4), P * (b % 4) + P)
+            c, s = codes[moving]
+            nc.tensor.matmul_mx(
+                out=banks[key][:],
+                lhsT=fc[:, rows_m].bitcast(FP8X4),
+                lhsT_scale=fs[:, rows_m],
+                rhs=c[:].bitcast(FP8X4),
+                rhs_scale=s[:],
+                start=(k == 0),
+                stop=(k == 1),
             )
 
-        def quant_p(pair):
-            c, s = codes["P"]
-            b = 2 * pair
-            nc.vector.quantize_mx(
-                out=c[:, b : b + 2, :, :].rearrange("p b k m -> p (b k m)").bitcast(FP8X4),
-                scales=s[:, b : b + 2, :, :].rearrange("p b k m -> p (b k m)"),
-                in_=grouped[("P", pair)][:].rearrange("p b k c -> p (b k c)"),
-            )
+        def first(b, gi, passes=(0, 1)):
+            for k in passes:
+                product(("H", b, gi), b, k, "P%d%d" % (gi, k))
 
-        def quant_f(nh, k):
-            c, s = codes["F"]
-            nc.vector.quantize_mx(
-                out=c[:, nh, k, :].bitcast(FP8X4),
-                scales=s[:, nh, k, :],
-                in_=grouped[("F", nh)][:, k, :, :].rearrange("p b c -> p (b c)"),
-            )
+        def second(m, nh, passes=(0, 1)):
+            for k in passes:
+                product(("Y", m, nh), m, k, "h%d%d" % (nh, k))
 
-        def first_product(gi, nh, t):
-            bank = psum.tile([P, 512], F32, name="bank", tag="bank")
-            banks[(gi, nh, t)] = bank
-            pc, ps = codes["P"]
-            fc, fs = codes["F"]
-            for k in range(2):
-                nc.tensor.matmul_mx(
-                    out=bank[:],
-                    lhsT=pc[:, 4 * gi + t, k, :].bitcast(FP8X4),
-                    lhsT_scale=ps[:, 4 * gi + t, k, :],
-                    rhs=fc[:, nh, k, :].bitcast(FP8X4),
-                    rhs_scale=fs[:, nh, k, :],
-                    start=(k == 0),
-                    stop=(k == 1),
-                )
-
-        def gain_h(gi, nh, t):
-            if t == 0:
-                tile_ht = keep.tile([P, 4, 512], BF16, name="ht_%d%d" % (gi, nh), align_bytes=64)
-                ht[(gi, nh)] = tile_ht
-            nc.vector.tensor_tensor(
-                out=ht[(gi, nh)][:, t, :],
-                in0=banks[(gi, nh, t)][:],
-                in1=g_rows[:, 512 * nh : 512 * nh + 512],
-                op=MULT,
-            )
-
-        def interleave_h(gi, nh, j):
-            tile_hg = keep.tile([P, 256, 4], BF16, name="hg_%d%d%d" % (gi, nh, j), align_bytes=64)
-            hg[(gi, nh, j)] = tile_hg
-            nc.scalar.copy(
-                out=tile_hg[:].rearrange("p (c i) t -> p c t i", i=4),
-                in_=ht[(gi, nh)][:, :, 256 * j : 256 * j + 256].rearrange("p t (c i) -> p c t i", i=4),
-            )
-
-        def quant_h(gi, nh, j):
-            c, s = h_codes[(gi, nh)]
-            nc.vector.quantize_mx(
-                out=c[:, 256 * j : 256 * j + 256].bitcast(FP8X4),
-                scales=s[:, 256 * j : 256 * j + 256],
-                in_=hg[(gi, nh, j)][:].rearrange("p n t -> p (n t)"),
-            )
-
-        def second_product(m, nh):
-            bank = psum.tile([P, 512], F32, name="bank", tag="bank")
-            banks[("o", m, nh)] = bank
-            fc, fs = codes["F"]
-            for gi in range(2):
-                c, s = h_codes[(gi, nh)]
-                nc.tensor.matmul_mx(
-                    out=bank[:],
-                    lhsT=fc[:, m // 4, gi, P * (m % 4) : P * (m % 4) + P].bitcast(FP8X4),
-                    lhsT_scale=fs[:, m // 4, gi, P * (m % 4) : P * (m % 4) + P],
-                    rhs=c[:].bitcast(FP8X4),
-                    rhs_scale=s[:],
-                    start=(gi == 0),
-                    stop=(gi == 1),
-                )
+        def gain(b, gi, on_vector=False):
+            hw = keep.tile([P, 512], BF16, name="h_wide%d%d" % (b, gi), align_bytes=64)
+            wide[("h", b // 2, gi, b % 2)] = hw
+            dst = hw[:].rearrange("p (u q x) -> p u q x", u=2, x=16)
+            src = banks[("H", b, gi)][:].rearrange("p (q u x) -> p u q x", u=2, x=16)
+            if on_vector:
+                nc.vector.tensor_scalar(out=dst, in0=src, scalar1=g_col[:, b : b + 1], scalar2=None, op0=MULT)
+            else:
+                nc.scalar.activation(out=dst, in_=src, func=COPY, scale=g_col[:, b : b + 1])
 
         def finish(m, nh):
-            bank = banks[("o", m, nh)]
             res = keep.tile([P, 512], F32, name="res_%d%d" % (m, nh))
-            q = q_tiles[m // 2][:, m % 2, 512 * nh : 512 * nh + 512]
-            if (m, nh) in on_gpsimd:
-                y = keep.tile([P, 512], F32, name="y_%d%d" % (m, nh))
-                nc.scalar.activation(out=y[:], in_=bank[:], func=COPY, scale=g_col[:, m : m + 1])
-                nc.gpsimd.tensor_tensor(out=res[:], in0=y[:], in1=q, op=ADD)
-            else:
-                nc.vector.scalar_tensor_tensor(
-                    out=res[:], in0=bank[:], scalar=g_col[:, m : m + 1], in1=q, op0=MULT, op1=ADD
-                )
+            nc.vector.scalar_tensor_tensor(
+                out=res[:],
+                in0=banks[("Y", m, nh)][:],
+                scalar=g_col[:, m : m + 1],
+                in1=q_tiles[m // 2][:, m % 2, 512 * nh : 512 * nh + 512],
+                op0=MULT,
+                op1=ADD,
+            )
             nc.sync.dma_start(out=out[P * m : P * m + P, 512 * nh : 512 * nh + 512], in_=res[:])
 
-        on_vector = [x for x in order if x not in on_scalar]
-        for x in on_scalar[:3]:
-            widen(x)
-        for x in on_vector[:10]:
-            widen(x)
-        for x in order[:8]:
-            turn(x)
-        for x in order[:8]:
-            empty(x)
-        for x in order[8:13]:
-            turn(x)
-        for x in order[8:12]:
-            empty(x)
-        widen(on_scalar[3])
-        quant_p(0)
-        quant_p(1)
-        widen(on_vector[10])
-        quant_f(0, 0)
-        quant_f(0, 1)
-        widen(on_vector[11])
-        empty(order[12])
-        gain_bank = psum.tile([P, 512], F32, name="bank", tag="bank")
-        for m in range(8):
-            nc.tensor.matmul(gain_bank[:, m : m + 1], lhsT=g_rows[:, P * m : P * m + P], rhs=first[:], start=True, stop=True)
-        for t in range(4):
-            first_product(0, 0, t)
-        for x in order[13:]:
-            turn(x)
-        for x in order[13:]:
-            empty(x)
-        g_col = keep.tile([P, 8], F32, name="g_col")
-        nc.scalar.copy(out=g_col[:], in_=gain_bank[:, 0:8])
-
-        inputs = [(quant_p, (2,)), (quant_p, (3,)), None, None, (quant_f, (1, 0)), (quant_f, (1, 1))]
-        halves = [(gi, nh, j) for nh in range(2) for gi in range(2) for j in range(2)]
-        done = 0
-        for i in range(16):
-            gi, nh, t = (i // 4) % 2, i // 8, i % 4
-            if i >= 4:
-                first_product(gi, nh, t)
-            gain_h(gi, nh, t)
-            if t == 3:
-                interleave_h(gi, nh, 0)
-                interleave_h(gi, nh, 1)
-            if i < len(inputs) and inputs[i] is not None:
-                inputs[i][0](*inputs[i][1])
-            if i >= 7 and i % 2 == 1:
-                quant_h(*halves[done])
-                done += 1
-        n = 0
-        for nh in range(2):
-            for m in range(8):
-                second_product(m, nh)
-                finish(m, nh)
-                n += 1
-                if n >= 3 and done < 8:
-                    quant_h(*halves[done])
-                    done += 1
+        widen("P", 0, 0, 0)
+        widen("P", 0, 0, 1)
+        turn("P", 0, 0)
+        empty("P", 0, 0)
+        widen("P", 1, 0, 0)
+        widen("P", 1, 0, 1)
+        turn("P", 1, 0)
+        empty("P", 1, 0)
+        widen("F", 0, 0, 0)
+        widen("F", 0, 0, 1)
+        gain_column()
+        turn("F", 0, 0)
+        empty("F", 0, 0)
+        quant("P", 0, 0)
+        widen("P", 0, 1, 0)
+        widen("P", 0, 1, 1)
+        turn("P", 0, 1)
+        empty("P", 0, 1)
+        quant("P", 1, 0)
+        widen("P", 1, 1, 0)
+        widen("P", 1, 1, 1)
+        turn("P", 1, 1)
+        empty("P", 1, 1)
+        quant("F", 0, 0)
+        widen("F", 0, 1, 0)
+        widen("F", 0, 1, 1)
+        turn("F", 0, 1)
+        empty("F", 0, 1)
+        quant("P", 0, 1)
+        first(0, 0, (0,))
+        first(1, 0, (0,))
+        widen("F", 1, 0, 0)
+        widen("F", 1, 0, 1)
+        quant("P", 1, 1)
+        widen("F", 1, 1, 0)
+        widen("F", 1, 1, 1)
+        turn("F", 1, 0)
+        quant("F", 0, 1)
+        turn("F", 1, 1)
+        empty("F", 1, 0)
+        empty("F", 1, 1)
+        widen("F", 2, 0, 0)
+        widen("F", 2, 0, 1)
+        widen("F", 2, 1, 0)
+        widen("F", 2, 1, 1)
+        first(0, 0, (1,))
+        first(1, 0, (1,))
+        turn("F", 2, 0)
+        turn("F", 2, 1)
+        gain(0, 0)
+        empty("F", 2, 0)
+        empty("F", 2, 1)
+        quant("F", 1, 0)
+        quant("F", 1, 1)
+        gain(1, 0)
+        widen("P", 2, 0, 0)
+        widen("P", 2, 0, 1)
+        widen("P", 3, 0, 0)
+        widen("P", 3, 0, 1)
+        first(2, 0)
+        first(3, 0)
+        turn("P", 2, 0)
+        turn("P", 3, 0)
+        gain(2, 0)
+        empty("P", 2, 0)
+        empty("P", 3, 0)
+        quant("F", 2, 0)
+        quant("F", 2, 1)
+        gain(3, 0)
+        widen("P", 2, 1, 0)
+        widen("P", 2, 1, 1)
+        widen("P", 3, 1, 0)
+        widen("P", 3, 1, 1)
+        first(4, 0)
+        first(5, 0)
+        turn("P", 2, 1)
+        turn("P", 3, 1)
+        turn("h", 0, 0)
+        empty("P", 2, 1)
+        gain(4, 0)
+        empty("P", 3, 1)
+        quant("P", 2, 0)
+        quant("P", 3, 0)
+        empty("h", 0, 0)
+        gain(5, 0)
+        widen("F", 3, 0, 0)
+        widen("F", 3, 0, 1)
+        widen("F", 3, 1, 0)
+        widen("F", 3, 1, 1)
+        first(0, 1, (0,))
+        first(1, 1, (0,))
+        first(2, 1, (0,))
+        first(3, 1, (0,))
+        turn("F", 3, 0)
+        turn("F", 3, 1)
+        turn("h", 1, 0)
+        empty("F", 3, 0)
+        empty("F", 3, 1)
+        quant("P", 2, 1)
+        quant("P", 3, 1)
+        quant("h", 0, 0)
+        empty("h", 1, 0)
+        first(0, 1, (1,))
+        first(1, 1, (1,))
+        first(2, 1, (1,))
+        first(3, 1, (1,))
+        first(4, 1)
+        gain(0, 1, True)
+        quant("F", 3, 0)
+        quant("F", 3, 1)
+        gain(1, 1)
+        gain(2, 1, True)
+        gain(3, 1)
+        quant("h", 1, 0)
+        first(5, 1)
+        first(6, 0)
+        turn("h", 0, 1)
+        turn("h", 1, 1)
+        turn("h", 2, 0)
+        gain(4, 1)
+        gain(5, 1, True)
+        first(7, 0)
+        first(6, 1)
+        first(7, 1)
+        empty("h", 0, 1)
+        empty("h", 1, 1, True)
+        gain(6, 0)
+        quant("h", 0, 1)
+        quant("h", 1, 1)
+        empty("h", 2, 0)
+        gain(7, 0)
+        gain(6, 1)
+        gain(7, 1)
+        second(0, 0)
+        second(1, 0)
+        quant("h", 2, 0)
+        turn("h", 2, 1)
+        turn("h", 3, 0)
+        finish(0, 0)
+        empty("h", 2, 1)
+        finish(1, 0)
+        empty("h", 3, 0)
+        second(2, 0)
+        second(3, 0)
+        turn("h", 3, 1)
+        finish(2, 0)
+        quant("h", 2, 1)
+        empty("h", 3, 1)
+        second(4, 0)
+        finish(3, 0)
+        quant("h", 3, 0)
+        second(5, 0)
+        finish(4, 0)
+        quant("h", 3, 1)
+        second(6, 0)
+        finish(5, 0)
+        second(7, 0)
+        finish(6, 0)
+        finish(7, 0)
+        second(0, 1)
+        finish(0, 1)
+        second(1, 1)
+        finish(1, 1)
+        second(2, 1)
+        finish(2, 1)
+        second(3, 1)
+        finish(3, 1)
+        second(4, 1)
+        finish(4, 1)
+        second(5, 1)
+        finish(5, 1)
+        second(6, 1)
+        finish(6, 1)
+        second(7, 1)
+        finish(7, 1)

@@ -18,6 +18,7 @@ ADD = mybir.AluOpType.add
 COPY = mybir.ActivationFunctionType.Copy
 
 TURN_BANKS = 3
+RUN = (16, 16)
 LOADS = [("P", 0, (0,)), ("P", 1, (0,)), ("F", 0, (0,)), ("P", 0, (1,)), ("P", 1, (1,)), ("F", 0, (1,)), ("F", 1, (0, 1)), ("F", 2, (0, 1)), ("P", 2, (0, 1)), ("P", 3, (0, 1)), ("F", 3, (0, 1))]
 
 
@@ -29,14 +30,19 @@ def tile_kalman_predicted_covariance_d2_kernel(tc, P_bytes, P_scale, F_bytes, F_
         ctx.enter_context(tc.manual_schedule())
 
         g_rows = keep.tile([P, P], BF16, name="g_rows")
-        nc.gpsimd.memset(g_rows[:], 0.0)
+        nc.vector.memset(g_rows[:], 0.0)
+        f_list = keep.tile([P, 1], F32, name="f_list")
+        nc.vector.memset(f_list[:], 0.0)
         ident = keep.tile([P, P], F32, name="ident")
         make_identity(nc, ident[:])
 
-        p_scale = keep.tile([P, 4, 16], F32, name="p_scale")
-        nc.scalar.dma_start(out=p_scale[:], in_=P_scale.rearrange("(h m e) c -> m h (e c)", h=4, e=2))
-        f_scale = keep.tile([P, 64], F32, name="f_scale")
-        nc.scalar.dma_start(out=f_scale[:], in_=F_scale.rearrange("b c -> (b c)").partition_broadcast(P))
+        p_scales = P_scale.rearrange("(h m e) c -> m h (e c)", h=4, e=2)
+        p_scale = []
+        for half in range(2):
+            tile_s = keep.tile([P, 2, 16], F32, name="p_scale%d" % half)
+            p_scale.append(tile_s)
+        nc.scalar.dma_start(out=p_scale[0][:], in_=p_scales[:, 0:2, :])
+        nc.scalar.dma_start(out=f_list[0:64, :], in_=F_scale.rearrange("b (c o) -> (b c) o", o=1))
         nc.scalar.dma_start(out=g_rows[0:8, :], in_=g.rearrange("(b p) -> b p", p=P))
 
         rows = {
@@ -45,16 +51,21 @@ def tile_kalman_predicted_covariance_d2_kernel(tc, P_bytes, P_scale, F_bytes, F_
         }
         raw = {}
         scale = {}
+        spread = keep.tile([P, 136], F32, name="spread")
+        f_scale = spread[:, 0:64]
+        g_col = spread[:, 128:136]
         for kind, pair, halves in LOADS:
             cols = slice(512 * halves[0], 512 * halves[-1] + 512)
             part = keep.tile([P, 2, 512 * len(halves)], U8, name="bytes_%s%d%d" % (kind, pair, halves[0]))
+            if (kind, pair) == ("P", 2):
+                nc.sync.dma_start(out=p_scale[1][:], in_=p_scales[:, 2:4, :])
             nc.sync.dma_start(out=part[:], in_=rows[kind][:, pair, :, cols])
             for e in range(2):
                 for i, k in enumerate(halves):
                     raw[(kind, pair, k, e)] = part[:, e, 512 * i : 512 * i + 512]
         for pair in range(4):
             for e in range(2):
-                scale[("P", pair, e)] = p_scale[:, pair, 8 * e : 8 * e + 8]
+                scale[("P", pair, e)] = p_scale[pair // 2][:, pair % 2, 8 * e : 8 * e + 8]
                 scale[("F", pair, e)] = f_scale[:, 16 * pair + 8 * e : 16 * pair + 8 * e + 8]
         q_rows = Q.rearrange("(b p) n -> p b n", p=P)
         q_tiles = []
@@ -65,9 +76,9 @@ def tile_kalman_predicted_covariance_d2_kernel(tc, P_bytes, P_scale, F_bytes, F_
 
         pick = keep.tile([P, 8], BF16, name="pick")
         nc.scalar.activation(out=pick[:], in_=ident[:, 0:8], func=COPY)
-        g_col = keep.tile([P, 8], F32, name="g_col")
 
         wide = {}
+        plain = set()
         banks = {}
         grouped = {}
         codes = {}
@@ -85,21 +96,30 @@ def tile_kalman_predicted_covariance_d2_kernel(tc, P_bytes, P_scale, F_bytes, F_
 
         def gain_column():
             bank = psum.tile([P, 512], F32, name="turn", tag="turn", bufs=TURN_BANKS)
-            nc.tensor.matmul(bank[:, 0:8], lhsT=g_rows[:], rhs=pick[:], start=True, stop=True)
-            nc.scalar.copy(out=g_col[:], in_=bank[:, 0:8])
+            nc.tensor.transpose(bank[:, 0:P], f_list[:].to_broadcast([P, P]), ident[:])
+            nc.tensor.matmul(bank[:, P : P + 8], lhsT=g_rows[:], rhs=pick[:], start=True, stop=True)
+            nc.scalar.copy(out=spread[:], in_=bank[:, 0:136])
 
-        def widen(kind, pair, k, e):
+        def warm_up(count):
+            if "warm" not in banks:
+                bank = psum.tile([P, 512], F32, name="sums", tag="sums", bufs=8 - TURN_BANKS)
+                banks["warm"] = bank
+            for i in range(count):
+                nc.tensor.matmul(banks["warm"][:, 0:P], lhsT=ident[:], rhs=ident[:], start=True, stop=True)
+
+        def widen(kind, pair, k, e, on_scalar=False):
             w = keep.tile([P, 512], BF16, name="wide_%s%d%d%d" % (kind, pair, k, e), align_bytes=64)
             wide[(kind, pair, k, e)] = w
-            blocks = w[:].rearrange("p (u c q x) -> p c q u x", u=2, c=4, q=4)
+            blocks = w[:].rearrange("p (u c q x) -> p c q u x", u=2, c=4, x=RUN[k])
+            if on_scalar:
+                plain.add((kind, pair, k, e))
             for c in range(4):
-                nc.vector.tensor_scalar(
-                    out=blocks[:, c],
-                    in0=raw[(kind, pair, k, e)][:, P * c : P * c + P].bitcast(FP8),
-                    scalar1=scale[(kind, pair, e)][:, 4 * k + c : 4 * k + c + 1],
-                    scalar2=None,
-                    op0=MULT,
-                )
+                src = raw[(kind, pair, k, e)][:, P * c : P * c + P].bitcast(FP8)
+                col = scale[(kind, pair, e)][:, 4 * k + c : 4 * k + c + 1]
+                if on_scalar:
+                    nc.scalar.activation(out=w[:, P * c : P * c + P], in_=src, func=COPY, scale=col)
+                else:
+                    nc.vector.tensor_scalar(out=blocks[:, c], in0=src, scalar1=col, scalar2=None, op0=MULT)
 
         def turn(kind, pair, k):
             bank = psum.tile([P, 2, 2, P], F32, name="turn", tag="turn", bufs=TURN_BANKS)
@@ -107,7 +127,8 @@ def tile_kalman_predicted_covariance_d2_kernel(tc, P_bytes, P_scale, F_bytes, F_
             for e in range(2):
                 words = wide[(kind, pair, k, e)][:].bitcast(F32)
                 for u in range(2):
-                    nc.tensor.transpose(bank[:, e, u, :], words[:, P * u : P * u + P], ident[:])
+                    half = words[:, u : 2 * P : 2] if (kind, pair, k, e) in plain else words[:, P * u : P * u + P]
+                    nc.tensor.transpose(bank[:, e, u, :], half, ident[:])
 
         def empty(kind, pair, k, on_vector=False):
             gr = keep.tile([P, N], BF16, name="grouped_%s%d%d" % (kind, pair, k), align_bytes=64)
@@ -158,25 +179,29 @@ def tile_kalman_predicted_covariance_d2_kernel(tc, P_bytes, P_scale, F_bytes, F_
         def gain(b, gi, on_vector=False):
             hw = keep.tile([P, 512], BF16, name="h_wide%d%d" % (b, gi), align_bytes=64)
             wide[("h", b // 2, gi, b % 2)] = hw
-            dst = hw[:].rearrange("p (u q x) -> p u q x", u=2, x=16)
-            src = banks[("H", b, gi)][:].rearrange("p (q u x) -> p u q x", u=2, x=16)
+            dst = hw[:].rearrange("p (u q x) -> p u q x", u=2, x=RUN[gi])
+            src = banks[("H", b, gi)][:].rearrange("p (q u x) -> p u q x", u=2, x=RUN[gi])
             if on_vector:
                 nc.vector.tensor_scalar(out=dst, in0=src, scalar1=g_col[:, b : b + 1], scalar2=None, op0=MULT)
             else:
                 nc.scalar.activation(out=dst, in_=src, func=COPY, scale=g_col[:, b : b + 1])
 
-        def finish(m, nh):
-            res = keep.tile([P, 512], F32, name="res_%d%d" % (m, nh))
-            nc.vector.scalar_tensor_tensor(
-                out=res[:],
-                in0=banks[("Y", m, nh)][:],
-                scalar=g_col[:, m : m + 1],
-                in1=q_tiles[m // 2][:, m % 2, 512 * nh : 512 * nh + 512],
-                op0=MULT,
-                op1=ADD,
-            )
-            nc.sync.dma_start(out=out[P * m : P * m + P, 512 * nh : 512 * nh + 512], in_=res[:])
+        def finish(m, nh, parts=1):
+            width = 512 // parts
+            for j in range(parts):
+                res = keep.tile([P, width], F32, name="res_%d%d%d" % (m, nh, j))
+                cols = slice(512 * nh + width * j, 512 * nh + width * j + width)
+                nc.vector.scalar_tensor_tensor(
+                    out=res[:],
+                    in0=banks[("Y", m, nh)][:, width * j : width * j + width],
+                    scalar=g_col[:, m : m + 1],
+                    in1=q_tiles[m // 2][:, m % 2, cols],
+                    op0=MULT,
+                    op1=ADD,
+                )
+                nc.sync.dma_start(out=out[P * m : P * m + P, cols], in_=res[:])
 
+        gain_column()
         widen("P", 0, 0, 0)
         widen("P", 0, 0, 1)
         turn("P", 0, 0)
@@ -187,7 +212,6 @@ def tile_kalman_predicted_covariance_d2_kernel(tc, P_bytes, P_scale, F_bytes, F_
         empty("P", 1, 0)
         widen("F", 0, 0, 0)
         widen("F", 0, 0, 1)
-        gain_column()
         turn("F", 0, 0)
         empty("F", 0, 0)
         quant("P", 0, 0)
@@ -351,4 +375,4 @@ def tile_kalman_predicted_covariance_d2_kernel(tc, P_bytes, P_scale, F_bytes, F_
         second(6, 1)
         finish(6, 1)
         second(7, 1)
-        finish(7, 1)
+        finish(7, 1, 2)

@@ -17,9 +17,8 @@ MULT = mybir.AluOpType.mult
 ADD = mybir.AluOpType.add
 COPY = mybir.ActivationFunctionType.Copy
 
-TURN_BANKS = 3
-RUN = (16, 16)
-LOADS = [("P", 0, (0,)), ("P", 1, (0,)), ("F", 0, (0,)), ("P", 0, (1,)), ("P", 1, (1,)), ("F", 0, (1,)), ("F", 1, (0, 1)), ("F", 2, (0, 1)), ("P", 2, (0, 1)), ("P", 3, (0, 1)), ("F", 3, (0, 1))]
+RUN = (2, 16)
+LOADS = [("P", 0, (0,)), ("F", 0, (0,)), ("P", 1, (0,)), ("F", 1, (0,)), ("P", 0, (1,)), ("P", 1, (1,)), ("P", 2, (0, 1)), ("F", 0, (1,)), ("F", 1, (1,)), ("P", 3, (0, 1)), ("F", 2, (0, 1)), ("F", 3, (0, 1))]
 
 
 def tile_kalman_predicted_covariance_d2_kernel(tc, P_bytes, P_scale, F_bytes, F_scale, g, Q, out):
@@ -75,13 +74,27 @@ def tile_kalman_predicted_covariance_d2_kernel(tc, P_bytes, P_scale, F_bytes, F_
             q_tiles.append(qt)
 
         pick = keep.tile([P, 8], BF16, name="pick")
-        nc.scalar.activation(out=pick[:], in_=ident[:, 0:8], func=COPY)
+        nc.vector.tensor_copy(out=pick[:], in_=ident[:, 0:8])
 
         wide = {}
         plain = set()
         banks = {}
         grouped = {}
         codes = {}
+
+        free = list(range(8))
+        taken = {}
+
+        def take_bank(key, shape):
+            i = free[0]
+            free.remove(i)
+            taken[key] = i
+            bank = psum.tile(shape, F32, name="bank%d" % i, tag="bank%d" % i)
+            banks[key] = bank
+            return bank
+
+        def give_bank(key):
+            free.append(taken[key])
 
         def mx_tiles(key, width):
             c = keep.tile([P, width], U32, name="codes_%s" % key, align_bytes=256)
@@ -95,17 +108,11 @@ def tile_kalman_predicted_covariance_d2_kernel(tc, P_bytes, P_scale, F_bytes, F_
                 mx_tiles("h%d%d" % (a, k), 512)
 
         def gain_column():
-            bank = psum.tile([P, 512], F32, name="turn", tag="turn", bufs=TURN_BANKS)
+            bank = take_bank("spread", [P, 512])
             nc.tensor.transpose(bank[:, 0:P], f_list[:].to_broadcast([P, P]), ident[:])
             nc.tensor.matmul(bank[:, P : P + 8], lhsT=g_rows[:], rhs=pick[:], start=True, stop=True)
-            nc.scalar.copy(out=spread[:], in_=bank[:, 0:136])
-
-        def warm_up(count):
-            if "warm" not in banks:
-                bank = psum.tile([P, 512], F32, name="sums", tag="sums", bufs=8 - TURN_BANKS)
-                banks["warm"] = bank
-            for i in range(count):
-                nc.tensor.matmul(banks["warm"][:, 0:P], lhsT=ident[:], rhs=ident[:], start=True, stop=True)
+            nc.scalar.activation(out=spread[:], in_=bank[:, 0:136], func=COPY)
+            give_bank("spread")
 
         def widen(kind, pair, k, e, on_scalar=False):
             w = keep.tile([P, 512], BF16, name="wide_%s%d%d%d" % (kind, pair, k, e), align_bytes=64)
@@ -121,10 +128,11 @@ def tile_kalman_predicted_covariance_d2_kernel(tc, P_bytes, P_scale, F_bytes, F_
                 else:
                     nc.vector.tensor_scalar(out=blocks[:, c], in0=src, scalar1=col, scalar2=None, op0=MULT)
 
-        def turn(kind, pair, k):
-            bank = psum.tile([P, 2, 2, P], F32, name="turn", tag="turn", bufs=TURN_BANKS)
-            banks[(kind, pair, k)] = bank
-            for e in range(2):
+        def turn(kind, pair, k, halves=(0, 1)):
+            if halves[0] == 0:
+                take_bank((kind, pair, k), [P, 2, 2, P])
+            bank = banks[(kind, pair, k)]
+            for e in halves:
                 words = wide[(kind, pair, k, e)][:].bitcast(F32)
                 for u in range(2):
                     half = words[:, u : 2 * P : 2] if (kind, pair, k, e) in plain else words[:, P * u : P * u + P]
@@ -145,6 +153,7 @@ def tile_kalman_predicted_covariance_d2_kernel(tc, P_bytes, P_scale, F_bytes, F_
                 nc.vector.tensor_copy(out=dst, in_=src)
             else:
                 nc.scalar.copy(out=dst, in_=src)
+            give_bank((kind, pair, k))
 
         def quant(kind, pair, k):
             c, s = codes["%s%d%d" % (kind, pair // 2, k)]
@@ -153,8 +162,7 @@ def tile_kalman_predicted_covariance_d2_kernel(tc, P_bytes, P_scale, F_bytes, F_
 
         def product(key, b, k, moving):
             if k == 0:
-                bank = psum.tile([P, 512], F32, name="sums", tag="sums", bufs=8 - TURN_BANKS)
-                banks[key] = bank
+                take_bank(key, [P, 512])
             fc, fs = codes["F%d%d" % (b // 4, k)]
             rows_m = slice(P * (b % 4), P * (b % 4) + P)
             c, s = codes[moving]
@@ -185,6 +193,7 @@ def tile_kalman_predicted_covariance_d2_kernel(tc, P_bytes, P_scale, F_bytes, F_
                 nc.vector.tensor_scalar(out=dst, in0=src, scalar1=g_col[:, b : b + 1], scalar2=None, op0=MULT)
             else:
                 nc.scalar.activation(out=dst, in_=src, func=COPY, scale=g_col[:, b : b + 1])
+            give_bank(("H", b, gi))
 
         def finish(m, nh, parts=1):
             width = 512 // parts
@@ -200,164 +209,169 @@ def tile_kalman_predicted_covariance_d2_kernel(tc, P_bytes, P_scale, F_bytes, F_
                     op1=ADD,
                 )
                 nc.sync.dma_start(out=out[P * m : P * m + P, cols], in_=res[:])
+            give_bank(("Y", m, nh))
 
         gain_column()
         widen("P", 0, 0, 0)
-        widen("P", 0, 0, 1)
+        widen("P", 0, 0, 1, True)
+        widen("F", 0, 0, 0)
         turn("P", 0, 0)
-        empty("P", 0, 0)
+        widen("F", 0, 0, 1, True)
         widen("P", 1, 0, 0)
         widen("P", 1, 0, 1)
-        turn("P", 1, 0)
-        empty("P", 1, 0)
-        widen("F", 0, 0, 0)
-        widen("F", 0, 0, 1)
         turn("F", 0, 0)
-        empty("F", 0, 0)
-        quant("P", 0, 0)
+        turn("P", 1, 0)
+        widen("F", 1, 0, 0)
+        widen("F", 1, 0, 1, True)
+        empty("P", 0, 0)
         widen("P", 0, 1, 0)
         widen("P", 0, 1, 1)
+        empty("F", 0, 0)
+        turn("F", 1, 0)
         turn("P", 0, 1)
-        empty("P", 0, 1)
-        quant("P", 1, 0)
+        empty("P", 1, 0)
         widen("P", 1, 1, 0)
         widen("P", 1, 1, 1)
-        turn("P", 1, 1)
-        empty("P", 1, 1)
+        quant("P", 0, 0)
         quant("F", 0, 0)
+        quant("P", 1, 0)
+        turn("P", 1, 1)
+        widen("P", 2, 0, 0, True)
+        widen("P", 2, 0, 1, True)
         widen("F", 0, 1, 0)
         widen("F", 0, 1, 1)
-        turn("F", 0, 1)
-        empty("F", 0, 1)
-        quant("P", 0, 1)
         first(0, 0, (0,))
         first(1, 0, (0,))
-        widen("F", 1, 0, 0)
-        widen("F", 1, 0, 1)
-        quant("P", 1, 1)
+        empty("F", 1, 0)
+        turn("F", 0, 1)
+        turn("P", 2, 0)
         widen("F", 1, 1, 0)
         widen("F", 1, 1, 1)
-        turn("F", 1, 0)
-        quant("F", 0, 1)
-        turn("F", 1, 1)
-        empty("F", 1, 0)
-        empty("F", 1, 1)
-        widen("F", 2, 0, 0)
-        widen("F", 2, 0, 1)
-        widen("F", 2, 1, 0)
-        widen("F", 2, 1, 1)
-        first(0, 0, (1,))
-        first(1, 0, (1,))
-        turn("F", 2, 0)
-        turn("F", 2, 1)
-        gain(0, 0)
-        empty("F", 2, 0)
-        empty("F", 2, 1)
+        empty("P", 0, 1)
         quant("F", 1, 0)
-        quant("F", 1, 1)
-        gain(1, 0)
-        widen("P", 2, 0, 0)
-        widen("P", 2, 0, 1)
-        widen("P", 3, 0, 0)
-        widen("P", 3, 0, 1)
-        first(2, 0)
-        first(3, 0)
-        turn("P", 2, 0)
-        turn("P", 3, 0)
-        gain(2, 0)
-        empty("P", 2, 0)
-        empty("P", 3, 0)
-        quant("F", 2, 0)
-        quant("F", 2, 1)
-        gain(3, 0)
+        empty("P", 1, 1)
         widen("P", 2, 1, 0)
         widen("P", 2, 1, 1)
+        first(2, 0, (0,))
+        first(3, 0, (0,))
+        turn("F", 1, 1)
+        empty("F", 0, 1)
+        quant("P", 0, 1)
+        quant("P", 1, 1)
+        turn("P", 2, 1)
+        widen("P", 3, 0, 0)
+        widen("P", 3, 0, 1)
+        empty("F", 1, 1)
+        quant("F", 0, 1)
+        turn("P", 3, 0)
+        empty("P", 2, 0)
         widen("P", 3, 1, 0)
         widen("P", 3, 1, 1)
-        first(4, 0)
-        first(5, 0)
-        turn("P", 2, 1)
+        first(0, 0, (1,))
+        first(1, 0, (1,))
+        quant("F", 1, 1)
+        empty("P", 3, 0)
         turn("P", 3, 1)
-        turn("h", 0, 0)
+        widen("F", 2, 0, 0)
+        widen("F", 2, 0, 1)
         empty("P", 2, 1)
-        gain(4, 0)
-        empty("P", 3, 1)
+        first(2, 0, (1,))
+        first(3, 0, (1,))
         quant("P", 2, 0)
         quant("P", 3, 0)
-        empty("h", 0, 0)
-        gain(5, 0)
-        widen("F", 3, 0, 0)
-        widen("F", 3, 0, 1)
-        widen("F", 3, 1, 0)
-        widen("F", 3, 1, 1)
+        empty("P", 3, 1)
+        turn("F", 2, 0)
+        gain(0, 0)
+        quant("P", 2, 1)
         first(0, 1, (0,))
         first(1, 1, (0,))
-        first(2, 1, (0,))
-        first(3, 1, (0,))
-        turn("F", 3, 0)
-        turn("F", 3, 1)
-        turn("h", 1, 0)
-        empty("F", 3, 0)
-        empty("F", 3, 1)
-        quant("P", 2, 1)
         quant("P", 3, 1)
-        quant("h", 0, 0)
-        empty("h", 1, 0)
+        first(2, 1, (0,))
+        gain(1, 0)
+        first(3, 1, (0,))
+        widen("F", 2, 1, 0)
+        widen("F", 2, 1, 1)
         first(0, 1, (1,))
         first(1, 1, (1,))
+        gain(2, 0)
         first(2, 1, (1,))
+        widen("F", 3, 0, 0)
+        widen("F", 3, 0, 1)
+        gain(3, 0)
         first(3, 1, (1,))
-        first(4, 1)
+        empty("F", 2, 0)
+        turn("F", 2, 1)
+        turn("F", 3, 0)
+        turn("h", 0, 0)
+        turn("h", 1, 0)
         gain(0, 1, True)
-        quant("F", 3, 0)
-        quant("F", 3, 1)
         gain(1, 1)
+        widen("F", 3, 1, 0)
+        widen("F", 3, 1, 1)
+        quant("F", 2, 0)
+        empty("F", 2, 1)
         gain(2, 1, True)
+        first(4, 0, (0,))
+        first(5, 0, (0,))
         gain(3, 1)
-        quant("h", 1, 0)
-        first(5, 1)
-        first(6, 0)
+        turn("F", 3, 1)
         turn("h", 0, 1)
         turn("h", 1, 1)
-        turn("h", 2, 0)
-        gain(4, 1)
-        gain(5, 1, True)
-        first(7, 0)
-        first(6, 1)
-        first(7, 1)
-        empty("h", 0, 1)
-        empty("h", 1, 1, True)
-        gain(6, 0)
+        empty("F", 3, 0)
+        quant("F", 2, 1)
+        empty("h", 0, 0, True)
+        empty("F", 3, 1)
+        first(4, 0, (1,))
+        first(5, 0, (1,))
+        first(4, 1)
+        empty("h", 1, 0)
+        quant("F", 3, 0)
+        quant("h", 0, 0)
+        first(5, 1)
+        empty("h", 0, 1, True)
+        quant("F", 3, 1)
+        empty("h", 1, 1)
+        quant("h", 1, 0)
         quant("h", 0, 1)
+        first(6, 0)
+        gain(4, 0)
         quant("h", 1, 1)
-        empty("h", 2, 0)
-        gain(7, 0)
-        gain(6, 1)
-        gain(7, 1)
+        gain(5, 0, True)
+        gain(4, 1)
         second(0, 0)
+        first(7, 0)
+        gain(5, 1)
         second(1, 0)
-        quant("h", 2, 0)
-        turn("h", 2, 1)
-        turn("h", 3, 0)
+        first(6, 1)
         finish(0, 0)
-        empty("h", 2, 1)
-        finish(1, 0)
-        empty("h", 3, 0)
+        gain(6, 0)
         second(2, 0)
+        first(7, 1)
+        finish(1, 0)
+        gain(7, 0)
         second(3, 0)
-        turn("h", 3, 1)
         finish(2, 0)
-        quant("h", 2, 1)
-        empty("h", 3, 1)
+        gain(6, 1)
         second(4, 0)
         finish(3, 0)
-        quant("h", 3, 0)
-        second(5, 0)
+        gain(7, 1)
+        turn("h", 2, 0)
+        turn("h", 3, 0)
+        turn("h", 2, 1)
+        turn("h", 3, 1)
         finish(4, 0)
-        quant("h", 3, 1)
+        empty("h", 2, 0)
+        empty("h", 3, 0, True)
+        second(5, 0)
+        empty("h", 2, 1)
         second(6, 0)
+        empty("h", 3, 1)
+        quant("h", 2, 0)
+        quant("h", 3, 0)
         finish(5, 0)
         second(7, 0)
+        quant("h", 2, 1)
+        quant("h", 3, 1)
         finish(6, 0)
         finish(7, 0)
         second(0, 1)

@@ -160,9 +160,10 @@ def tile_kalman_predicted_covariance_d2_kernel(tc, P_bytes, P_scale, F_bytes, F_
             cols = slice(256 * (pair % 2), 256 * (pair % 2) + 256)
             nc.vector.quantize_mx(out=c[:, cols].bitcast(FP8X4), scales=s[:, cols], in_=grouped[(kind, pair, k)][:])
 
-        def product(key, b, k, moving):
+        def product(key, b, k, moving, cols=slice(0, 512)):
+            width = cols.stop - cols.start
             if k == 0:
-                take_bank(key, [P, 512])
+                take_bank(key, [P, width])
             fc, fs = codes["F%d%d" % (b // 4, k)]
             rows_m = slice(P * (b % 4), P * (b % 4) + P)
             c, s = codes[moving]
@@ -170,8 +171,8 @@ def tile_kalman_predicted_covariance_d2_kernel(tc, P_bytes, P_scale, F_bytes, F_
                 out=banks[key][:],
                 lhsT=fc[:, rows_m].bitcast(FP8X4),
                 lhsT_scale=fs[:, rows_m],
-                rhs=c[:].bitcast(FP8X4),
-                rhs_scale=s[:],
+                rhs=c[:, cols].bitcast(FP8X4),
+                rhs_scale=s[:, cols],
                 start=(k == 0),
                 stop=(k == 1),
             )
@@ -180,9 +181,9 @@ def tile_kalman_predicted_covariance_d2_kernel(tc, P_bytes, P_scale, F_bytes, F_
             for k in passes:
                 product(("H", b, gi), b, k, "P%d%d" % (gi, k))
 
-        def second(m, nh, passes=(0, 1)):
+        def second(m, nh, passes=(0, 1), cols=slice(0, 512)):
             for k in passes:
-                product(("Y", m, nh), m, k, "h%d%d" % (nh, k))
+                product(("Y", m, nh, cols.start), m, k, "h%d%d" % (nh, k), cols)
 
         def gain(b, gi, on_vector=False):
             hw = keep.tile([P, 512], BF16, name="h_wide%d%d" % (b, gi), align_bytes=64)
@@ -195,21 +196,20 @@ def tile_kalman_predicted_covariance_d2_kernel(tc, P_bytes, P_scale, F_bytes, F_
                 nc.scalar.activation(out=dst, in_=src, func=COPY, scale=g_col[:, b : b + 1])
             give_bank(("H", b, gi))
 
-        def finish(m, nh, parts=1):
-            width = 512 // parts
-            for j in range(parts):
-                res = keep.tile([P, width], F32, name="res_%d%d%d" % (m, nh, j))
-                cols = slice(512 * nh + width * j, 512 * nh + width * j + width)
-                nc.vector.scalar_tensor_tensor(
-                    out=res[:],
-                    in0=banks[("Y", m, nh)][:, width * j : width * j + width],
-                    scalar=g_col[:, m : m + 1],
-                    in1=q_tiles[m // 2][:, m % 2, cols],
-                    op0=MULT,
-                    op1=ADD,
-                )
-                nc.sync.dma_start(out=out[P * m : P * m + P, cols], in_=res[:])
-            give_bank(("Y", m, nh))
+        def finish(m, nh, cols=slice(0, 512), queue=nc.sync):
+            key = ("Y", m, nh, cols.start)
+            res = keep.tile([P, cols.stop - cols.start], F32, name="res_%d%d%d" % (m, nh, cols.start))
+            out_cols = slice(512 * nh + cols.start, 512 * nh + cols.stop)
+            nc.vector.scalar_tensor_tensor(
+                out=res[:],
+                in0=banks[key][:],
+                scalar=g_col[:, m : m + 1],
+                in1=q_tiles[m // 2][:, m % 2, out_cols],
+                op0=MULT,
+                op1=ADD,
+            )
+            give_bank(key)
+            queue.dma_start(out=out[P * m : P * m + P, out_cols], in_=res[:])
 
         gain_column()
         widen("P", 0, 0, 0)
@@ -368,25 +368,27 @@ def tile_kalman_predicted_covariance_d2_kernel(tc, P_bytes, P_scale, F_bytes, F_
         empty("h", 3, 1)
         quant("h", 2, 0)
         quant("h", 3, 0)
+        quant("h", 2, 1)
         finish(5, 0)
         second(7, 0)
-        quant("h", 2, 1)
         quant("h", 3, 1)
-        finish(6, 0)
+        finish(6, 0, queue=nc.scalar)
         finish(7, 0)
         second(0, 1)
-        finish(0, 1)
+        finish(0, 1, queue=nc.scalar)
         second(1, 1)
         finish(1, 1)
         second(2, 1)
-        finish(2, 1)
+        finish(2, 1, queue=nc.scalar)
         second(3, 1)
         finish(3, 1)
         second(4, 1)
-        finish(4, 1)
+        finish(4, 1, queue=nc.scalar)
         second(5, 1)
         finish(5, 1)
         second(6, 1)
-        finish(6, 1)
-        second(7, 1)
-        finish(7, 1, 2)
+        finish(6, 1, queue=nc.scalar)
+        second(7, 1, cols=slice(0, 256))
+        second(7, 1, cols=slice(256, 512))
+        finish(7, 1, slice(0, 256))
+        finish(7, 1, slice(256, 512), nc.scalar)

@@ -18,7 +18,7 @@ ADD = mybir.AluOpType.add
 COPY = mybir.ActivationFunctionType.Copy
 
 RUN = (2, 16)
-LOADS = [("P", 0, (0,)), ("F", 0, (0,)), ("P", 1, (0,)), ("F", 1, (0,)), ("P", 0, (1,)), ("P", 1, (1,)), ("P", 2, (0, 1)), ("F", 0, (1,)), ("F", 1, (1,)), ("P", 3, (0, 1)), ("F", 2, (0, 1)), ("F", 3, (0, 1))]
+LOADS = [("P", 0, (0,)), ("P", 1, (0,)), ("F", 0, (0,)), ("F", 1, (0,)), ("P", 0, (1,)), ("P", 1, (1,)), ("P", 2, (0, 1)), ("F", 0, (1,)), ("F", 1, (1,)), ("P", 3, (0, 1)), ("F", 2, (0, 1)), ("F", 3, (0, 1))]
 
 
 def tile_kalman_predicted_covariance_d2_kernel(tc, P_bytes, P_scale, F_bytes, F_scale, g, Q, out):
@@ -30,8 +30,8 @@ def tile_kalman_predicted_covariance_d2_kernel(tc, P_bytes, P_scale, F_bytes, F_
 
         g_rows = keep.tile([P, P], BF16, name="g_rows")
         nc.vector.memset(g_rows[:], 0.0)
-        f_list = keep.tile([P, 1], F32, name="f_list")
-        nc.vector.memset(f_list[:], 0.0)
+        f_row = keep.tile([P, 64], F32, name="f_row")
+        nc.vector.memset(f_row[:], 0.0)
         ident = keep.tile([P, P], F32, name="ident")
         make_identity(nc, ident[:])
 
@@ -41,7 +41,7 @@ def tile_kalman_predicted_covariance_d2_kernel(tc, P_bytes, P_scale, F_bytes, F_
             tile_s = keep.tile([P, 2, 16], F32, name="p_scale%d" % half)
             p_scale.append(tile_s)
         nc.scalar.dma_start(out=p_scale[0][:], in_=p_scales[:, 0:2, :])
-        nc.scalar.dma_start(out=f_list[0:64, :], in_=F_scale.rearrange("b (c o) -> (b c) o", o=1))
+        nc.scalar.dma_start(out=f_row[0:1, :], in_=F_scale.rearrange("(o b) c -> o (b c)", o=1))
         nc.scalar.dma_start(out=g_rows[0:8, :], in_=g.rearrange("(b p) -> b p", p=P))
 
         rows = {
@@ -50,9 +50,9 @@ def tile_kalman_predicted_covariance_d2_kernel(tc, P_bytes, P_scale, F_bytes, F_
         }
         raw = {}
         scale = {}
-        spread = keep.tile([P, 136], F32, name="spread")
+        spread = keep.tile([P, 72], F32, name="spread")
         f_scale = spread[:, 0:64]
-        g_col = spread[:, 128:136]
+        g_col = spread[:, 64:72]
         for kind, pair, halves in LOADS:
             cols = slice(512 * halves[0], 512 * halves[-1] + 512)
             part = keep.tile([P, 2, 512 * len(halves)], U8, name="bytes_%s%d%d" % (kind, pair, halves[0]))
@@ -109,9 +109,9 @@ def tile_kalman_predicted_covariance_d2_kernel(tc, P_bytes, P_scale, F_bytes, F_
 
         def gain_column():
             bank = take_bank("spread", [P, 512])
-            nc.tensor.transpose(bank[:, 0:P], f_list[:].to_broadcast([P, P]), ident[:])
-            nc.tensor.matmul(bank[:, P : P + 8], lhsT=g_rows[:], rhs=pick[:], start=True, stop=True)
-            nc.scalar.activation(out=spread[:], in_=bank[:, 0:136], func=COPY)
+            nc.tensor.matmul(bank[:, 0:64], lhsT=ident[:, 0:1].to_broadcast([P, P]), rhs=f_row[:], start=True, stop=True)
+            nc.tensor.matmul(bank[:, 64:72], lhsT=g_rows[:], rhs=pick[:], start=True, stop=True)
+            nc.scalar.activation(out=spread[:], in_=bank[:, 0:72], func=COPY)
             give_bank("spread")
 
         def widen(kind, pair, k, e, on_scalar=False):
@@ -211,30 +211,32 @@ def tile_kalman_predicted_covariance_d2_kernel(tc, P_bytes, P_scale, F_bytes, F_
             give_bank(key)
             queue.dma_start(out=out[P * m : P * m + P, out_cols], in_=res[:])
 
-        gain_column()
         widen("P", 0, 0, 0)
         widen("P", 0, 0, 1, True)
-        widen("F", 0, 0, 0)
-        turn("P", 0, 0)
-        widen("F", 0, 0, 1, True)
+        gain_column()
         widen("P", 1, 0, 0)
         widen("P", 1, 0, 1)
-        turn("F", 0, 0)
-        turn("P", 1, 0)
+        turn("P", 0, 0, (0,))
+        turn("P", 1, 0, (0,))
+        turn("P", 0, 0, (1,))
+        turn("P", 1, 0, (1,))
+        widen("F", 0, 0, 1, True)
+        widen("F", 0, 0, 0)
         widen("F", 1, 0, 0)
         widen("F", 1, 0, 1, True)
+        turn("F", 0, 0)
         empty("P", 0, 0)
         widen("P", 0, 1, 0)
         widen("P", 0, 1, 1)
-        empty("F", 0, 0)
+        empty("P", 1, 0)
         turn("F", 1, 0)
         turn("P", 0, 1)
-        empty("P", 1, 0)
+        empty("F", 0, 0)
         widen("P", 1, 1, 0)
         widen("P", 1, 1, 1)
         quant("P", 0, 0)
-        quant("F", 0, 0)
         quant("P", 1, 0)
+        quant("F", 0, 0)
         turn("P", 1, 1)
         widen("P", 2, 0, 0, True)
         widen("P", 2, 0, 1, True)
@@ -372,23 +374,23 @@ def tile_kalman_predicted_covariance_d2_kernel(tc, P_bytes, P_scale, F_bytes, F_
         finish(5, 0)
         second(7, 0)
         quant("h", 3, 1)
-        finish(6, 0, queue=nc.scalar)
+        finish(6, 0)
         finish(7, 0)
         second(0, 1)
-        finish(0, 1, queue=nc.scalar)
+        finish(0, 1)
         second(1, 1)
         finish(1, 1)
         second(2, 1)
-        finish(2, 1, queue=nc.scalar)
+        finish(2, 1)
         second(3, 1)
         finish(3, 1)
         second(4, 1)
-        finish(4, 1, queue=nc.scalar)
+        finish(4, 1)
         second(5, 1)
         finish(5, 1)
         second(6, 1)
-        finish(6, 1, queue=nc.scalar)
+        finish(6, 1)
         second(7, 1, cols=slice(0, 256))
         second(7, 1, cols=slice(256, 512))
         finish(7, 1, slice(0, 256))
-        finish(7, 1, slice(256, 512), nc.scalar)
+        finish(7, 1, slice(256, 512))

@@ -74,7 +74,7 @@ def tile_kalman_predicted_covariance_d2_kernel(tc, P_bytes, P_scale, F_bytes, F_
             q_tiles.append(qt)
 
         pick = keep.tile([P, 8], BF16, name="pick")
-        nc.vector.tensor_copy(out=pick[:], in_=ident[:, 0:8])
+        nc.scalar.activation(out=pick[:], in_=ident[:, 0:8], func=COPY)
 
         wide = {}
         plain = set()
@@ -216,10 +216,8 @@ def tile_kalman_predicted_covariance_d2_kernel(tc, P_bytes, P_scale, F_bytes, F_
         gain_column()
         widen("P", 1, 0, 0)
         widen("P", 1, 0, 1)
-        turn("P", 0, 0, (0,))
-        turn("P", 1, 0, (0,))
-        turn("P", 0, 0, (1,))
-        turn("P", 1, 0, (1,))
+        turn("P", 0, 0)
+        turn("P", 1, 0)
         widen("F", 0, 0, 1, True)
         widen("F", 0, 0, 0)
         widen("F", 1, 0, 0)
@@ -229,43 +227,43 @@ def tile_kalman_predicted_covariance_d2_kernel(tc, P_bytes, P_scale, F_bytes, F_
         widen("P", 0, 1, 0)
         widen("P", 0, 1, 1)
         empty("P", 1, 0)
-        turn("F", 1, 0)
         turn("P", 0, 1)
+        turn("F", 1, 0)
         empty("F", 0, 0)
         widen("P", 1, 1, 0)
-        widen("P", 1, 1, 1)
         quant("P", 0, 0)
+        widen("P", 1, 1, 1)
         quant("P", 1, 0)
         quant("F", 0, 0)
         turn("P", 1, 1)
         widen("P", 2, 0, 0, True)
+        empty("P", 0, 1)
         widen("P", 2, 0, 1, True)
-        widen("F", 0, 1, 0)
-        widen("F", 0, 1, 1)
         first(0, 0, (0,))
         first(1, 0, (0,))
-        empty("F", 1, 0)
-        turn("F", 0, 1)
-        turn("P", 2, 0)
+        widen("F", 0, 1, 0)
+        widen("F", 0, 1, 1)
         widen("F", 1, 1, 0)
         widen("F", 1, 1, 1)
-        empty("P", 0, 1)
-        quant("F", 1, 0)
+        empty("F", 1, 0)
+        turn("P", 2, 0)
+        turn("F", 0, 1)
+        turn("F", 1, 1)
         empty("P", 1, 1)
+        widen("P", 3, 0, 0)
+        widen("P", 3, 0, 1)
+        quant("F", 1, 0)
+        empty("F", 0, 1)
+        turn("P", 3, 0)
         widen("P", 2, 1, 0)
         widen("P", 2, 1, 1)
         first(2, 0, (0,))
         first(3, 0, (0,))
-        turn("F", 1, 1)
-        empty("F", 0, 1)
+        empty("F", 1, 1)
         quant("P", 0, 1)
         quant("P", 1, 1)
-        turn("P", 2, 1)
-        widen("P", 3, 0, 0)
-        widen("P", 3, 0, 1)
-        empty("F", 1, 1)
         quant("F", 0, 1)
-        turn("P", 3, 0)
+        turn("P", 2, 1)
         empty("P", 2, 0)
         widen("P", 3, 1, 0)
         widen("P", 3, 1, 1)
@@ -274,68 +272,70 @@ def tile_kalman_predicted_covariance_d2_kernel(tc, P_bytes, P_scale, F_bytes, F_
         quant("F", 1, 1)
         empty("P", 3, 0)
         turn("P", 3, 1)
-        widen("F", 2, 0, 0)
-        widen("F", 2, 0, 1)
         empty("P", 2, 1)
-        first(2, 0, (1,))
-        first(3, 0, (1,))
         quant("P", 2, 0)
         quant("P", 3, 0)
-        empty("P", 3, 1)
-        turn("F", 2, 0)
-        gain(0, 0)
+        first(2, 0, (1,))
+        first(3, 0, (1,))
         quant("P", 2, 1)
+        widen("F", 2, 0, 0)
         first(0, 1, (0,))
         first(1, 1, (0,))
-        quant("P", 3, 1)
         first(2, 1, (0,))
-        gain(1, 0)
+        empty("P", 3, 1)
         first(3, 1, (0,))
-        widen("F", 2, 1, 0)
-        widen("F", 2, 1, 1)
-        first(0, 1, (1,))
-        first(1, 1, (1,))
-        gain(2, 0)
-        first(2, 1, (1,))
+        quant("P", 3, 1)
+        widen("F", 2, 0, 1)
+        gain(0, 0)
+        gain(1, 0)
         widen("F", 3, 0, 0)
         widen("F", 3, 0, 1)
-        gain(3, 0)
+        first(0, 1, (1,))
+        first(1, 1, (1,))
+        first(2, 1, (1,))
         first(3, 1, (1,))
-        empty("F", 2, 0)
-        turn("F", 2, 1)
-        turn("F", 3, 0)
-        turn("h", 0, 0)
-        turn("h", 1, 0)
-        gain(0, 1, True)
-        gain(1, 1)
+        widen("F", 2, 1, 0)
+        widen("F", 2, 1, 1)
+        gain(2, 0)
+        gain(3, 0)
         widen("F", 3, 1, 0)
         widen("F", 3, 1, 1)
-        quant("F", 2, 0)
-        empty("F", 2, 1)
+        turn("h", 0, 0)
+        turn("F", 2, 0)
+        turn("F", 3, 0)
+        turn("h", 1, 0)
+        gain(0, 1)
+        turn("F", 2, 1)
+        gain(1, 1)
         gain(2, 1, True)
+        turn("F", 3, 1)
+        empty("F", 2, 0, True)
+        turn("h", 0, 1)
+        gain(3, 1)
+        turn("h", 1, 1)
+        quant("F", 2, 0)
+        empty("F", 3, 0)
+        empty("F", 2, 1, True)
         first(4, 0, (0,))
         first(5, 0, (0,))
-        gain(3, 1)
-        turn("F", 3, 1)
-        turn("h", 0, 1)
-        turn("h", 1, 1)
-        empty("F", 3, 0)
+        first(4, 1, (0,))
+        empty("h", 0, 0)
+        first(5, 1, (0,))
+        quant("F", 3, 0)
         quant("F", 2, 1)
-        empty("h", 0, 0, True)
-        empty("F", 3, 1)
+        empty("h", 1, 0)
         first(4, 0, (1,))
         first(5, 0, (1,))
-        first(4, 1)
-        empty("h", 1, 0)
-        quant("F", 3, 0)
+        first(4, 1, (1,))
+        first(5, 1, (1,))
+        empty("F", 3, 1)
         quant("h", 0, 0)
-        first(5, 1)
         empty("h", 0, 1, True)
-        quant("F", 3, 1)
-        empty("h", 1, 1)
         quant("h", 1, 0)
-        quant("h", 0, 1)
+        empty("h", 1, 1)
+        quant("F", 3, 1)
         first(6, 0)
+        quant("h", 0, 1)
         gain(4, 0)
         quant("h", 1, 1)
         gain(5, 0, True)

@@ -107,6 +107,12 @@ def tile_kalman_predicted_covariance_d2_kernel(tc, P_bytes, P_scale, F_bytes, F_
                 mx_tiles("F%d%d" % (a, k), 512)
                 mx_tiles("h%d%d" % (a, k), 512)
 
+        for kind, count, width in [("P", 2, 2 * N), ("F", 4, N), ("h", 2, 2 * N)]:
+            for a in range(count):
+                for k in range(2):
+                    gr = keep.tile([P, width], BF16, name="grouped_%s%d%d" % (kind, a, k), align_bytes=64)
+                    grouped[(kind, a, k)] = gr
+
         def gain_column():
             bank = take_bank("spread", [P, 512])
             nc.tensor.matmul(bank[:, 0:64], lhsT=ident[:, 0:1].to_broadcast([P, P]), rhs=f_row[:], start=True, stop=True)
@@ -139,9 +145,10 @@ def tile_kalman_predicted_covariance_d2_kernel(tc, P_bytes, P_scale, F_bytes, F_
                     nc.tensor.transpose(bank[:, e, u, :], half, ident[:])
 
         def empty(kind, pair, k, on_vector=False):
-            gr = keep.tile([P, N], BF16, name="grouped_%s%d%d" % (kind, pair, k), align_bytes=64)
-            grouped[(kind, pair, k)] = gr
-            words = gr[:].bitcast(F32)
+            if kind == "F":
+                words = grouped[("F", pair, k)][:].bitcast(F32)
+            else:
+                words = grouped[(kind, pair // 2, k)][:, N * (pair % 2) : N * (pair % 2) + N].bitcast(F32)
             bank = banks[(kind, pair, k)]
             if kind == "P":
                 dst = words.rearrange("p (r e u) -> p r e u", e=2, u=2)
@@ -155,10 +162,14 @@ def tile_kalman_predicted_covariance_d2_kernel(tc, P_bytes, P_scale, F_bytes, F_
                 nc.scalar.copy(out=dst, in_=src)
             give_bank((kind, pair, k))
 
-        def quant(kind, pair, k):
-            c, s = codes["%s%d%d" % (kind, pair // 2, k)]
-            cols = slice(256 * (pair % 2), 256 * (pair % 2) + 256)
-            nc.vector.quantize_mx(out=c[:, cols].bitcast(FP8X4), scales=s[:, cols], in_=grouped[(kind, pair, k)][:])
+        def quant(kind, a, k):
+            if kind == "F":
+                c, s = codes["F%d%d" % (a // 2, k)]
+                cols = slice(256 * (a % 2), 256 * (a % 2) + 256)
+            else:
+                c, s = codes["%s%d%d" % (kind, a, k)]
+                cols = slice(0, 512)
+            nc.vector.quantize_mx(out=c[:, cols].bitcast(FP8X4), scales=s[:, cols], in_=grouped[(kind, a, k)][:])
 
         def product(key, b, k, moving, cols=slice(0, 512)):
             width = cols.stop - cols.start
@@ -227,136 +238,130 @@ def tile_kalman_predicted_covariance_d2_kernel(tc, P_bytes, P_scale, F_bytes, F_
         widen("P", 0, 1, 0)
         widen("P", 0, 1, 1)
         empty("P", 1, 0)
-        turn("P", 0, 1)
         turn("F", 1, 0)
+        turn("P", 0, 1)
         empty("F", 0, 0)
         widen("P", 1, 1, 0)
-        quant("P", 0, 0)
         widen("P", 1, 1, 1)
-        quant("P", 1, 0)
-        quant("F", 0, 0)
+        quant("P", 0, 0)
         turn("P", 1, 1)
+        quant("F", 0, 0)
         widen("P", 2, 0, 0, True)
+        widen("P", 3, 0, 0, True)
+        empty("F", 1, 0)
         empty("P", 0, 1)
-        widen("P", 2, 0, 1, True)
-        first(0, 0, (0,))
-        first(1, 0, (0,))
+        empty("P", 1, 1)
         widen("F", 0, 1, 0)
         widen("F", 0, 1, 1)
-        widen("F", 1, 1, 0)
-        widen("F", 1, 1, 1)
-        empty("F", 1, 0)
-        turn("P", 2, 0)
-        turn("F", 0, 1)
-        turn("F", 1, 1)
-        empty("P", 1, 1)
-        widen("P", 3, 0, 0)
+        first(0, 0, (0,))
+        first(1, 0, (0,))
         widen("P", 3, 0, 1)
-        quant("F", 1, 0)
-        empty("F", 0, 1)
+        turn("F", 0, 1)
         turn("P", 3, 0)
         widen("P", 2, 1, 0)
         widen("P", 2, 1, 1)
+        quant("F", 1, 0)
+        turn("P", 2, 1)
         first(2, 0, (0,))
         first(3, 0, (0,))
-        empty("F", 1, 1)
+        widen("F", 1, 1, 0)
+        widen("F", 1, 1, 1)
+        widen("P", 2, 0, 1, True)
         quant("P", 0, 1)
-        quant("P", 1, 1)
-        quant("F", 0, 1)
-        turn("P", 2, 1)
-        empty("P", 2, 0)
+        empty("F", 0, 1)
+        empty("P", 3, 0)
+        turn("F", 1, 1)
+        turn("P", 2, 0)
         widen("P", 3, 1, 0)
+        quant("F", 0, 1)
+        empty("F", 1, 1)
         widen("P", 3, 1, 1)
         first(0, 0, (1,))
         first(1, 0, (1,))
-        quant("F", 1, 1)
-        empty("P", 3, 0)
+        empty("P", 2, 0)
+        widen("F", 3, 0, 0)
         turn("P", 3, 1)
+        quant("F", 1, 1)
         empty("P", 2, 1)
-        quant("P", 2, 0)
-        quant("P", 3, 0)
+        quant("P", 1, 0)
         first(2, 0, (1,))
         first(3, 0, (1,))
-        quant("P", 2, 1)
+        gain(0, 0)
+        empty("P", 3, 1)
         widen("F", 2, 0, 0)
+        widen("F", 2, 0, 1)
         first(0, 1, (0,))
         first(1, 1, (0,))
-        first(2, 1, (0,))
-        empty("P", 3, 1)
-        first(3, 1, (0,))
-        quant("P", 3, 1)
-        widen("F", 2, 0, 1)
-        gain(0, 0)
         gain(1, 0)
-        widen("F", 3, 0, 0)
+        quant("P", 1, 1)
+        first(2, 1, (0,))
+        gain(2, 0)
+        first(3, 1, (0,))
+        turn("F", 2, 0)
         widen("F", 3, 0, 1)
+        gain(3, 0)
+        empty("F", 2, 0)
         first(0, 1, (1,))
         first(1, 1, (1,))
         first(2, 1, (1,))
         first(3, 1, (1,))
         widen("F", 2, 1, 0)
         widen("F", 2, 1, 1)
-        gain(2, 0)
-        gain(3, 0)
+        quant("F", 2, 0)
         widen("F", 3, 1, 0)
         widen("F", 3, 1, 1)
-        turn("h", 0, 0)
-        turn("F", 2, 0)
-        turn("F", 3, 0)
-        turn("h", 1, 0)
-        gain(0, 1)
         turn("F", 2, 1)
+        turn("F", 3, 0)
+        gain(0, 1)
         gain(1, 1)
-        gain(2, 1, True)
+        turn("h", 0, 0)
         turn("F", 3, 1)
-        empty("F", 2, 0, True)
-        turn("h", 0, 1)
-        gain(3, 1)
-        turn("h", 1, 1)
-        quant("F", 2, 0)
-        empty("F", 3, 0)
         empty("F", 2, 1, True)
+        gain(2, 1)
         first(4, 0, (0,))
         first(5, 0, (0,))
-        first(4, 1, (0,))
-        empty("h", 0, 0)
-        first(5, 1, (0,))
-        quant("F", 3, 0)
         quant("F", 2, 1)
-        empty("h", 1, 0)
+        gain(3, 1)
+        first(4, 1, (0,))
+        first(5, 1, (0,))
+        empty("F", 3, 0, True)
+        empty("h", 0, 0)
+        turn("h", 1, 0)
+        empty("F", 3, 1)
+        turn("h", 0, 1)
+        quant("F", 3, 0)
+        turn("h", 1, 1)
         first(4, 0, (1,))
         first(5, 0, (1,))
+        empty("h", 1, 0)
+        quant("F", 3, 1)
         first(4, 1, (1,))
         first(5, 1, (1,))
-        empty("F", 3, 1)
-        quant("h", 0, 0)
         empty("h", 0, 1, True)
-        quant("h", 1, 0)
         empty("h", 1, 1)
-        quant("F", 3, 1)
+        quant("h", 0, 0)
         first(6, 0)
-        quant("h", 0, 1)
         gain(4, 0)
-        quant("h", 1, 1)
-        gain(5, 0, True)
-        gain(4, 1)
-        second(0, 0)
+        quant("h", 0, 1)
         first(7, 0)
-        gain(5, 1)
-        second(1, 0)
+        gain(5, 0)
         first(6, 1)
-        finish(0, 0)
-        gain(6, 0)
-        second(2, 0)
+        gain(4, 1)
+        gain(5, 1)
+        second(0, 0)
         first(7, 1)
-        finish(1, 0)
+        gain(6, 0, True)
+        second(1, 0)
         gain(7, 0)
-        second(3, 0)
-        finish(2, 0)
+        finish(0, 0)
+        second(2, 0)
         gain(6, 1)
+        finish(1, 0)
+        second(3, 0)
+        gain(7, 1)
+        finish(2, 0)
         second(4, 0)
         finish(3, 0)
-        gain(7, 1)
         turn("h", 2, 0)
         turn("h", 3, 0)
         turn("h", 2, 1)
@@ -368,12 +373,10 @@ def tile_kalman_predicted_covariance_d2_kernel(tc, P_bytes, P_scale, F_bytes, F_
         empty("h", 2, 1)
         second(6, 0)
         empty("h", 3, 1)
-        quant("h", 2, 0)
-        quant("h", 3, 0)
-        quant("h", 2, 1)
+        quant("h", 1, 0)
         finish(5, 0)
         second(7, 0)
-        quant("h", 3, 1)
+        quant("h", 1, 1)
         finish(6, 0)
         finish(7, 0)
         second(0, 1)

@@ -18,7 +18,7 @@ ADD = mybir.AluOpType.add
 COPY = mybir.ActivationFunctionType.Copy
 
 RUN = (2, 16)
-LOADS = [("P", 0, (0,)), ("P", 1, (0,)), ("F", 0, (0,)), ("F", 1, (0,)), ("P", 0, (1,)), ("P", 1, (1,)), ("P", 2, (0, 1)), ("F", 0, (1,)), ("F", 1, (1,)), ("P", 3, (0, 1)), ("F", 2, (0, 1)), ("F", 3, (0, 1))]
+LOADS = [("P", 0, (0, 1)), ("P", 1, (0, 1)), ("F", 0, (0, 1)), ("F", 1, (0, 1)), ("P", 2, (0, 1)), ("P", 3, (0, 1)), ("F", 2, (0, 1)), ("F", 3, (0, 1))]
 
 
 def tile_kalman_predicted_covariance_d2_kernel(tc, P_bytes, P_scale, F_bytes, F_scale, g, Q, out):
@@ -36,11 +36,13 @@ def tile_kalman_predicted_covariance_d2_kernel(tc, P_bytes, P_scale, F_bytes, F_
         make_identity(nc, ident[:])
 
         p_scales = P_scale.rearrange("(h m e) c -> m h (e c)", h=4, e=2)
-        p_scale = []
-        for half in range(2):
-            tile_s = keep.tile([P, 2, 16], F32, name="p_scale%d" % half)
-            p_scale.append(tile_s)
-        nc.scalar.dma_start(out=p_scale[0][:], in_=p_scales[:, 0:2, :])
+        p_scale = {}
+        for first_pair, count in [(0, 1), (1, 1), (2, 2)]:
+            tile_s = keep.tile([P, count, 16], F32, name="p_scale%d" % first_pair)
+            for j in range(count):
+                p_scale[first_pair + j] = tile_s[:, j, :]
+            p_scale[("tile", first_pair)] = (tile_s, count)
+        nc.scalar.dma_start(out=p_scale[("tile", 0)][0][:], in_=p_scales[:, 0:1, :])
         nc.scalar.dma_start(out=f_row[0:1, :], in_=F_scale.rearrange("(o b) c -> o (b c)", o=1))
         nc.scalar.dma_start(out=g_rows[0:8, :], in_=g.rearrange("(b p) -> b p", p=P))
 
@@ -56,15 +58,16 @@ def tile_kalman_predicted_covariance_d2_kernel(tc, P_bytes, P_scale, F_bytes, F_
         for kind, pair, halves in LOADS:
             cols = slice(512 * halves[0], 512 * halves[-1] + 512)
             part = keep.tile([P, 2, 512 * len(halves)], U8, name="bytes_%s%d%d" % (kind, pair, halves[0]))
-            if (kind, pair) == ("P", 2):
-                nc.sync.dma_start(out=p_scale[1][:], in_=p_scales[:, 2:4, :])
+            if kind == "P" and pair in (1, 2) and halves[0] == 0:
+                tile_s, count = p_scale[("tile", pair)]
+                nc.sync.dma_start(out=tile_s[:], in_=p_scales[:, pair : pair + count, :])
             nc.sync.dma_start(out=part[:], in_=rows[kind][:, pair, :, cols])
             for e in range(2):
                 for i, k in enumerate(halves):
                     raw[(kind, pair, k, e)] = part[:, e, 512 * i : 512 * i + 512]
         for pair in range(4):
             for e in range(2):
-                scale[("P", pair, e)] = p_scale[pair // 2][:, pair % 2, 8 * e : 8 * e + 8]
+                scale[("P", pair, e)] = p_scale[pair][:, 8 * e : 8 * e + 8]
                 scale[("F", pair, e)] = f_scale[:, 16 * pair + 8 * e : 16 * pair + 8 * e + 8]
         q_rows = Q.rearrange("(b p) n -> p b n", p=P)
         q_tiles = []
@@ -117,7 +120,9 @@ def tile_kalman_predicted_covariance_d2_kernel(tc, P_bytes, P_scale, F_bytes, F_
             bank = take_bank("spread", [P, 512])
             nc.tensor.matmul(bank[:, 0:64], lhsT=ident[:, 0:1].to_broadcast([P, P]), rhs=f_row[:], start=True, stop=True)
             nc.tensor.matmul(bank[:, 64:72], lhsT=g_rows[:], rhs=pick[:], start=True, stop=True)
-            nc.scalar.activation(out=spread[:], in_=bank[:, 0:72], func=COPY)
+
+        def copy_spread():
+            nc.vector.tensor_copy(out=spread[:], in_=banks["spread"][:, 0:72])
             give_bank("spread")
 
         def widen(kind, pair, k, e, on_scalar=False):
@@ -224,129 +229,131 @@ def tile_kalman_predicted_covariance_d2_kernel(tc, P_bytes, P_scale, F_bytes, F_
 
         widen("P", 0, 0, 0)
         widen("P", 0, 0, 1, True)
-        gain_column()
-        widen("P", 1, 0, 0)
-        widen("P", 1, 0, 1)
-        turn("P", 0, 0)
-        turn("P", 1, 0)
-        widen("F", 0, 0, 1, True)
-        widen("F", 0, 0, 0)
-        widen("F", 1, 0, 0)
-        widen("F", 1, 0, 1, True)
-        turn("F", 0, 0)
-        empty("P", 0, 0)
         widen("P", 0, 1, 0)
         widen("P", 0, 1, 1)
-        empty("P", 1, 0)
-        turn("F", 1, 0)
+        turn("P", 0, 0)
+        gain_column()
         turn("P", 0, 1)
-        empty("F", 0, 0)
+        widen("P", 1, 0, 0, True)
+        widen("P", 1, 0, 1)
         widen("P", 1, 1, 0)
+        copy_spread()
         widen("P", 1, 1, 1)
-        quant("P", 0, 0)
+        turn("P", 1, 0)
         turn("P", 1, 1)
-        quant("F", 0, 0)
-        widen("P", 2, 0, 0, True)
-        widen("P", 3, 0, 0, True)
-        empty("F", 1, 0)
-        empty("P", 0, 1)
-        empty("P", 1, 1)
+        widen("F", 0, 0, 1, True)
+        widen("F", 0, 0, 0)
         widen("F", 0, 1, 0)
         widen("F", 0, 1, 1)
+        empty("P", 0, 0)
+        turn("F", 0, 0)
+        turn("F", 0, 1)
+        empty("P", 1, 0)
+        widen("F", 1, 0, 0)
+        widen("F", 1, 0, 1)
+        widen("F", 1, 1, 0)
+        widen("F", 1, 1, 1)
+        empty("F", 0, 0)
+        turn("F", 1, 0)
+        quant("P", 0, 0)
+        empty("P", 0, 1)
+        widen("P", 2, 0, 1, True)
+        quant("F", 0, 0)
+        widen("P", 2, 0, 0)
+        turn("F", 1, 1)
+        empty("P", 1, 1)
+        widen("P", 3, 0, 0)
+        widen("P", 3, 0, 1)
+        empty("F", 1, 0)
         first(0, 0, (0,))
         first(1, 0, (0,))
-        widen("P", 3, 0, 1)
-        turn("F", 0, 1)
+        turn("P", 2, 0)
         turn("P", 3, 0)
+        empty("F", 0, 1)
         widen("P", 2, 1, 0)
         widen("P", 2, 1, 1)
         quant("F", 1, 0)
+        empty("F", 1, 1)
+        widen("P", 3, 1, 0)
+        widen("P", 3, 1, 1)
         turn("P", 2, 1)
+        quant("P", 0, 1)
+        empty("P", 2, 0)
         first(2, 0, (0,))
         first(3, 0, (0,))
-        widen("F", 1, 1, 0)
-        widen("F", 1, 1, 1)
-        widen("P", 2, 0, 1, True)
-        quant("P", 0, 1)
-        empty("F", 0, 1)
-        empty("P", 3, 0)
-        turn("F", 1, 1)
-        turn("P", 2, 0)
-        widen("P", 3, 1, 0)
+        turn("P", 3, 1)
         quant("F", 0, 1)
-        empty("F", 1, 1)
-        widen("P", 3, 1, 1)
+        empty("P", 3, 0)
+        quant("F", 1, 1)
         first(0, 0, (1,))
         first(1, 0, (1,))
-        empty("P", 2, 0)
-        widen("F", 3, 0, 0)
-        turn("P", 3, 1)
-        quant("F", 1, 1)
         empty("P", 2, 1)
         quant("P", 1, 0)
         first(2, 0, (1,))
         first(3, 0, (1,))
-        gain(0, 0)
         empty("P", 3, 1)
         widen("F", 2, 0, 0)
-        widen("F", 2, 0, 1)
+        gain(0, 0)
         first(0, 1, (0,))
         first(1, 1, (0,))
-        gain(1, 0)
         quant("P", 1, 1)
         first(2, 1, (0,))
-        gain(2, 0)
+        gain(1, 0)
         first(3, 1, (0,))
-        turn("F", 2, 0)
-        widen("F", 3, 0, 1)
-        gain(3, 0)
-        empty("F", 2, 0)
+        widen("F", 2, 0, 1)
+        gain(2, 0)
         first(0, 1, (1,))
         first(1, 1, (1,))
         first(2, 1, (1,))
         first(3, 1, (1,))
         widen("F", 2, 1, 0)
         widen("F", 2, 1, 1)
-        quant("F", 2, 0)
+        gain(3, 0)
+        widen("F", 3, 0, 0)
+        widen("F", 3, 0, 1)
+        turn("F", 2, 0)
+        turn("F", 2, 1)
+        turn("h", 0, 0)
+        turn("h", 1, 0)
+        gain(0, 1)
+        gain(1, 1, True)
+        turn("F", 3, 0)
         widen("F", 3, 1, 0)
         widen("F", 3, 1, 1)
-        turn("F", 2, 1)
-        turn("F", 3, 0)
-        gain(0, 1)
-        gain(1, 1)
-        turn("h", 0, 0)
+        empty("F", 2, 0)
+        gain(2, 1, True)
+        turn("h", 0, 1)
+        gain(3, 1)
+        quant("F", 2, 0)
         turn("F", 3, 1)
-        empty("F", 2, 1, True)
-        gain(2, 1)
+        empty("F", 2, 1)
+        turn("h", 1, 1)
         first(4, 0, (0,))
         first(5, 0, (0,))
-        quant("F", 2, 1)
-        gain(3, 1)
-        first(4, 1, (0,))
-        first(5, 1, (0,))
-        empty("F", 3, 0, True)
         empty("h", 0, 0)
-        turn("h", 1, 0)
-        empty("F", 3, 1)
-        turn("h", 0, 1)
-        quant("F", 3, 0)
-        turn("h", 1, 1)
+        quant("F", 2, 1)
+        empty("F", 3, 0, True)
+        first(4, 1, (0,))
         first(4, 0, (1,))
-        first(5, 0, (1,))
         empty("h", 1, 0)
-        quant("F", 3, 1)
+        first(5, 0, (1,))
         first(4, 1, (1,))
-        first(5, 1, (1,))
+        quant("F", 3, 0)
+        empty("F", 3, 1)
+        first(5, 1, (0,))
         empty("h", 0, 1, True)
         empty("h", 1, 1)
+        quant("F", 3, 1)
+        first(5, 1, (1,))
+        first(6, 0, (0,))
         quant("h", 0, 0)
-        first(6, 0)
         gain(4, 0)
-        quant("h", 0, 1)
+        first(6, 0, (1,))
         first(7, 0)
+        quant("h", 0, 1)
         gain(5, 0)
         first(6, 1)
-        gain(4, 1)
+        gain(4, 1, True)
         gain(5, 1)
         second(0, 0)
         first(7, 1)
@@ -360,23 +367,23 @@ def tile_kalman_predicted_covariance_d2_kernel(tc, P_bytes, P_scale, F_bytes, F_
         second(3, 0)
         gain(7, 1)
         finish(2, 0)
-        second(4, 0)
-        finish(3, 0)
         turn("h", 2, 0)
         turn("h", 3, 0)
         turn("h", 2, 1)
         turn("h", 3, 1)
-        finish(4, 0)
+        finish(3, 0)
         empty("h", 2, 0)
         empty("h", 3, 0, True)
-        second(5, 0)
+        second(4, 0)
         empty("h", 2, 1)
-        second(6, 0)
+        second(5, 0)
         empty("h", 3, 1)
         quant("h", 1, 0)
+        finish(4, 0)
+        second(6, 0)
+        quant("h", 1, 1)
         finish(5, 0)
         second(7, 0)
-        quant("h", 1, 1)
         finish(6, 0)
         finish(7, 0)
         second(0, 1)

@@ -17,7 +17,7 @@ MULT = mybir.AluOpType.mult
 ADD = mybir.AluOpType.add
 COPY = mybir.ActivationFunctionType.Copy
 
-RUN = (2, 16)
+RUN = (2, 2)
 LOADS = [("P", 0, (0, 1)), ("P", 1, (0, 1)), ("F", 0, (0, 1)), ("F", 1, (0, 1)), ("P", 2, (0, 1)), ("P", 3, (0, 1)), ("F", 2, (0, 1)), ("F", 3, (0, 1))]
 
 
@@ -156,11 +156,11 @@ def tile_kalman_predicted_covariance_d2_kernel(tc, P_bytes, P_scale, F_bytes, F_
                 words = grouped[(kind, pair // 2, k)][:, N * (pair % 2) : N * (pair % 2) + N].bitcast(F32)
             bank = banks[(kind, pair, k)]
             if kind == "P":
-                dst = words.rearrange("p (r e u) -> p r e u", e=2, u=2)
-                src = bank[:].rearrange("p e u r -> p r e u")
+                both = grouped[(kind, pair // 2, k)][:].bitcast(F32)
+                dst = both.rearrange("p (e a r u) -> p a e r u", e=2, a=2, u=2)[:, pair % 2]
             else:
                 dst = words.rearrange("p (e r u) -> p e r u", e=2, u=2)
-                src = bank[:].rearrange("p e u r -> p e r u")
+            src = bank[:].rearrange("p e u r -> p e r u")
             if on_vector:
                 nc.vector.tensor_copy(out=dst, in_=src)
             else:
@@ -205,7 +205,7 @@ def tile_kalman_predicted_covariance_d2_kernel(tc, P_bytes, P_scale, F_bytes, F_
             hw = keep.tile([P, 512], BF16, name="h_wide%d%d" % (b, gi), align_bytes=64)
             wide[("h", b // 2, gi, b % 2)] = hw
             dst = hw[:].rearrange("p (u q x) -> p u q x", u=2, x=RUN[gi])
-            src = banks[("H", b, gi)][:].rearrange("p (q u x) -> p u q x", u=2, x=RUN[gi])
+            src = banks[("H", b, gi)][:].rearrange("p (x q u) -> p u q x", u=2, x=2)
             if on_vector:
                 nc.vector.tensor_scalar(out=dst, in0=src, scalar1=g_col[:, b : b + 1], scalar2=None, op0=MULT)
             else:
@@ -341,7 +341,7 @@ def tile_kalman_predicted_covariance_d2_kernel(tc, P_bytes, P_scale, F_bytes, F_
         quant("F", 3, 0)
         empty("F", 3, 1)
         first(5, 1, (0,))
-        empty("h", 0, 1, True)
+        empty("h", 0, 1)
         empty("h", 1, 1)
         quant("F", 3, 1)
         first(5, 1, (1,))
@@ -357,33 +357,33 @@ def tile_kalman_predicted_covariance_d2_kernel(tc, P_bytes, P_scale, F_bytes, F_
         gain(5, 1)
         second(0, 0)
         first(7, 1)
-        gain(6, 0, True)
+        gain(6, 0)
         second(1, 0)
-        gain(7, 0)
         finish(0, 0)
+        gain(7, 0)
         second(2, 0)
-        gain(6, 1)
         finish(1, 0)
+        gain(6, 1)
         second(3, 0)
-        gain(7, 1)
         finish(2, 0)
+        gain(7, 1)
+        second(4, 0)
+        finish(3, 0)
         turn("h", 2, 0)
         turn("h", 3, 0)
         turn("h", 2, 1)
         turn("h", 3, 1)
-        finish(3, 0)
+        finish(4, 0)
         empty("h", 2, 0)
         empty("h", 3, 0, True)
-        second(4, 0)
-        empty("h", 2, 1)
         second(5, 0)
+        empty("h", 2, 1)
+        second(6, 0)
         empty("h", 3, 1)
         quant("h", 1, 0)
-        finish(4, 0)
-        second(6, 0)
-        quant("h", 1, 1)
         finish(5, 0)
         second(7, 0)
+        quant("h", 1, 1)
         finish(6, 0)
         finish(7, 0)
         second(0, 1)

@@ -5,6 +5,7 @@ from concourse.masks import make_identity
 
 N = 1024
 P = 128
+PASS = 512
 FLOPS = 2 * 2 * N * N * N
 
 F32 = mybir.dt.float32
@@ -17,8 +18,10 @@ MULT = mybir.AluOpType.mult
 ADD = mybir.AluOpType.add
 COPY = mybir.ActivationFunctionType.Copy
 
-RUN = (2, 2)
-LOADS = [("P", 0, (0, 1)), ("P", 1, (0, 1)), ("F", 0, (0, 1)), ("F", 1, (0, 1)), ("P", 2, (0, 1)), ("P", 3, (0, 1)), ("F", 2, (0, 1)), ("F", 3, (0, 1))]
+LOADS = [("P", 0), ("P", 1), ("F", 0), ("F", 1), ("P", 2), ("P", 3), ("F", 2), ("F", 3)]
+SHARED = [("P", 0, 0), ("P", 1, 0), ("F", 0, 0), ("P", 2, 0)]
+EMPTY_LAG = 4
+EARLY_TILES = 5
 
 
 def tile_kalman_predicted_covariance_d2_kernel(tc, P_bytes, P_scale, F_bytes, F_scale, g, Q, out):
@@ -35,58 +38,64 @@ def tile_kalman_predicted_covariance_d2_kernel(tc, P_bytes, P_scale, F_bytes, F_
         ident = keep.tile([P, P], F32, name="ident")
         make_identity(nc, ident[:])
 
-        p_scales = P_scale.rearrange("(h m e) c -> m h (e c)", h=4, e=2)
-        p_scale = {}
-        for first_pair, count in [(0, 1), (1, 1), (2, 2)]:
-            tile_s = keep.tile([P, count, 16], F32, name="p_scale%d" % first_pair)
-            for j in range(count):
-                p_scale[first_pair + j] = tile_s[:, j, :]
-            p_scale[("tile", first_pair)] = (tile_s, count)
-        nc.scalar.dma_start(out=p_scale[("tile", 0)][0][:], in_=p_scales[:, 0:1, :])
-        nc.scalar.dma_start(out=f_row[0:1, :], in_=F_scale.rearrange("(o b) c -> o (b c)", o=1))
-        nc.scalar.dma_start(out=g_rows[0:8, :], in_=g.rearrange("(b p) -> b p", p=P))
-
         rows = {
             "P": P_bytes.rearrange("(h p e) j -> p h e j", h=4, e=2),
             "F": F_bytes.rearrange("(h e p) j -> p h e j", h=4, e=2),
         }
+        p_scale_rows = P_scale.rearrange("(h p e) c -> p h (e c)", h=4, e=2)
+        p_scale = {}
+
+        def load_p_scales(queue, first_pair, count):
+            part = keep.tile([P, count, 16], F32, name="p_scale%d" % first_pair)
+            queue.dma_start(out=part[:], in_=p_scale_rows[:, first_pair : first_pair + count, :])
+            for j in range(count):
+                p_scale[first_pair + j] = part[:, j, :]
+
+        load_p_scales(nc.scalar, 0, 1)
+        nc.scalar.dma_start(out=f_row[0:1, :], in_=F_scale.rearrange("(o b) c -> o (b c)", o=1))
+        nc.scalar.dma_start(out=g_rows[0:8, :], in_=g.rearrange("(b p) -> b p", p=P))
+
         raw = {}
-        scale = {}
-        spread = keep.tile([P, 72], F32, name="spread")
-        f_scale = spread[:, 0:64]
-        g_col = spread[:, 64:72]
-        for kind, pair, halves in LOADS:
-            cols = slice(512 * halves[0], 512 * halves[-1] + 512)
-            part = keep.tile([P, 2, 512 * len(halves)], U8, name="bytes_%s%d%d" % (kind, pair, halves[0]))
-            if kind == "P" and pair in (1, 2) and halves[0] == 0:
-                tile_s, count = p_scale[("tile", pair)]
-                nc.sync.dma_start(out=tile_s[:], in_=p_scales[:, pair : pair + count, :])
-            nc.sync.dma_start(out=part[:], in_=rows[kind][:, pair, :, cols])
-            for e in range(2):
-                for i, k in enumerate(halves):
-                    raw[(kind, pair, k, e)] = part[:, e, 512 * i : 512 * i + 512]
-        for pair in range(4):
-            for e in range(2):
-                scale[("P", pair, e)] = p_scale[pair][:, 8 * e : 8 * e + 8]
-                scale[("F", pair, e)] = f_scale[:, 16 * pair + 8 * e : 16 * pair + 8 * e + 8]
+        for kind, pair in LOADS:
+            if (kind, pair) == ("P", 1):
+                load_p_scales(nc.sync, 1, 1)
+            if (kind, pair) == ("P", 2):
+                load_p_scales(nc.sync, 2, 2)
+            part = keep.tile([P, 2, N], U8, name="bytes_%s%d" % (kind, pair))
+            nc.sync.dma_start(out=part[:], in_=rows[kind][:, pair, :, :])
+            raw[(kind, pair)] = part
+
         q_rows = Q.rearrange("(b p) n -> p b n", p=P)
         q_tiles = []
-        for h in range(4):
-            qt = keep.tile([P, 2, N], BF16, name="q%d" % h)
-            nc.sync.dma_start(out=qt[:], in_=q_rows[:, 2 * h : 2 * h + 2, :])
-            q_tiles.append(qt)
+        for pair in range(4):
+            part = keep.tile([P, 2, N], BF16, name="q%d" % pair)
+            nc.sync.dma_start(out=part[:], in_=q_rows[:, 2 * pair : 2 * pair + 2, :])
+            q_tiles.append(part)
 
-        pick = keep.tile([P, 8], BF16, name="pick")
-        nc.scalar.activation(out=pick[:], in_=ident[:, 0:8], func=COPY)
+        unit_cols = keep.tile([P, 8], BF16, name="unit_cols")
+        nc.scalar.activation(out=unit_cols[:], in_=ident[:, 0:8], func=COPY)
 
-        wide = {}
-        plain = set()
-        banks = {}
+        spread = keep.tile([P, 72], F32, name="spread")
+        g_col = spread[:, 64:72]
+
         grouped = {}
         codes = {}
+        for half in range(2):
+            for k in range(2):
+                for kind in ["P", "F", "h"]:
+                    name = "%s%d%d" % (kind, half, k)
+                    words = keep.tile([P, PASS], U32, name="codes_" + name, align_bytes=256)
+                    scales = keep.tile([P, PASS], U8, name="scales_" + name, align_bytes=256)
+                    codes[(kind, half, k)] = (words, scales)
+        for kind in ["P", "F", "h"]:
+            for half in range(2):
+                for k in range(2):
+                    values = keep.tile([P, 4 * PASS], BF16, name="grouped_%s%d%d" % (kind, half, k), align_bytes=64)
+                    grouped[(kind, half, k)] = values
 
         free = list(range(8))
         taken = {}
+        banks = {}
 
         def take_bank(key, shape):
             i = free[0]
@@ -94,313 +103,234 @@ def tile_kalman_predicted_covariance_d2_kernel(tc, P_bytes, P_scale, F_bytes, F_
             taken[key] = i
             bank = psum.tile(shape, F32, name="bank%d" % i, tag="bank%d" % i)
             banks[key] = bank
-            return bank
 
         def give_bank(key):
             free.append(taken[key])
 
-        def mx_tiles(key, width):
-            c = keep.tile([P, width], U32, name="codes_%s" % key, align_bytes=256)
-            s = keep.tile([P, width], U8, name="scales_%s" % key, align_bytes=256)
-            codes[key] = (c, s)
-
-        for a in range(2):
-            for k in range(2):
-                mx_tiles("P%d%d" % (a, k), 512)
-                mx_tiles("F%d%d" % (a, k), 512)
-                mx_tiles("h%d%d" % (a, k), 512)
-
-        for kind, count, width in [("P", 2, 2 * N), ("F", 4, N), ("h", 2, 2 * N)]:
-            for a in range(count):
-                for k in range(2):
-                    gr = keep.tile([P, width], BF16, name="grouped_%s%d%d" % (kind, a, k), align_bytes=64)
-                    grouped[(kind, a, k)] = gr
-
-        def gain_column():
-            bank = take_bank("spread", [P, 512])
-            nc.tensor.matmul(bank[:, 0:64], lhsT=ident[:, 0:1].to_broadcast([P, P]), rhs=f_row[:], start=True, stop=True)
-            nc.tensor.matmul(bank[:, 64:72], lhsT=g_rows[:], rhs=pick[:], start=True, stop=True)
+        def spread_matmuls():
+            take_bank("spread", [P, PASS])
+            row_0 = ident[:, 0:1].to_broadcast([P, P])
+            nc.tensor.matmul(banks["spread"][:, 0:64], lhsT=row_0, rhs=f_row[:], start=True, stop=True)
+            nc.tensor.matmul(banks["spread"][:, 64:72], lhsT=g_rows[:], rhs=unit_cols[:], start=True, stop=True)
 
         def copy_spread():
             nc.vector.tensor_copy(out=spread[:], in_=banks["spread"][:, 0:72])
             give_bank("spread")
 
-        def widen(kind, pair, k, e, on_scalar=False):
-            w = keep.tile([P, 512], BF16, name="wide_%s%d%d%d" % (kind, pair, k, e), align_bytes=64)
-            wide[(kind, pair, k, e)] = w
-            blocks = w[:].rearrange("p (u c q x) -> p c q u x", u=2, c=4, x=RUN[k])
-            if on_scalar:
-                plain.add((kind, pair, k, e))
-            for c in range(4):
-                src = raw[(kind, pair, k, e)][:, P * c : P * c + P].bitcast(FP8)
-                col = scale[(kind, pair, e)][:, 4 * k + c : 4 * k + c + 1]
-                if on_scalar:
-                    nc.scalar.activation(out=w[:, P * c : P * c + P], in_=src, func=COPY, scale=col)
-                else:
-                    nc.vector.tensor_scalar(out=blocks[:, c], in0=src, scalar1=col, scalar2=None, op0=MULT)
+        wide = {}
 
-        def turn(kind, pair, k, halves=(0, 1)):
-            if halves[0] == 0:
-                take_bank((kind, pair, k), [P, 2, 2, P])
-            bank = banks[(kind, pair, k)]
-            for e in halves:
-                words = wide[(kind, pair, k, e)][:].bitcast(F32)
+        def widen(unit, tiles=(0, 1)):
+            kind, pair, k = unit
+            for e in tiles:
+                tile = keep.tile([P, PASS], BF16, name="wide_%s%d%d%d" % (kind, pair, k, e), align_bytes=64)
+                wide[(unit, e)] = tile
+                by_u = tile[:].rearrange("p (u c q x) -> p c q u x", u=2, c=4, x=2)
+                for c in range(4):
+                    block = 4 * k + c
+                    src = raw[(kind, pair)][:, e, P * block : P * block + P].bitcast(FP8)
+                    if kind == "P":
+                        col = p_scale[pair][:, 8 * e + block : 8 * e + block + 1]
+                    else:
+                        col = spread[:, 16 * pair + 8 * e + block : 16 * pair + 8 * e + block + 1]
+                    if e == 1 and unit in SHARED:
+                        nc.scalar.activation(out=tile[:, P * c : P * c + P], in_=src, func=COPY, scale=col)
+                    else:
+                        nc.vector.tensor_scalar(out=by_u[:, c], in0=src, scalar1=col, scalar2=None, op0=MULT)
+
+        def turn(unit):
+            take_bank(unit, [P, 2, 2, P])
+            for e in range(2):
+                words = wide[(unit, e)][:].bitcast(F32)
                 for u in range(2):
-                    half = words[:, u : 2 * P : 2] if (kind, pair, k, e) in plain else words[:, P * u : P * u + P]
-                    nc.tensor.transpose(bank[:, e, u, :], half, ident[:])
+                    if e == 1 and unit in SHARED:
+                        src = words[:, u : 2 * P : 2]
+                    else:
+                        src = words[:, P * u : P * u + P]
+                    nc.tensor.transpose(banks[unit][:, e, u, :], src, ident[:])
 
-        def empty(kind, pair, k, on_vector=False):
-            if kind == "F":
-                words = grouped[("F", pair, k)][:].bitcast(F32)
-            else:
-                words = grouped[(kind, pair // 2, k)][:, N * (pair % 2) : N * (pair % 2) + N].bitcast(F32)
-            bank = banks[(kind, pair, k)]
-            if kind == "P":
-                both = grouped[(kind, pair // 2, k)][:].bitcast(F32)
-                dst = both.rearrange("p (e a r u) -> p a e r u", e=2, a=2, u=2)[:, pair % 2]
-            else:
-                dst = words.rearrange("p (e r u) -> p e r u", e=2, u=2)
-            src = bank[:].rearrange("p e u r -> p e r u")
+        def empty(unit, on_vector=False):
+            kind, pair, k = unit
+            words = grouped[(kind, pair // 2, k)][:].bitcast(F32)
+            order = "p (e a r u) -> p a e r u" if kind == "P" else "p (a e r u) -> p a e r u"
+            dst = words.rearrange(order, e=2, a=2, u=2)[:, pair % 2]
+            src = banks[unit][:].rearrange("p e u r -> p e r u")
             if on_vector:
                 nc.vector.tensor_copy(out=dst, in_=src)
             else:
                 nc.scalar.copy(out=dst, in_=src)
-            give_bank((kind, pair, k))
+            give_bank(unit)
 
-        def quant(kind, a, k):
-            if kind == "F":
-                c, s = codes["F%d%d" % (a // 2, k)]
-                cols = slice(256 * (a % 2), 256 * (a % 2) + 256)
-            else:
-                c, s = codes["%s%d%d" % (kind, a, k)]
-                cols = slice(0, 512)
-            nc.vector.quantize_mx(out=c[:, cols].bitcast(FP8X4), scales=s[:, cols], in_=grouped[(kind, a, k)][:])
+        def quantise(kind, half, k, cols=slice(0, PASS)):
+            words, scales = codes[(kind, half, k)]
+            values = grouped[(kind, half, k)][:, 4 * cols.start : 4 * cols.stop]
+            nc.vector.quantize_mx(out=words[:, cols].bitcast(FP8X4), scales=scales[:, cols], in_=values)
 
-        def product(key, b, k, moving, cols=slice(0, 512)):
-            width = cols.stop - cols.start
+        def quantise_f(pair, k):
+            quantise("F", pair // 2, k, slice(256 * (pair % 2), 256 * (pair % 2) + 256))
+
+        def one_pass(key, b, k, moving, cols):
             if k == 0:
-                take_bank(key, [P, width])
-            fc, fs = codes["F%d%d" % (b // 4, k)]
-            rows_m = slice(P * (b % 4), P * (b % 4) + P)
-            c, s = codes[moving]
+                take_bank(key, [P, cols.stop - cols.start])
+            f_words, f_scales = codes[("F", b // 4, k)]
+            tile_b = slice(P * (b % 4), P * (b % 4) + P)
+            words, scales = codes[moving]
             nc.tensor.matmul_mx(
                 out=banks[key][:],
-                lhsT=fc[:, rows_m].bitcast(FP8X4),
-                lhsT_scale=fs[:, rows_m],
-                rhs=c[:, cols].bitcast(FP8X4),
-                rhs_scale=s[:, cols],
+                lhsT=f_words[:, tile_b].bitcast(FP8X4),
+                lhsT_scale=f_scales[:, tile_b],
+                rhs=words[:, cols].bitcast(FP8X4),
+                rhs_scale=scales[:, cols],
                 start=(k == 0),
                 stop=(k == 1),
             )
 
-        def first(b, gi, passes=(0, 1)):
-            for k in passes:
-                product(("H", b, gi), b, k, "P%d%d" % (gi, k))
+        def first(b, half, k):
+            one_pass(("h", b, half, "sum"), b, k, ("P", half, k), slice(0, PASS))
 
-        def second(m, nh, passes=(0, 1), cols=slice(0, 512)):
-            for k in passes:
-                product(("Y", m, nh, cols.start), m, k, "h%d%d" % (nh, k), cols)
-
-        def gain(b, gi, on_vector=False):
-            hw = keep.tile([P, 512], BF16, name="h_wide%d%d" % (b, gi), align_bytes=64)
-            wide[("h", b // 2, gi, b % 2)] = hw
-            dst = hw[:].rearrange("p (u q x) -> p u q x", u=2, x=RUN[gi])
-            src = banks[("H", b, gi)][:].rearrange("p (x q u) -> p u q x", u=2, x=2)
+        def gain(b, half, on_vector=False):
+            key = ("h", b, half, "sum")
+            tile = keep.tile([P, PASS], BF16, name="h_wide%d%d" % (b, half), align_bytes=64)
+            wide[(("h", b // 2, half), b % 2)] = tile
+            dst = tile[:].rearrange("p (u q x) -> p u q x", u=2, x=2)
+            src = banks[key][:].rearrange("p (x q u) -> p u q x", u=2, x=2)
             if on_vector:
                 nc.vector.tensor_scalar(out=dst, in0=src, scalar1=g_col[:, b : b + 1], scalar2=None, op0=MULT)
             else:
                 nc.scalar.activation(out=dst, in_=src, func=COPY, scale=g_col[:, b : b + 1])
-            give_bank(("H", b, gi))
+            give_bank(key)
 
-        def finish(m, nh, cols=slice(0, 512), queue=nc.sync):
-            key = ("Y", m, nh, cols.start)
-            res = keep.tile([P, cols.stop - cols.start], F32, name="res_%d%d%d" % (m, nh, cols.start))
-            out_cols = slice(512 * nh + cols.start, 512 * nh + cols.stop)
+        def second(b, half, cols=slice(0, PASS)):
+            for k in range(2):
+                one_pass(("out", b, half, cols.start), b, k, ("h", half, k), cols)
+
+        def finish(b, half, cols=slice(0, PASS)):
+            key = ("out", b, half, cols.start)
+            result = keep.tile([P, cols.stop - cols.start], F32, name="res_%d%d%d" % (b, half, cols.start))
+            out_cols = slice(PASS * half + cols.start, PASS * half + cols.stop)
             nc.vector.scalar_tensor_tensor(
-                out=res[:],
+                out=result[:],
                 in0=banks[key][:],
-                scalar=g_col[:, m : m + 1],
-                in1=q_tiles[m // 2][:, m % 2, out_cols],
+                scalar=g_col[:, b : b + 1],
+                in1=q_tiles[b // 2][:, b % 2, out_cols],
                 op0=MULT,
                 op1=ADD,
             )
             give_bank(key)
-            queue.dma_start(out=out[P * m : P * m + P, out_cols], in_=res[:])
+            nc.sync.dma_start(out=out[P * b : P * b + P, out_cols], in_=result[:])
 
-        widen("P", 0, 0, 0)
-        widen("P", 0, 0, 1, True)
-        widen("P", 0, 1, 0)
-        widen("P", 0, 1, 1)
-        turn("P", 0, 0)
-        gain_column()
-        turn("P", 0, 1)
-        widen("P", 1, 0, 0, True)
-        widen("P", 1, 0, 1)
-        widen("P", 1, 1, 0)
-        copy_spread()
-        widen("P", 1, 1, 1)
-        turn("P", 1, 0)
-        turn("P", 1, 1)
-        widen("F", 0, 0, 1, True)
-        widen("F", 0, 0, 0)
-        widen("F", 0, 1, 0)
-        widen("F", 0, 1, 1)
-        empty("P", 0, 0)
-        turn("F", 0, 0)
-        turn("F", 0, 1)
-        empty("P", 1, 0)
-        widen("F", 1, 0, 0)
-        widen("F", 1, 0, 1)
-        widen("F", 1, 1, 0)
-        widen("F", 1, 1, 1)
-        empty("F", 0, 0)
-        turn("F", 1, 0)
-        quant("P", 0, 0)
-        empty("P", 0, 1)
-        widen("P", 2, 0, 1, True)
-        quant("F", 0, 0)
-        widen("P", 2, 0, 0)
-        turn("F", 1, 1)
-        empty("P", 1, 1)
-        widen("P", 3, 0, 0)
-        widen("P", 3, 0, 1)
-        empty("F", 1, 0)
-        first(0, 0, (0,))
-        first(1, 0, (0,))
-        turn("P", 2, 0)
-        turn("P", 3, 0)
-        empty("F", 0, 1)
-        widen("P", 2, 1, 0)
-        widen("P", 2, 1, 1)
-        quant("F", 1, 0)
-        empty("F", 1, 1)
-        widen("P", 3, 1, 0)
-        widen("P", 3, 1, 1)
-        turn("P", 2, 1)
-        quant("P", 0, 1)
-        empty("P", 2, 0)
-        first(2, 0, (0,))
-        first(3, 0, (0,))
-        turn("P", 3, 1)
-        quant("F", 0, 1)
-        empty("P", 3, 0)
-        quant("F", 1, 1)
-        first(0, 0, (1,))
-        first(1, 0, (1,))
-        empty("P", 2, 1)
-        quant("P", 1, 0)
-        first(2, 0, (1,))
-        first(3, 0, (1,))
-        empty("P", 3, 1)
-        widen("F", 2, 0, 0)
-        gain(0, 0)
-        first(0, 1, (0,))
-        first(1, 1, (0,))
-        quant("P", 1, 1)
-        first(2, 1, (0,))
-        gain(1, 0)
-        first(3, 1, (0,))
-        widen("F", 2, 0, 1)
-        gain(2, 0)
-        first(0, 1, (1,))
-        first(1, 1, (1,))
-        first(2, 1, (1,))
-        first(3, 1, (1,))
-        widen("F", 2, 1, 0)
-        widen("F", 2, 1, 1)
-        gain(3, 0)
-        widen("F", 3, 0, 0)
-        widen("F", 3, 0, 1)
-        turn("F", 2, 0)
-        turn("F", 2, 1)
-        turn("h", 0, 0)
-        turn("h", 1, 0)
-        gain(0, 1)
-        gain(1, 1, True)
-        turn("F", 3, 0)
-        widen("F", 3, 1, 0)
-        widen("F", 3, 1, 1)
-        empty("F", 2, 0)
-        gain(2, 1, True)
-        turn("h", 0, 1)
-        gain(3, 1)
-        quant("F", 2, 0)
-        turn("F", 3, 1)
-        empty("F", 2, 1)
-        turn("h", 1, 1)
-        first(4, 0, (0,))
-        first(5, 0, (0,))
-        empty("h", 0, 0)
-        quant("F", 2, 1)
-        empty("F", 3, 0, True)
-        first(4, 1, (0,))
-        first(4, 0, (1,))
-        empty("h", 1, 0)
-        first(5, 0, (1,))
-        first(4, 1, (1,))
-        quant("F", 3, 0)
-        empty("F", 3, 1)
-        first(5, 1, (0,))
-        empty("h", 0, 1)
-        empty("h", 1, 1)
-        quant("F", 3, 1)
-        first(5, 1, (1,))
-        first(6, 0, (0,))
-        quant("h", 0, 0)
-        gain(4, 0)
-        first(6, 0, (1,))
-        first(7, 0)
-        quant("h", 0, 1)
-        gain(5, 0)
-        first(6, 1)
-        gain(4, 1, True)
-        gain(5, 1)
-        second(0, 0)
-        first(7, 1)
-        gain(6, 0)
-        second(1, 0)
-        finish(0, 0)
-        gain(7, 0)
-        second(2, 0)
-        finish(1, 0)
-        gain(6, 1)
-        second(3, 0)
-        finish(2, 0)
-        gain(7, 1)
-        second(4, 0)
-        finish(3, 0)
-        turn("h", 2, 0)
-        turn("h", 3, 0)
-        turn("h", 2, 1)
-        turn("h", 3, 1)
-        finish(4, 0)
-        empty("h", 2, 0)
-        empty("h", 3, 0, True)
-        second(5, 0)
-        empty("h", 2, 1)
-        second(6, 0)
-        empty("h", 3, 1)
-        quant("h", 1, 0)
-        finish(5, 0)
+        head = [(kind, pair, k) for kind in ["P", "F"] for pair in range(2) for k in range(2)]
+        for n, unit in enumerate(head):
+            widen(unit, (0,))
+            if unit == ("P", 1, 1):
+                copy_spread()
+            widen(unit, (1,))
+            turn(unit)
+            if n == 0:
+                spread_matmuls()
+            if n >= EMPTY_LAG:
+                empty(head[n - EMPTY_LAG])
+        empty(head[len(head) - EMPTY_LAG])
+
+        quantise("P", 0, 0)
+        quantise_f(0, 0)
+        for pair in (2, 3):
+            widen(("P", pair, 0))
+        for unit in head[len(head) - EMPTY_LAG + 1 :]:
+            empty(unit)
+        for b in (0, 1):
+            first(b, 0, 0)
+        for pair in (2, 3):
+            turn(("P", pair, 0))
+        widen(("P", 2, 1))
+        turn(("P", 2, 1))
+        quantise_f(1, 0)
+        widen(("P", 3, 1))
+        for b in (2, 3):
+            first(b, 0, 0)
+        turn(("P", 3, 1))
+
+        for pair in (2, 3):
+            empty(("P", pair, 0))
+        quantise("P", 0, 1)
+        for pair in (0, 1):
+            quantise_f(pair, 1)
+        for b in range(4):
+            first(b, 0, 1)
+        for pair in (2, 3):
+            empty(("P", pair, 1))
+        quantise("P", 1, 0)
+        widen(("F", 2, 0))
+        for b in range(4):
+            first(b, 1, 0)
+        quantise("P", 1, 1)
+        for b in range(4):
+            gain(b, 0)
+        for b in range(4):
+            first(b, 1, 1)
+
+        for unit in [("F", 2, 1), ("F", 3, 0), ("F", 3, 1)]:
+            widen(unit)
+        for unit in [("F", 2, 0), ("F", 2, 1), ("h", 0, 0), ("h", 1, 0)]:
+            turn(unit)
+        for pair, kind in [(0, "F"), (1, "h")]:
+            gain(2 * pair, 1)
+            gain(2 * pair + 1, 1, on_vector=True)
+            for j in range(2):
+                turn(("F", 3, j) if kind == "F" else ("h", j, 1))
+
+        third = [(b, half) for half in range(2) for b in (4, 5)]
+        empty(("F", 2, 0))
+        quantise_f(2, 0)
+        empty(("F", 2, 1))
+        empty(("F", 3, 0), on_vector=True)
+        empty(("h", 0, 0))
+        for b, half in third:
+            first(b, half, 0)
+        quantise_f(2, 1)
+        empty(("h", 1, 0))
+        for b, half in third:
+            first(b, half, 1)
+        quantise_f(3, 0)
+        empty(("F", 3, 1))
+        empty(("h", 0, 1))
+        quantise_f(3, 1)
+        quantise("h", 0, 0)
+        empty(("h", 1, 1))
+        quantise("h", 0, 1)
+
+        fourth = [(b, half) for half in range(2) for b in (6, 7)]
+        for n in range(4):
+            gain(third[n][0], third[n][1], on_vector=(n % 2 == 1))
+            for k in range(2):
+                first(fourth[n][0], fourth[n][1], k)
+        for b in range(EARLY_TILES):
+            second(b, 0)
+            if b > 0:
+                finish(b - 1, 0)
+            if b < 4:
+                gain(fourth[b][0], fourth[b][1])
+
+        for k in range(2):
+            for pair in (2, 3):
+                turn(("h", pair, k))
+        finish(EARLY_TILES - 1, 0)
+        empty(("h", 2, 0))
+        empty(("h", 3, 0), on_vector=True)
+        for pair in (2, 3):
+            second(EARLY_TILES + pair - 2, 0)
+            empty(("h", pair, 1))
+        quantise("h", 1, 0)
+        finish(EARLY_TILES, 0)
         second(7, 0)
-        quant("h", 1, 1)
-        finish(6, 0)
-        finish(7, 0)
-        second(0, 1)
-        finish(0, 1)
-        second(1, 1)
-        finish(1, 1)
-        second(2, 1)
-        finish(2, 1)
-        second(3, 1)
-        finish(3, 1)
-        second(4, 1)
-        finish(4, 1)
-        second(5, 1)
-        finish(5, 1)
-        second(6, 1)
-        finish(6, 1)
-        second(7, 1, cols=slice(0, 256))
-        second(7, 1, cols=slice(256, 512))
-        finish(7, 1, slice(0, 256))
-        finish(7, 1, slice(256, 512))
+        quantise("h", 1, 1)
+        for b in (6, 7):
+            finish(b, 0)
+
+        for b in range(7):
+            second(b, 1)
+            finish(b, 1)
+        halves = [slice(0, 256), slice(256, PASS)]
+        for cols in halves:
+            second(7, 1, cols)
+        for cols in halves:
+            finish(7, 1, cols)

@@ -219,6 +219,11 @@ def tile_kalman_predicted_covariance_d2_kernel(tc, P_bytes, P_scale, F_bytes, F_
             nc.sync.dma_start(out=out[P * b : P * b + P, out_cols], in_=result[:])
 
         head = [(kind, pair, k) for kind in ["P", "F"] for pair in range(2) for k in range(2)]
+        f_banks = [("F", pair, k) for k in range(2) for pair in range(2)]
+        to_empty = []
+        for k in range(2):
+            to_empty.extend([("P", 0, k), ("P", 1, k), f_banks[k]])
+        to_empty.extend(f_banks[2:])
         for n, unit in enumerate(head):
             widen(unit, (0,))
             if unit == ("P", 1, 1):
@@ -228,14 +233,13 @@ def tile_kalman_predicted_covariance_d2_kernel(tc, P_bytes, P_scale, F_bytes, F_
             if n == 0:
                 spread_matmuls()
             if n >= EMPTY_LAG:
-                empty(head[n - EMPTY_LAG])
-        empty(head[len(head) - EMPTY_LAG])
+                empty(to_empty[n - EMPTY_LAG])
 
         quantise("P", 0, 0)
         quantise_f(0, 0)
         for pair in (2, 3):
             widen(("P", pair, 0))
-        for unit in head[len(head) - EMPTY_LAG + 1 :]:
+        for unit in to_empty[len(head) - EMPTY_LAG :]:
             empty(unit)
         for b in (0, 1):
             first(b, 0, 0)
@@ -259,10 +263,11 @@ def tile_kalman_predicted_covariance_d2_kernel(tc, P_bytes, P_scale, F_bytes, F_
         for pair in (2, 3):
             empty(("P", pair, 1))
         quantise("P", 1, 0)
-        widen(("F", 2, 0))
+        widen(("F", 2, 0), (0,))
         for b in range(4):
             first(b, 1, 0)
         quantise("P", 1, 1)
+        widen(("F", 2, 0), (1,))
         for b in range(4):
             gain(b, 0)
         for b in range(4):

@@ -6,6 +6,7 @@ from concourse.masks import make_identity
 N = 1024
 P = 128
 PASS = 512
+PAIR = 256
 FLOPS = 2 * 2 * N * N * N
 
 F32 = mybir.dt.float32
@@ -19,10 +20,8 @@ ADD = mybir.AluOpType.add
 COPY = mybir.ActivationFunctionType.Copy
 
 LOADS = [("P", 0), ("P", 1), ("F", 0), ("F", 1), ("P", 2), ("P", 3), ("F", 2), ("F", 3)]
-SHARED = [("P", 0, 0), ("P", 1, 0), ("F", 0, 0), ("P", 2, 0)]
+SHARED = [("P", 0, 0), ("P", 1, 0), ("P", 1, 1), ("F", 0, 0), ("P", 2, 0)]
 EMPTY_LAG = 4
-EARLY_TILES = 5
-
 
 def tile_kalman_predicted_covariance_d2_kernel(tc, P_bytes, P_scale, F_bytes, F_scale, g, Q, out):
     nc = tc.nc
@@ -31,38 +30,39 @@ def tile_kalman_predicted_covariance_d2_kernel(tc, P_bytes, P_scale, F_bytes, F_
         psum = ctx.enter_context(tc.psum_pool(name="psum", bufs=1))
         ctx.enter_context(tc.manual_schedule())
 
-        g_rows = keep.tile([P, P], BF16, name="g_rows")
-        nc.vector.memset(g_rows[:], 0.0)
         f_row = keep.tile([P, 64], F32, name="f_row")
         nc.vector.memset(f_row[:], 0.0)
+        g_rows = keep.tile([P, P], BF16, name="g_rows")
+        nc.vector.memset(g_rows[:], 0.0)
         ident = keep.tile([P, P], F32, name="ident")
         make_identity(nc, ident[:])
 
-        rows = {
-            "P": P_bytes.rearrange("(h p e) j -> p h e j", h=4, e=2),
-            "F": F_bytes.rearrange("(h e p) j -> p h e j", h=4, e=2),
-        }
-        p_scale_rows = P_scale.rearrange("(h p e) c -> p h (e c)", h=4, e=2)
+        p_rows = P_bytes.rearrange("(c p u e) j -> p c u e j", c=2, u=2, e=2)
+        f_rows = F_bytes.rearrange("(h e p) j -> p h e j", h=4, e=2)
+        p_scale_rows = P_scale.rearrange("(c p t) b -> p c (t b)", c=2, t=4)
         p_scale = {}
 
-        def load_p_scales(queue, first_pair, count):
-            part = keep.tile([P, count, 16], F32, name="p_scale%d" % first_pair)
-            queue.dma_start(out=part[:], in_=p_scale_rows[:, first_pair : first_pair + count, :])
-            for j in range(count):
-                p_scale[first_pair + j] = part[:, j, :]
+        def load_p_scales(queue, c):
+            part = keep.tile([P, 32], F32, name="p_scale%d" % c)
+            queue.dma_start(out=part[:], in_=p_scale_rows[:, c, :])
+            for u in range(2):
+                p_scale[2 * c + u] = part[:, 16 * u : 16 * u + 16]
 
-        load_p_scales(nc.scalar, 0, 1)
+        load_p_scales(nc.scalar, 0)
         nc.scalar.dma_start(out=f_row[0:1, :], in_=F_scale.rearrange("(o b) c -> o (b c)", o=1))
         nc.scalar.dma_start(out=g_rows[0:8, :], in_=g.rearrange("(b p) -> b p", p=P))
 
         raw = {}
         for kind, pair in LOADS:
-            if (kind, pair) == ("P", 1):
-                load_p_scales(nc.sync, 1, 1)
             if (kind, pair) == ("P", 2):
-                load_p_scales(nc.sync, 2, 2)
+                load_p_scales(nc.sync, 1)
             part = keep.tile([P, 2, N], U8, name="bytes_%s%d" % (kind, pair))
-            nc.sync.dma_start(out=part[:], in_=rows[kind][:, pair, :, :])
+            rows = p_rows[:, pair // 2, pair % 2] if kind == "P" else f_rows[:, pair]
+            if not raw:
+                for e in range(2):
+                    nc.sync.dma_start(out=part[:, e, :], in_=rows[:, e, :])
+            else:
+                nc.sync.dma_start(out=part[:], in_=rows)
             raw[(kind, pair)] = part
 
         q_rows = Q.rearrange("(b p) n -> p b n", p=P)
@@ -80,18 +80,18 @@ def tile_kalman_predicted_covariance_d2_kernel(tc, P_bytes, P_scale, F_bytes, F_
 
         grouped = {}
         codes = {}
-        for half in range(2):
-            for k in range(2):
-                for kind in ["P", "F", "h"]:
-                    name = "%s%d%d" % (kind, half, k)
-                    words = keep.tile([P, PASS], U32, name="codes_" + name, align_bytes=256)
-                    scales = keep.tile([P, PASS], U8, name="scales_" + name, align_bytes=256)
-                    codes[(kind, half, k)] = (words, scales)
         for kind in ["P", "F", "h"]:
-            for half in range(2):
-                for k in range(2):
-                    values = keep.tile([P, 4 * PASS], BF16, name="grouped_%s%d%d" % (kind, half, k), align_bytes=64)
-                    grouped[(kind, half, k)] = values
+            for n in range(4):
+                name = "%s%d" % (kind, n)
+                words = keep.tile([P, PASS], U32, name="codes_" + name, align_bytes=256)
+                scales = keep.tile([P, PASS], U8, name="scales_" + name, align_bytes=256)
+                codes[(kind, n)] = (words, scales)
+                grouped[(kind, n)] = keep.tile([P, 4 * PASS], BF16, name="grouped_" + name, align_bytes=64)
+
+        def place(kind, pair, k):
+            if kind == "P":
+                return (kind, 2 * (pair // 2) + k), PAIR * (pair % 2)
+            return (kind, pair), PAIR * k
 
         free = list(range(8))
         taken = {}
@@ -118,41 +118,43 @@ def tile_kalman_predicted_covariance_d2_kernel(tc, P_bytes, P_scale, F_bytes, F_
             give_bank("spread")
 
         wide = {}
+        in_order = set()
 
-        def widen(unit, tiles=(0, 1)):
-            kind, pair, k = unit
+        def widen(kind, pair, k, e, on_scalar=False):
+            tile = keep.tile([P, PASS], BF16, name="wide_%s%d%d%d" % (kind, pair, k, e), align_bytes=64)
+            wide[(kind, pair, k, e)] = tile
+            by_u = tile[:].rearrange("p (u c q x) -> p c q u x", u=2, c=4, x=2)
+            for c in range(4):
+                block = 4 * k + c
+                src = raw[(kind, pair)][:, e, P * block : P * block + P].bitcast(FP8)
+                if kind == "P":
+                    col = p_scale[pair][:, 8 * e + block : 8 * e + block + 1]
+                else:
+                    col = spread[:, 16 * pair + 8 * e + block : 16 * pair + 8 * e + block + 1]
+                if on_scalar:
+                    in_order.add((kind, pair, k, e))
+                    nc.scalar.activation(out=tile[:, P * c : P * c + P], in_=src, func=COPY, scale=col)
+                else:
+                    nc.vector.tensor_scalar(out=by_u[:, c], in0=src, scalar1=col, scalar2=None, op0=MULT)
+
+        def turn(kind, pair, k, tiles=(0, 1)):
+            unit = (kind, pair, k)
+            if 0 in tiles:
+                take_bank(unit, [P, 2, 2, P])
             for e in tiles:
-                tile = keep.tile([P, PASS], BF16, name="wide_%s%d%d%d" % (kind, pair, k, e), align_bytes=64)
-                wide[(unit, e)] = tile
-                by_u = tile[:].rearrange("p (u c q x) -> p c q u x", u=2, c=4, x=2)
-                for c in range(4):
-                    block = 4 * k + c
-                    src = raw[(kind, pair)][:, e, P * block : P * block + P].bitcast(FP8)
-                    if kind == "P":
-                        col = p_scale[pair][:, 8 * e + block : 8 * e + block + 1]
-                    else:
-                        col = spread[:, 16 * pair + 8 * e + block : 16 * pair + 8 * e + block + 1]
-                    if e == 1 and unit in SHARED:
-                        nc.scalar.activation(out=tile[:, P * c : P * c + P], in_=src, func=COPY, scale=col)
-                    else:
-                        nc.vector.tensor_scalar(out=by_u[:, c], in0=src, scalar1=col, scalar2=None, op0=MULT)
-
-        def turn(unit):
-            take_bank(unit, [P, 2, 2, P])
-            for e in range(2):
-                words = wide[(unit, e)][:].bitcast(F32)
+                words = wide[(kind, pair, k, e)][:].bitcast(F32)
                 for u in range(2):
-                    if e == 1 and unit in SHARED:
+                    if (kind, pair, k, e) in in_order:
                         src = words[:, u : 2 * P : 2]
                     else:
                         src = words[:, P * u : P * u + P]
                     nc.tensor.transpose(banks[unit][:, e, u, :], src, ident[:])
 
-        def empty(unit, on_vector=False):
-            kind, pair, k = unit
-            words = grouped[(kind, pair // 2, k)][:].bitcast(F32)
-            order = "p (e a r u) -> p a e r u" if kind == "P" else "p (a e r u) -> p a e r u"
-            dst = words.rearrange(order, e=2, a=2, u=2)[:, pair % 2]
+        def empty(kind, pair, k, on_vector=False):
+            unit = (kind, pair, k)
+            group, col = place(kind, pair, k)
+            words = grouped[group][:].bitcast(F32)[:, 2 * col : 2 * col + 2 * PAIR]
+            dst = words.rearrange("p (e r u) -> p e r u", e=2, u=2)
             src = banks[unit][:].rearrange("p e u r -> p e r u")
             if on_vector:
                 nc.vector.tensor_copy(out=dst, in_=src)
@@ -160,63 +162,88 @@ def tile_kalman_predicted_covariance_d2_kernel(tc, P_bytes, P_scale, F_bytes, F_
                 nc.scalar.copy(out=dst, in_=src)
             give_bank(unit)
 
-        def quantise(kind, half, k, cols=slice(0, PASS)):
-            words, scales = codes[(kind, half, k)]
-            values = grouped[(kind, half, k)][:, 4 * cols.start : 4 * cols.stop]
+        def quantise(group, cols=slice(0, PASS)):
+            words, scales = codes[group]
+            values = grouped[group][:, 4 * cols.start : 4 * cols.stop]
             nc.vector.quantize_mx(out=words[:, cols].bitcast(FP8X4), scales=scales[:, cols], in_=values)
 
-        def quantise_f(pair, k):
-            quantise("F", pair // 2, k, slice(256 * (pair % 2), 256 * (pair % 2) + 256))
+        def quantise_part(kind, pair, k):
+            group, col = place(kind, pair, k)
+            quantise(group, slice(col, col + PAIR))
 
-        def one_pass(key, b, k, moving, cols):
-            if k == 0:
-                take_bank(key, [P, cols.stop - cols.start])
-            f_words, f_scales = codes[("F", b // 4, k)]
-            tile_b = slice(P * (b % 4), P * (b % 4) + P)
-            words, scales = codes[moving]
+        def one_pass(dst, b, k, group, cols, closes=True):
+            f_words, f_scales = codes[("F", b // 2)]
+            tile_b = slice(PAIR * k + P * (b % 2), PAIR * k + P * (b % 2) + P)
+            words, scales = codes[group]
             nc.tensor.matmul_mx(
-                out=banks[key][:],
+                out=dst,
                 lhsT=f_words[:, tile_b].bitcast(FP8X4),
                 lhsT_scale=f_scales[:, tile_b],
                 rhs=words[:, cols].bitcast(FP8X4),
                 rhs_scale=scales[:, cols],
                 start=(k == 0),
-                stop=(k == 1),
+                stop=(k == 1 and closes),
             )
 
-        def first(b, half, k):
-            one_pass(("h", b, half, "sum"), b, k, ("P", half, k), slice(0, PASS))
+        def first(b, c, passes=(0, 1)):
+            key = ("sum", b, c)
+            for k in passes:
+                if k == 0:
+                    take_bank(key, [P, PASS])
+                one_pass(banks[key][:], b, k, ("P", 2 * c + k), slice(0, PASS))
 
-        def gain(b, half, on_vector=False):
-            key = ("h", b, half, "sum")
-            tile = keep.tile([P, PASS], BF16, name="h_wide%d%d" % (b, half), align_bytes=64)
-            wide[(("h", b // 2, half), b % 2)] = tile
+        def first_part(b, c, u):
+            cols = slice(PAIR * u, PAIR * u + PAIR)
+            one_pass(banks[("sum", b, c)][:, cols], b, 1, ("P", 2 * c + 1), cols, closes=(u == 1))
+
+        def gain(b, c, on_vector=False):
+            key = ("sum", b, c)
+            tile = keep.tile([P, PASS], BF16, name="h_wide%d%d" % (b, c), align_bytes=64)
+            wide[("h", b // 2, c, b % 2)] = tile
             dst = tile[:].rearrange("p (u q x) -> p u q x", u=2, x=2)
-            src = banks[key][:].rearrange("p (x q u) -> p u q x", u=2, x=2)
+            src = banks[key][:].rearrange("p (u x q) -> p u q x", u=2, x=2)
             if on_vector:
                 nc.vector.tensor_scalar(out=dst, in0=src, scalar1=g_col[:, b : b + 1], scalar2=None, op0=MULT)
             else:
                 nc.scalar.activation(out=dst, in_=src, func=COPY, scale=g_col[:, b : b + 1])
             give_bank(key)
 
-        def second(b, half, cols=slice(0, PASS)):
-            for k in range(2):
-                one_pass(("out", b, half, cols.start), b, k, ("h", half, k), cols)
+        def second(parts):
+            take_bank(parts, [P, len(parts), PAIR])
+            for j, (b, h_pair) in enumerate(parts):
+                for k in range(2):
+                    one_pass(banks[parts][:, j, :], b, k, ("h", h_pair), slice(PAIR * k, PAIR * k + PAIR))
 
-        def finish(b, half, cols=slice(0, PASS)):
-            key = ("out", b, half, cols.start)
-            result = keep.tile([P, cols.stop - cols.start], F32, name="res_%d%d%d" % (b, half, cols.start))
-            out_cols = slice(PASS * half + cols.start, PASS * half + cols.stop)
-            nc.vector.scalar_tensor_tensor(
-                out=result[:],
-                in0=banks[key][:],
-                scalar=g_col[:, b : b + 1],
-                in1=q_tiles[b // 2][:, b % 2, out_cols],
-                op0=MULT,
-                op1=ADD,
-            )
-            give_bank(key)
-            nc.sync.dma_start(out=out[P * b : P * b + P, out_cols], in_=result[:])
+        def finish(parts, split=False):
+            result = keep.tile([P, len(parts), PAIR], F32, name="res_%d_%d" % parts[0])
+            b, h_pair = parts[0]
+            if len(parts) == 2 and parts[1][0] == b:
+                cols = slice(PAIR * h_pair, PAIR * h_pair + PASS)
+                steps = [(b, cols, result[:].rearrange("p j n -> p (j n)"), banks[parts][:].rearrange("p j n -> p (j n)"))]
+                dst = out[P * b : P * b + P, cols].rearrange("p (j n) -> p j n", j=2)
+            else:
+                cols = slice(PAIR * h_pair, PAIR * h_pair + PAIR)
+                steps = [(b + j, cols, result[:, j, :], banks[parts][:, j, :]) for j in range(len(parts))]
+                dst = out[P * b : P * b + len(parts) * P, cols].rearrange("(j p) n -> p j n", p=P)
+            for j, (row_tile, cols, res, src) in enumerate(steps):
+                nc.vector.scalar_tensor_tensor(
+                    out=res,
+                    in0=src,
+                    scalar=g_col[:, row_tile : row_tile + 1],
+                    in1=q_tiles[row_tile // 2][:, row_tile % 2, cols],
+                    op0=MULT,
+                    op1=ADD,
+                )
+                if split:
+                    nc.sync.dma_start(out=dst[:, j, :], in_=res)
+            give_bank(parts)
+            if not split:
+                nc.sync.dma_start(out=dst, in_=result[:])
+
+
+        def widen_unit(kind, pair, k, tiles=(0, 1)):
+            for e in tiles:
+                widen(kind, pair, k, e, on_scalar=(e == 1 and (kind, pair, k) in SHARED))
 
         head = [(kind, pair, k) for kind in ["P", "F"] for pair in range(2) for k in range(2)]
         f_banks = [("F", pair, k) for k in range(2) for pair in range(2)]
@@ -224,118 +251,129 @@ def tile_kalman_predicted_covariance_d2_kernel(tc, P_bytes, P_scale, F_bytes, F_
         for k in range(2):
             to_empty.extend([("P", 0, k), ("P", 1, k), f_banks[k]])
         to_empty.extend(f_banks[2:])
+        widen_unit("P", 0, 0, (0,))
+        widen_unit("P", 0, 1, (0,))
         for n, unit in enumerate(head):
-            widen(unit, (0,))
-            if unit == ("P", 1, 1):
-                copy_spread()
-            widen(unit, (1,))
-            turn(unit)
+            if unit[:2] != ("P", 0):
+                if unit == ("P", 1, 1):
+                    copy_spread()
+                widen_unit(*unit, (0,))
+            widen_unit(*unit, (1,))
             if n == 0:
+                turn(*unit, (0,))
                 spread_matmuls()
+                turn(*unit, (1,))
+            else:
+                turn(*unit)
             if n >= EMPTY_LAG:
-                empty(to_empty[n - EMPTY_LAG])
-
-        quantise("P", 0, 0)
-        quantise_f(0, 0)
+                empty(*to_empty[n - EMPTY_LAG])
+        quantise(("P", 0))
+        quantise_part("F", 0, 0)
         for pair in (2, 3):
-            widen(("P", pair, 0))
+            widen_unit("P", pair, 0)
         for unit in to_empty[len(head) - EMPTY_LAG :]:
-            empty(unit)
+            empty(*unit)
         for b in (0, 1):
-            first(b, 0, 0)
+            first(b, 0, (0,))
         for pair in (2, 3):
-            turn(("P", pair, 0))
-        widen(("P", 2, 1))
-        turn(("P", 2, 1))
-        quantise_f(1, 0)
-        widen(("P", 3, 1))
+            turn("P", pair, 0)
+        widen_unit("P", 2, 1)
+        turn("P", 2, 1)
+        quantise_part("F", 1, 0)
+        widen_unit("P", 3, 1)
         for b in (2, 3):
-            first(b, 0, 0)
-        turn(("P", 3, 1))
-
+            first(b, 0, (0,))
+        turn("P", 3, 1)
         for pair in (2, 3):
-            empty(("P", pair, 0))
-        quantise("P", 0, 1)
+            empty("P", pair, 0)
+        quantise(("P", 1))
         for pair in (0, 1):
-            quantise_f(pair, 1)
+            quantise_part("F", pair, 1)
         for b in range(4):
-            first(b, 0, 1)
+            first(b, 0, (1,))
         for pair in (2, 3):
-            empty(("P", pair, 1))
-        quantise("P", 1, 0)
-        widen(("F", 2, 0), (0,))
+            empty("P", pair, 1)
+        quantise(("P", 2))
+        widen_unit("F", 2, 0, (0,))
         for b in range(4):
-            first(b, 1, 0)
-        quantise("P", 1, 1)
-        widen(("F", 2, 0), (1,))
+            first(b, 1, (0,))
+        quantise(("P", 3))
+        widen_unit("F", 2, 0, (1,))
         for b in range(4):
             gain(b, 0)
         for b in range(4):
-            first(b, 1, 1)
+            first(b, 1, (1,))
 
         for unit in [("F", 2, 1), ("F", 3, 0), ("F", 3, 1)]:
-            widen(unit)
+            widen_unit(*unit)
         for unit in [("F", 2, 0), ("F", 2, 1), ("h", 0, 0), ("h", 1, 0)]:
-            turn(unit)
+            turn(*unit)
         for pair, kind in [(0, "F"), (1, "h")]:
             gain(2 * pair, 1)
             gain(2 * pair + 1, 1, on_vector=True)
             for j in range(2):
-                turn(("F", 3, j) if kind == "F" else ("h", j, 1))
-
+                if kind == "F":
+                    turn("F", 3, j)
+                else:
+                    turn("h", j, 1)
         third = [(b, half) for half in range(2) for b in (4, 5)]
-        empty(("F", 2, 0))
-        quantise_f(2, 0)
-        empty(("F", 2, 1))
-        empty(("F", 3, 0), on_vector=True)
-        empty(("h", 0, 0))
+        empty("F", 2, 0)
+        quantise_part("F", 2, 0)
+        empty("F", 2, 1)
+        empty("F", 3, 0, on_vector=True)
+        empty("h", 0, 0)
         for b, half in third:
-            first(b, half, 0)
-        quantise_f(2, 1)
-        empty(("h", 1, 0))
+            first(b, half, (0,))
+        quantise_part("F", 2, 1)
+        empty("h", 1, 0)
         for b, half in third:
-            first(b, half, 1)
-        quantise_f(3, 0)
-        empty(("F", 3, 1))
-        empty(("h", 0, 1))
-        quantise_f(3, 1)
-        quantise("h", 0, 0)
-        empty(("h", 1, 1))
-        quantise("h", 0, 1)
+            first(b, half, (1,))
+        empty("F", 3, 1)
+        empty("h", 0, 1)
+        quantise(("F", 3))
+        quantise(("h", 0))
+        empty("h", 1, 1)
+        quantise(("h", 1))
 
         fourth = [(b, half) for half in range(2) for b in (6, 7)]
+        left = [((b, 0), (b, 1)) for b in range(8)]
         for n in range(4):
             gain(third[n][0], third[n][1], on_vector=(n % 2 == 1))
-            for k in range(2):
-                first(fourth[n][0], fourth[n][1], k)
-        for b in range(EARLY_TILES):
-            second(b, 0)
-            if b > 0:
-                finish(b - 1, 0)
-            if b < 4:
-                gain(fourth[b][0], fourth[b][1])
-
-        for k in range(2):
-            for pair in (2, 3):
-                turn(("h", pair, k))
-        finish(EARLY_TILES - 1, 0)
-        empty(("h", 2, 0))
-        empty(("h", 3, 0), on_vector=True)
-        for pair in (2, 3):
-            second(EARLY_TILES + pair - 2, 0)
-            empty(("h", pair, 1))
-        quantise("h", 1, 0)
-        finish(EARLY_TILES, 0)
-        second(7, 0)
-        quantise("h", 1, 1)
-        for b in (6, 7):
-            finish(b, 0)
-
-        for b in range(7):
-            second(b, 1)
-            finish(b, 1)
-        halves = [slice(0, 256), slice(256, PASS)]
-        for cols in halves:
-            second(7, 1, cols)
-        for cols in halves:
-            finish(7, 1, cols)
+        for n in range(2):
+            first(*fourth[n])
+        for b in range(2):
+            second(left[b])
+            gain(*fourth[b])
+        finish(left[0])
+        second(left[2])
+        finish(left[1])
+        for unit in [("h", 2, 0), ("h", 2, 1), ("h", 3, 0)]:
+            turn(*unit)
+        finish(left[2])
+        first(*fourth[2])
+        empty("h", 2, 0)
+        first(*fourth[3])
+        empty("h", 2, 1, on_vector=True)
+        empty("h", 3, 0)
+        second(left[3])
+        quantise(("h", 2))
+        gain(*fourth[2])
+        second(left[4])
+        gain(*fourth[3])
+        quantise_part("h", 3, 0)
+        finish(left[3])
+        second(left[5])
+        finish(left[4])
+        turn("h", 3, 1)
+        finish(left[5])
+        empty("h", 3, 1)
+        thirds = [((2 * j, 2), (2 * j + 1, 2)) for j in range(4)]
+        last = [((2 * j, 3), (2 * j + 1, 3)) for j in range(3)] + [((6, 3),), ((7, 3),)]
+        rest = left[6:] + thirds + last
+        for n, parts in enumerate(rest):
+            second(parts)
+            if n > 0:
+                finish(rest[n - 1])
+            if n == 1:
+                quantise_part("h", 3, 1)
+        finish(rest[-1])

@@ -31,9 +31,9 @@ def tile_kalman_predicted_covariance_d2_kernel(tc, P_bytes, P_scale, F_bytes, F_
         ctx.enter_context(tc.manual_schedule())
 
         f_row = keep.tile([P, 64], F32, name="f_row")
-        nc.vector.memset(f_row[:], 0.0)
+        nc.gpsimd.memset(f_row[:], 0.0)
         g_rows = keep.tile([P, P], BF16, name="g_rows")
-        nc.vector.memset(g_rows[:], 0.0)
+        nc.gpsimd.memset(g_rows[:], 0.0)
         ident = keep.tile([P, P], F32, name="ident")
         make_identity(nc, ident[:])
 
@@ -89,7 +89,7 @@ def tile_kalman_predicted_covariance_d2_kernel(tc, P_bytes, P_scale, F_bytes, F_
                 grouped[(kind, n)] = keep.tile([P, 4 * PASS], BF16, name="grouped_" + name, align_bytes=64)
 
         def place(kind, pair, k):
-            if kind == "P":
+            if kind == "P" or (kind == "h" and pair < 2):
                 return (kind, 2 * (pair // 2) + k), PAIR * (pair % 2)
             return (kind, pair), PAIR * k
 
@@ -210,11 +210,16 @@ def tile_kalman_predicted_covariance_d2_kernel(tc, P_bytes, P_scale, F_bytes, F_
 
         def second(parts):
             take_bank(parts, [P, len(parts), PAIR])
+            if parts[0][1] < 2:
+                cols = slice(PAIR * parts[0][1], PAIR * parts[-1][1] + PAIR)
+                for k in range(2):
+                    one_pass(banks[parts][:].rearrange("p j n -> p (j n)"), parts[0][0], k, ("h", k), cols)
+                return
             for j, (b, h_pair) in enumerate(parts):
                 for k in range(2):
                     one_pass(banks[parts][:, j, :], b, k, ("h", h_pair), slice(PAIR * k, PAIR * k + PAIR))
 
-        def finish(parts, split=False):
+        def finish(parts, queue=nc.sync):
             result = keep.tile([P, len(parts), PAIR], F32, name="res_%d_%d" % parts[0])
             b, h_pair = parts[0]
             if len(parts) == 2 and parts[1][0] == b:
@@ -225,7 +230,7 @@ def tile_kalman_predicted_covariance_d2_kernel(tc, P_bytes, P_scale, F_bytes, F_
                 cols = slice(PAIR * h_pair, PAIR * h_pair + PAIR)
                 steps = [(b + j, cols, result[:, j, :], banks[parts][:, j, :]) for j in range(len(parts))]
                 dst = out[P * b : P * b + len(parts) * P, cols].rearrange("(j p) n -> p j n", p=P)
-            for j, (row_tile, cols, res, src) in enumerate(steps):
+            for row_tile, cols, res, src in steps:
                 nc.vector.scalar_tensor_tensor(
                     out=res,
                     in0=src,
@@ -234,11 +239,8 @@ def tile_kalman_predicted_covariance_d2_kernel(tc, P_bytes, P_scale, F_bytes, F_
                     op0=MULT,
                     op1=ADD,
                 )
-                if split:
-                    nc.sync.dma_start(out=dst[:, j, :], in_=res)
             give_bank(parts)
-            if not split:
-                nc.sync.dma_start(out=dst, in_=result[:])
+            queue.dma_start(out=dst, in_=result[:])
 
 
         def widen_unit(kind, pair, k, tiles=(0, 1)):
@@ -369,11 +371,11 @@ def tile_kalman_predicted_covariance_d2_kernel(tc, P_bytes, P_scale, F_bytes, F_
         empty("h", 3, 1)
         thirds = [((2 * j, 2), (2 * j + 1, 2)) for j in range(4)]
         last = [((2 * j, 3), (2 * j + 1, 3)) for j in range(3)] + [((6, 3),), ((7, 3),)]
-        rest = left[6:] + thirds + last
+        rest = [((6, 0),), ((6, 1),), left[7]] + thirds + last
         for n, parts in enumerate(rest):
             second(parts)
             if n > 0:
-                finish(rest[n - 1])
-            if n == 1:
+                finish(rest[n - 1], nc.scalar if n > 3 and n % 2 == 1 else nc.sync)
+            if n == 2:
                 quantise_part("h", 3, 1)
         finish(rest[-1])

@@ -72,6 +72,9 @@ def tile_kalman_predicted_covariance_d2_kernel(tc, P_bytes, P_scale, F_bytes, F_
             nc.sync.dma_start(out=part[:], in_=q_rows[:, 2 * pair : 2 * pair + 2, :])
             q_tiles.append(part)
 
+        g_all = keep.tile([P, PASS], BF16, name="g_all")
+        nc.sync.dma_start(out=g_all[:], in_=g[PASS:N].partition_broadcast(P))
+
         unit_cols = keep.tile([P, 8], BF16, name="unit_cols")
         nc.scalar.activation(out=unit_cols[:], in_=ident[:, 0:8], func=COPY)
 
@@ -196,6 +199,32 @@ def tile_kalman_predicted_covariance_d2_kernel(tc, P_bytes, P_scale, F_bytes, F_
             cols = slice(PAIR * u, PAIR * u + PAIR)
             one_pass(banks[("sum", b, c)][:, cols], b, 1, ("P", 2 * c + 1), cols, closes=(u == 1))
 
+        def direct(b, c):
+            key = ("direct", b, c)
+            take_bank(key, [P, 4, P])
+            f_words, f_scales = codes[("F", b // 2)]
+            for t in range(4):
+                for k in range(2):
+                    words, scales = codes[("P", 2 * c + k)]
+                    tile_b = slice(PAIR * k + P * (b % 2), PAIR * k + P * (b % 2) + P)
+                    nc.tensor.matmul_mx(
+                        out=banks[key][:, t, :],
+                        lhsT=words[:, P * t : P * t + P].bitcast(FP8X4),
+                        lhsT_scale=scales[:, P * t : P * t + P],
+                        rhs=f_words[:, tile_b].bitcast(FP8X4),
+                        rhs_scale=f_scales[:, tile_b],
+                        start=(k == 0),
+                        stop=(k == 1),
+                    )
+
+        def direct_gain(b, c):
+            key = ("direct", b, c)
+            col = PAIR * c + P * (b % 2)
+            dst = grouped[("h", b // 2)][:, 4 * col : 4 * col + PASS].rearrange("p (r t) -> p r t", t=4)
+            factor = g_all[:, P * b - PASS : P * b - PASS + P].unsqueeze(2).to_broadcast([P, P, 4])
+            nc.vector.tensor_tensor(out=dst, in0=banks[key][:].rearrange("p t r -> p r t"), in1=factor, op=MULT)
+            give_bank(key)
+
         def gain(b, c, on_vector=False):
             key = ("sum", b, c)
             tile = keep.tile([P, PASS], BF16, name="h_wide%d%d" % (b, c), align_bytes=64)
@@ -218,6 +247,34 @@ def tile_kalman_predicted_covariance_d2_kernel(tc, P_bytes, P_scale, F_bytes, F_
             for j, (b, h_pair) in enumerate(parts):
                 for k in range(2):
                     one_pass(banks[parts][:, j, :], b, k, ("h", h_pair), slice(PAIR * k, PAIR * k + PAIR))
+
+        def finish_shared(parts):
+            b, h_pair = parts[0]
+            scaled = keep.tile([P, 2, PAIR], F32, name="scaled_%d_%d" % parts[0])
+            result = keep.tile([P, 2, PAIR], F32, name="res_%d_%d" % parts[0])
+            if parts[1][0] == b:
+                cols = slice(PAIR * h_pair, PAIR * h_pair + PASS)
+                flat = "p j n -> p (j n)"
+                src = banks[parts][:].rearrange(flat)
+                nc.scalar.activation(out=scaled[:].rearrange(flat), in_=src, func=COPY, scale=g_col[:, b : b + 1])
+                noise = q_tiles[b // 2][:, b % 2, cols].rearrange("p (j n) -> p j n", j=2)
+                dst = out[P * b : P * b + P, cols].rearrange("p (j n) -> p j n", j=2)
+            else:
+                cols = slice(PAIR * h_pair, PAIR * h_pair + PAIR)
+                for j in range(2):
+                    factor = g_col[:, b + j : b + j + 1]
+                    nc.scalar.activation(out=scaled[:, j, :], in_=banks[parts][:, j, :], func=COPY, scale=factor)
+                noise = q_tiles[b // 2][:, :, cols]
+                dst = out[P * b : P * b + 2 * P, cols].rearrange("(j p) n -> p j n", p=P)
+            give_bank(parts)
+            nc.gpsimd.tensor_tensor(out=result[:], in0=scaled[:], in1=noise, op=ADD)
+            pending[parts] = (dst, result)
+
+        pending = {}
+
+        def store(parts):
+            dst, result = pending[parts]
+            nc.scalar.dma_start(out=dst, in_=result[:])
 
         def finish(parts, queue=nc.sync):
             result = keep.tile([P, len(parts), PAIR], F32, name="res_%d_%d" % parts[0])
@@ -337,45 +394,51 @@ def tile_kalman_predicted_covariance_d2_kernel(tc, P_bytes, P_scale, F_bytes, F_
         empty("h", 1, 1)
         quantise(("h", 1))
 
-        fourth = [(b, half) for half in range(2) for b in (6, 7)]
         left = [((b, 0), (b, 1)) for b in range(8)]
-        for n in range(4):
-            gain(third[n][0], third[n][1], on_vector=(n % 2 == 1))
-        for n in range(2):
-            first(*fourth[n])
-        for b in range(2):
-            second(left[b])
-            gain(*fourth[b])
-        finish(left[0])
-        second(left[2])
-        finish(left[1])
-        for unit in [("h", 2, 0), ("h", 2, 1), ("h", 3, 0)]:
-            turn(*unit)
-        finish(left[2])
-        first(*fourth[2])
-        empty("h", 2, 0)
-        first(*fourth[3])
-        empty("h", 2, 1, on_vector=True)
-        empty("h", 3, 0)
-        second(left[3])
-        quantise(("h", 2))
-        gain(*fourth[2])
-        second(left[4])
-        gain(*fourth[3])
-        quantise_part("h", 3, 0)
-        finish(left[3])
-        second(left[5])
-        finish(left[4])
-        turn("h", 3, 1)
-        finish(left[5])
-        empty("h", 3, 1)
         thirds = [((2 * j, 2), (2 * j + 1, 2)) for j in range(4)]
         last = [((2 * j, 3), (2 * j + 1, 3)) for j in range(3)] + [((6, 3),), ((7, 3),)]
-        rest = [((6, 0),), ((6, 1),), left[7]] + thirds + last
+        shared = [left[b] for b in (5,)]
+        for b, c in third:
+            gain(b, c)
+        for b in (6, 7):
+            direct(b, 0)
+            direct_gain(b, 0)
+        for b in range(3):
+            second(left[b])
+            finish(left[b])
+            if b == 0:
+                quantise_part("h", 3, 0)
+        for k in range(2):
+            turn("h", 2, k)
+        for k in range(2):
+            empty("h", 2, k)
+        halves = [((3, 0),), ((3, 1),)]
+        for parts in halves:
+            second(parts)
+        for parts in halves:
+            finish(parts)
+        for b in range(4, 7):
+            second(left[b])
+            if b == 4:
+                quantise(("h", 2))
+            if left[b] in shared:
+                finish_shared(left[b])
+            else:
+                finish(left[b])
+        direct(6, 1)
+        second(left[7])
+        direct_gain(6, 1)
+        direct(7, 1)
+        finish(left[7])
+        for parts in shared:
+            store(parts)
+        rest = thirds + last
         for n, parts in enumerate(rest):
             second(parts)
+            if n == 0:
+                direct_gain(7, 1)
             if n > 0:
-                finish(rest[n - 1], nc.scalar if n > 3 and n % 2 == 1 else nc.sync)
-            if n == 2:
+                finish(rest[n - 1], nc.scalar if n % 2 == 1 else nc.sync)
+            if n == 1:
                 quantise_part("h", 3, 1)
         finish(rest[-1])

@@ -20,7 +20,7 @@ ADD = mybir.AluOpType.add
 COPY = mybir.ActivationFunctionType.Copy
 
 LOADS = [("P", 0), ("P", 1), ("F", 0), ("F", 1), ("P", 2), ("P", 3), ("F", 2), ("F", 3)]
-SHARED = [("P", 0, 0), ("P", 1, 0), ("P", 1, 1), ("F", 0, 0), ("P", 2, 0)]
+SHARED = [("P", 0, 0), ("P", 1, 0), ("P", 1, 1), ("F", 0, 0), ("P", 2, 0), ("F", 3, 1)]
 EMPTY_LAG = 4
 
 def tile_kalman_predicted_covariance_d2_kernel(tc, P_bytes, P_scale, F_bytes, F_scale, g, Q, out):
@@ -65,15 +65,15 @@ def tile_kalman_predicted_covariance_d2_kernel(tc, P_bytes, P_scale, F_bytes, F_
                 nc.sync.dma_start(out=part[:], in_=rows)
             raw[(kind, pair)] = part
 
+        g_all = keep.tile([P, N], BF16, name="g_all")
+        nc.sync.dma_start(out=g_all[:], in_=g.partition_broadcast(P))
+
         q_rows = Q.rearrange("(b p) n -> p b n", p=P)
         q_tiles = []
         for pair in range(4):
             part = keep.tile([P, 2, N], BF16, name="q%d" % pair)
             nc.sync.dma_start(out=part[:], in_=q_rows[:, 2 * pair : 2 * pair + 2, :])
             q_tiles.append(part)
-
-        g_all = keep.tile([P, PASS], BF16, name="g_all")
-        nc.sync.dma_start(out=g_all[:], in_=g[PASS:N].partition_broadcast(P))
 
         unit_cols = keep.tile([P, 8], BF16, name="unit_cols")
         nc.scalar.activation(out=unit_cols[:], in_=ident[:, 0:8], func=COPY)
@@ -199,29 +199,31 @@ def tile_kalman_predicted_covariance_d2_kernel(tc, P_bytes, P_scale, F_bytes, F_
             cols = slice(PAIR * u, PAIR * u + PAIR)
             one_pass(banks[("sum", b, c)][:, cols], b, 1, ("P", 2 * c + 1), cols, closes=(u == 1))
 
-        def direct(b, c):
+        def direct(b, c, passes=(0, 1)):
             key = ("direct", b, c)
-            take_bank(key, [P, 4, P])
             f_words, f_scales = codes[("F", b // 2)]
-            for t in range(4):
-                for k in range(2):
-                    words, scales = codes[("P", 2 * c + k)]
-                    tile_b = slice(PAIR * k + P * (b % 2), PAIR * k + P * (b % 2) + P)
+            for k in passes:
+                if k == 0:
+                    take_bank(key, [P, 4, P])
+                words, scales = codes[("P", 2 * c + k)]
+                tile_b = slice(PAIR * k + P * (b % 2), PAIR * k + P * (b % 2) + P)
+                for t in range(4):
                     nc.tensor.matmul_mx(
                         out=banks[key][:, t, :],
                         lhsT=words[:, P * t : P * t + P].bitcast(FP8X4),
                         lhsT_scale=scales[:, P * t : P * t + P],
                         rhs=f_words[:, tile_b].bitcast(FP8X4),
                         rhs_scale=f_scales[:, tile_b],
-                        start=(k == 0),
-                        stop=(k == 1),
+                        start=(k == 0 and t == 0),
+                        stop=(k == 1 and t == 3),
                     )
 
         def direct_gain(b, c):
             key = ("direct", b, c)
-            col = PAIR * c + P * (b % 2)
-            dst = grouped[("h", b // 2)][:, 4 * col : 4 * col + PASS].rearrange("p (r t) -> p r t", t=4)
-            factor = g_all[:, P * b - PASS : P * b - PASS + P].unsqueeze(2).to_broadcast([P, P, 4])
+            group, col = place("h", b // 2, c)
+            col = col + P * (b % 2)
+            dst = grouped[group][:, 4 * col : 4 * col + PASS].rearrange("p (r t) -> p r t", t=4)
+            factor = g_all[:, P * b : P * b + P].unsqueeze(2).to_broadcast([P, P, 4])
             nc.vector.tensor_tensor(out=dst, in0=banks[key][:].rearrange("p t r -> p r t"), in1=factor, op=MULT)
             give_bank(key)
 
@@ -355,44 +357,42 @@ def tile_kalman_predicted_covariance_d2_kernel(tc, P_bytes, P_scale, F_bytes, F_
         quantise(("P", 2))
         widen_unit("F", 2, 0, (0,))
         for b in range(4):
-            first(b, 1, (0,))
+            direct(b, 1, (0,))
         quantise(("P", 3))
         widen_unit("F", 2, 0, (1,))
         for b in range(4):
             gain(b, 0)
         for b in range(4):
-            first(b, 1, (1,))
+            direct(b, 1, (1,))
 
         for unit in [("F", 2, 1), ("F", 3, 0), ("F", 3, 1)]:
             widen_unit(*unit)
         for unit in [("F", 2, 0), ("F", 2, 1), ("h", 0, 0), ("h", 1, 0)]:
             turn(*unit)
-        for pair, kind in [(0, "F"), (1, "h")]:
-            gain(2 * pair, 1)
-            gain(2 * pair + 1, 1, on_vector=True)
-            for j in range(2):
-                if kind == "F":
-                    turn("F", 3, j)
-                else:
-                    turn("h", j, 1)
         third = [(b, half) for half in range(2) for b in (4, 5)]
+        direct_gain(0, 1)
+        turn("F", 3, 0)
         empty("F", 2, 0)
+        turn("F", 3, 1)
+        direct_gain(1, 1)
         quantise_part("F", 2, 0)
         empty("F", 2, 1)
-        empty("F", 3, 0, on_vector=True)
-        empty("h", 0, 0)
-        for b, half in third:
+        for b, half in third[:2]:
             first(b, half, (0,))
         quantise_part("F", 2, 1)
-        empty("h", 1, 0)
+        empty("F", 3, 0)
+        direct_gain(2, 1)
+        for b, half in third[2:]:
+            first(b, half, (0,))
         for b, half in third:
             first(b, half, (1,))
         empty("F", 3, 1)
-        empty("h", 0, 1)
+        direct_gain(3, 1)
+        for pair in range(2):
+            empty("h", pair, 0)
         quantise(("F", 3))
-        quantise(("h", 0))
-        empty("h", 1, 1)
         quantise(("h", 1))
+        quantise(("h", 0))
 
         left = [((b, 0), (b, 1)) for b in range(8)]
         thirds = [((2 * j, 2), (2 * j + 1, 2)) for j in range(4)]

@@ -30,10 +30,10 @@ def tile_kalman_predicted_covariance_d2_kernel(tc, P_bytes, P_scale, F_bytes, F_
         psum = ctx.enter_context(tc.psum_pool(name="psum", bufs=1))
         ctx.enter_context(tc.manual_schedule())
 
-        f_row = keep.tile([P, 64], F32, name="f_row")
-        nc.gpsimd.memset(f_row[:], 0.0)
-        g_rows = keep.tile([P, P], BF16, name="g_rows")
-        nc.gpsimd.memset(g_rows[:], 0.0)
+        small = keep.tile([P, P], F32, name="small")
+        nc.gpsimd.memset(small[:], 0.0)
+        f_row = small[:, 0:64]
+        g_rows = small[:, 64:P].bitcast(BF16)
         ident = keep.tile([P, P], F32, name="ident")
         make_identity(nc, ident[:])
 
@@ -113,8 +113,8 @@ def tile_kalman_predicted_covariance_d2_kernel(tc, P_bytes, P_scale, F_bytes, F_
         def spread_matmuls():
             take_bank("spread", [P, PASS])
             row_0 = ident[:, 0:1].to_broadcast([P, P])
-            nc.tensor.matmul(banks["spread"][:, 0:64], lhsT=row_0, rhs=f_row[:], start=True, stop=True)
-            nc.tensor.matmul(banks["spread"][:, 64:72], lhsT=g_rows[:], rhs=unit_cols[:], start=True, stop=True)
+            nc.tensor.matmul(banks["spread"][:, 0:64], lhsT=row_0, rhs=f_row, start=True, stop=True)
+            nc.tensor.matmul(banks["spread"][:, 64:72], lhsT=g_rows, rhs=unit_cols[:], start=True, stop=True)
 
         def copy_spread():
             nc.vector.tensor_copy(out=spread[:], in_=banks["spread"][:, 0:72])
@@ -226,6 +226,46 @@ def tile_kalman_predicted_covariance_d2_kernel(tc, P_bytes, P_scale, F_bytes, F_
             factor = g_all[:, P * b : P * b + P].unsqueeze(2).to_broadcast([P, P, 4])
             nc.vector.tensor_tensor(out=dst, in0=banks[key][:].rearrange("p t r -> p r t"), in1=factor, op=MULT)
             give_bank(key)
+
+        def direct_wide(pair, c, u, passes=(0, 1)):
+            key = ("wide", pair, c, u)
+            f_words, f_scales = codes[("F", pair)]
+            for k in passes:
+                if k == 0:
+                    take_bank(key, [P, 2, PAIR])
+                words, scales = codes[("P", 2 * c + k)]
+                cols = slice(PAIR * k, PAIR * k + PAIR)
+                for x in range(2):
+                    place_t = slice(P * (2 * u + x), P * (2 * u + x) + P)
+                    nc.tensor.matmul_mx(
+                        out=banks[key][:, x, :],
+                        lhsT=words[:, place_t].bitcast(FP8X4),
+                        lhsT_scale=scales[:, place_t],
+                        rhs=f_words[:, cols].bitcast(FP8X4),
+                        rhs_scale=f_scales[:, cols],
+                        start=(k == 0 and x == 0),
+                        stop=(k == 1 and x == 1),
+                    )
+
+        paired = {}
+
+        def wide_gain(pair, c, u):
+            key = ("wide", pair, c, u)
+            if u == 0:
+                paired[(pair, c)] = keep.tile([P, 4 * PAIR], BF16, name="paired%d%d" % (pair, c), align_bytes=64)
+            dst = paired[(pair, c)][:, PASS * u : PASS * u + PASS].rearrange("p (n x) -> p n x", x=2)
+            factor = g_all[:, PAIR * pair : PAIR * pair + PAIR].unsqueeze(2).to_broadcast([P, PAIR, 2])
+            nc.vector.tensor_tensor(out=dst, in0=banks[key][:].rearrange("p x n -> p n x"), in1=factor, op=MULT)
+            give_bank(key)
+
+        def join(pair, c, on_vector=False):
+            group, col = place("h", pair, c)
+            dst = grouped[group][:].bitcast(F32)[:, 2 * col : 2 * col + 2 * PAIR].rearrange("p (n u) -> p n u", u=2)
+            src = paired[(pair, c)][:].bitcast(F32).rearrange("p (u n) -> p n u", u=2)
+            if on_vector:
+                nc.vector.tensor_copy(out=dst, in_=src)
+            else:
+                nc.scalar.copy(out=dst, in_=src)
 
         def gain(b, c, on_vector=False):
             key = ("sum", b, c)
@@ -357,57 +397,59 @@ def tile_kalman_predicted_covariance_d2_kernel(tc, P_bytes, P_scale, F_bytes, F_
         quantise(("P", 2))
         widen_unit("F", 2, 0, (0,))
         for b in range(4):
-            direct(b, 1, (0,))
+            direct_wide(b // 2, 1, b % 2, (0,))
         quantise(("P", 3))
         widen_unit("F", 2, 0, (1,))
         for b in range(4):
             gain(b, 0)
         for b in range(4):
-            direct(b, 1, (1,))
+            direct_wide(b // 2, 1, b % 2, (1,))
 
         for unit in [("F", 2, 1), ("F", 3, 0), ("F", 3, 1)]:
             widen_unit(*unit)
         for unit in [("F", 2, 0), ("F", 2, 1), ("h", 0, 0), ("h", 1, 0)]:
             turn(*unit)
         third = [(b, half) for half in range(2) for b in (4, 5)]
-        direct_gain(0, 1)
+        wide_gain(0, 1, 0)
         turn("F", 3, 0)
         empty("F", 2, 0)
         turn("F", 3, 1)
-        direct_gain(1, 1)
+        wide_gain(0, 1, 1)
         quantise_part("F", 2, 0)
+        join(0, 1, on_vector=True)
         empty("F", 2, 1)
+        empty("h", 0, 0)
         for b, half in third[:2]:
             first(b, half, (0,))
         quantise_part("F", 2, 1)
         empty("F", 3, 0)
-        direct_gain(2, 1)
+        wide_gain(1, 1, 0)
         for b, half in third[2:]:
             first(b, half, (0,))
         for b, half in third:
             first(b, half, (1,))
         empty("F", 3, 1)
-        direct_gain(3, 1)
-        for pair in range(2):
-            empty("h", pair, 0)
+        wide_gain(1, 1, 1)
+        empty("h", 1, 0)
+        join(1, 1)
         quantise(("F", 3))
-        quantise(("h", 1))
         quantise(("h", 0))
+        quantise(("h", 1))
 
         left = [((b, 0), (b, 1)) for b in range(8)]
         thirds = [((2 * j, 2), (2 * j + 1, 2)) for j in range(4)]
         last = [((2 * j, 3), (2 * j + 1, 3)) for j in range(3)] + [((6, 3),), ((7, 3),)]
-        shared = [left[b] for b in (5,)]
+        shared = [left[b] for b in (4,)]
         for b, c in third:
             gain(b, c)
-        for b in (6, 7):
-            direct(b, 0)
-            direct_gain(b, 0)
+        for u in range(2):
+            direct_wide(3, 0, u)
+            wide_gain(3, 0, u)
+        join(3, 0)
         for b in range(3):
             second(left[b])
             finish(left[b])
-            if b == 0:
-                quantise_part("h", 3, 0)
+        quantise_part("h", 3, 0)
         for k in range(2):
             turn("h", 2, k)
         for k in range(2):
@@ -430,6 +472,7 @@ def tile_kalman_predicted_covariance_d2_kernel(tc, P_bytes, P_scale, F_bytes, F_
         direct_gain(6, 1)
         direct(7, 1)
         finish(left[7])
+        quantise(("h", 3), slice(PAIR, PAIR + P))
         for parts in shared:
             store(parts)
         rest = thirds + last
@@ -440,5 +483,5 @@ def tile_kalman_predicted_covariance_d2_kernel(tc, P_bytes, P_scale, F_bytes, F_
             if n > 0:
                 finish(rest[n - 1], nc.scalar if n % 2 == 1 else nc.sync)
             if n == 1:
-                quantise_part("h", 3, 1)
-        finish(rest[-1])
+                quantise(("h", 3), slice(PAIR + P, PASS))
+        finish(rest[-1], nc.scalar)

@@ -439,7 +439,7 @@ def tile_kalman_predicted_covariance_d2_kernel(tc, P_bytes, P_scale, F_bytes, F_
         left = [((b, 0), (b, 1)) for b in range(8)]
         thirds = [((2 * j, 2), (2 * j + 1, 2)) for j in range(4)]
         last = [((2 * j, 3), (2 * j + 1, 3)) for j in range(3)] + [((6, 3),), ((7, 3),)]
-        shared = [left[b] for b in (4,)]
+        shared = [left[b] for b in (5,)]
         for b, c in third:
             gain(b, c)
         for u in range(2):
@@ -472,7 +472,6 @@ def tile_kalman_predicted_covariance_d2_kernel(tc, P_bytes, P_scale, F_bytes, F_
         direct_gain(6, 1)
         direct(7, 1)
         finish(left[7])
-        quantise(("h", 3), slice(PAIR, PAIR + P))
         for parts in shared:
             store(parts)
         rest = thirds + last
@@ -483,5 +482,5 @@ def tile_kalman_predicted_covariance_d2_kernel(tc, P_bytes, P_scale, F_bytes, F_
             if n > 0:
                 finish(rest[n - 1], nc.scalar if n % 2 == 1 else nc.sync)
             if n == 1:
-                quantise(("h", 3), slice(PAIR + P, PASS))
+                quantise_part("h", 3, 1)
         finish(rest[-1], nc.scalar)

@@ -402,13 +402,16 @@ def tile_kalman_predicted_covariance_d2_kernel(tc, P_bytes, P_scale, F_bytes, F_
         widen_unit("F", 2, 0, (1,))
         for b in range(4):
             gain(b, 0)
-        for b in range(4):
-            direct_wide(b // 2, 1, b % 2, (1,))
+        for u in range(2):
+            direct_wide(0, 1, u, (1,))
 
         for unit in [("F", 2, 1), ("F", 3, 0), ("F", 3, 1)]:
             widen_unit(*unit)
-        for unit in [("F", 2, 0), ("F", 2, 1), ("h", 0, 0), ("h", 1, 0)]:
+        for unit in [("F", 2, 0), ("F", 2, 1), ("h", 0, 0)]:
             turn(*unit)
+        for u in range(2):
+            direct_wide(1, 1, u, (1,))
+        turn("h", 1, 0)
         third = [(b, half) for half in range(2) for b in (4, 5)]
         wide_gain(0, 1, 0)
         turn("F", 3, 0)

@@ -20,8 +20,11 @@ ADD = mybir.AluOpType.add
 COPY = mybir.ActivationFunctionType.Copy
 
 LOADS = [("P", 0), ("P", 1), ("F", 0), ("F", 1), ("P", 2), ("P", 3), ("F", 2), ("F", 3)]
-SHARED = [("P", 0, 0), ("P", 1, 0), ("P", 1, 1), ("F", 0, 0), ("P", 2, 0), ("F", 3, 1)]
+ON_SCALAR = [("P", 0, 0), ("P", 1, 0), ("P", 1, 1), ("F", 0, 0), ("P", 2, 0), ("F", 3, 1)]
 EMPTY_LAG = 4
+EARLY_TILES = 3
+SHARED_TILE = 5
+
 
 def tile_kalman_predicted_covariance_d2_kernel(tc, P_bytes, P_scale, F_bytes, F_scale, g, Q, out):
     nc = tc.nc
@@ -58,22 +61,24 @@ def tile_kalman_predicted_covariance_d2_kernel(tc, P_bytes, P_scale, F_bytes, F_
                 load_p_scales(nc.sync, 1)
             part = keep.tile([P, 2, N], U8, name="bytes_%s%d" % (kind, pair))
             rows = p_rows[:, pair // 2, pair % 2] if kind == "P" else f_rows[:, pair]
-            if not raw:
+            if (kind, pair) == LOADS[0]:
                 for e in range(2):
                     nc.sync.dma_start(out=part[:, e, :], in_=rows[:, e, :])
             else:
                 nc.sync.dma_start(out=part[:], in_=rows)
             raw[(kind, pair)] = part
 
-        g_all = keep.tile([P, N], BF16, name="g_all")
-        nc.sync.dma_start(out=g_all[:], in_=g.partition_broadcast(P))
-
+        g_first = keep.tile([P, PASS], BF16, name="g_first")
+        nc.sync.dma_start(out=g_first[:], in_=g[0:PASS].partition_broadcast(P))
         q_rows = Q.rearrange("(b p) n -> p b n", p=P)
         q_tiles = []
         for pair in range(4):
             part = keep.tile([P, 2, N], BF16, name="q%d" % pair)
             nc.sync.dma_start(out=part[:], in_=q_rows[:, 2 * pair : 2 * pair + 2, :])
             q_tiles.append(part)
+        g_last = keep.tile([P, PAIR], BF16, name="g_last")
+        nc.sync.dma_start(out=g_last[:], in_=g[N - PAIR : N].partition_broadcast(P))
+        g_free = {0: g_first[:, 0:PAIR], 1: g_first[:, PAIR:PASS], 3: g_last[:]}
 
         unit_cols = keep.tile([P, 8], BF16, name="unit_cols")
         nc.scalar.activation(out=unit_cols[:], in_=ident[:, 0:8], func=COPY)
@@ -121,24 +126,26 @@ def tile_kalman_predicted_covariance_d2_kernel(tc, P_bytes, P_scale, F_bytes, F_
             give_bank("spread")
 
         wide = {}
-        in_order = set()
 
-        def widen(kind, pair, k, e, on_scalar=False):
-            tile = keep.tile([P, PASS], BF16, name="wide_%s%d%d%d" % (kind, pair, k, e), align_bytes=64)
-            wide[(kind, pair, k, e)] = tile
-            by_u = tile[:].rearrange("p (u c q x) -> p c q u x", u=2, c=4, x=2)
-            for c in range(4):
-                block = 4 * k + c
-                src = raw[(kind, pair)][:, e, P * block : P * block + P].bitcast(FP8)
-                if kind == "P":
-                    col = p_scale[pair][:, 8 * e + block : 8 * e + block + 1]
-                else:
-                    col = spread[:, 16 * pair + 8 * e + block : 16 * pair + 8 * e + block + 1]
-                if on_scalar:
-                    in_order.add((kind, pair, k, e))
-                    nc.scalar.activation(out=tile[:, P * c : P * c + P], in_=src, func=COPY, scale=col)
-                else:
-                    nc.vector.tensor_scalar(out=by_u[:, c], in0=src, scalar1=col, scalar2=None, op0=MULT)
+        def in_order(kind, pair, k, e):
+            return e == 1 and (kind, pair, k) in ON_SCALAR
+
+        def widen(kind, pair, k, tiles=(0, 1)):
+            for e in tiles:
+                tile = keep.tile([P, PASS], BF16, name="wide_%s%d%d%d" % (kind, pair, k, e), align_bytes=64)
+                wide[(kind, pair, k, e)] = tile
+                by_u = tile[:].rearrange("p (u c q x) -> p c q u x", u=2, c=4, x=2)
+                for c in range(4):
+                    block = 4 * k + c
+                    src = raw[(kind, pair)][:, e, P * block : P * block + P].bitcast(FP8)
+                    if kind == "P":
+                        col = p_scale[pair][:, 8 * e + block : 8 * e + block + 1]
+                    else:
+                        col = spread[:, 16 * pair + 8 * e + block : 16 * pair + 8 * e + block + 1]
+                    if in_order(kind, pair, k, e):
+                        nc.scalar.activation(out=tile[:, P * c : P * c + P], in_=src, func=COPY, scale=col)
+                    else:
+                        nc.vector.tensor_scalar(out=by_u[:, c], in0=src, scalar1=col, scalar2=None, op0=MULT)
 
         def turn(kind, pair, k, tiles=(0, 1)):
             unit = (kind, pair, k)
@@ -147,22 +154,20 @@ def tile_kalman_predicted_covariance_d2_kernel(tc, P_bytes, P_scale, F_bytes, F_
             for e in tiles:
                 words = wide[(kind, pair, k, e)][:].bitcast(F32)
                 for u in range(2):
-                    if (kind, pair, k, e) in in_order:
+                    if in_order(kind, pair, k, e):
                         src = words[:, u : 2 * P : 2]
                     else:
                         src = words[:, P * u : P * u + P]
                     nc.tensor.transpose(banks[unit][:, e, u, :], src, ident[:])
 
-        def empty(kind, pair, k, on_vector=False):
-            unit = (kind, pair, k)
+        def unit_words(kind, pair, k):
             group, col = place(kind, pair, k)
-            words = grouped[group][:].bitcast(F32)[:, 2 * col : 2 * col + 2 * PAIR]
-            dst = words.rearrange("p (e r u) -> p e r u", e=2, u=2)
-            src = banks[unit][:].rearrange("p e u r -> p e r u")
-            if on_vector:
-                nc.vector.tensor_copy(out=dst, in_=src)
-            else:
-                nc.scalar.copy(out=dst, in_=src)
+            return grouped[group][:].bitcast(F32)[:, 2 * col : 2 * col + 2 * PAIR]
+
+        def empty(kind, pair, k):
+            unit = (kind, pair, k)
+            dst = unit_words(kind, pair, k).rearrange("p (e r u) -> p e r u", e=2, u=2)
+            nc.scalar.copy(out=dst, in_=banks[unit][:].rearrange("p e u r -> p e r u"))
             give_bank(unit)
 
         def quantise(group, cols=slice(0, PASS)):
@@ -170,181 +175,120 @@ def tile_kalman_predicted_covariance_d2_kernel(tc, P_bytes, P_scale, F_bytes, F_
             values = grouped[group][:, 4 * cols.start : 4 * cols.stop]
             nc.vector.quantize_mx(out=words[:, cols].bitcast(FP8X4), scales=scales[:, cols], in_=values)
 
-        def quantise_part(kind, pair, k):
+        def quantise_unit(kind, pair, k):
             group, col = place(kind, pair, k)
             quantise(group, slice(col, col + PAIR))
 
-        def one_pass(dst, b, k, group, cols, closes=True):
-            f_words, f_scales = codes[("F", b // 2)]
-            tile_b = slice(PAIR * k + P * (b % 2), PAIR * k + P * (b % 2) + P)
-            words, scales = codes[group]
+        def one_pass(dst, stationary, moving, start, stop):
+            lhs_words, lhs_scales = codes[stationary[0]]
+            rhs_words, rhs_scales = codes[moving[0]]
             nc.tensor.matmul_mx(
                 out=dst,
-                lhsT=f_words[:, tile_b].bitcast(FP8X4),
-                lhsT_scale=f_scales[:, tile_b],
-                rhs=words[:, cols].bitcast(FP8X4),
-                rhs_scale=scales[:, cols],
-                start=(k == 0),
-                stop=(k == 1 and closes),
+                lhsT=lhs_words[:, stationary[1]].bitcast(FP8X4),
+                lhsT_scale=lhs_scales[:, stationary[1]],
+                rhs=rhs_words[:, moving[1]].bitcast(FP8X4),
+                rhs_scale=rhs_scales[:, moving[1]],
+                start=start,
+                stop=stop,
             )
 
-        def first(b, c, passes=(0, 1)):
-            key = ("sum", b, c)
-            for k in passes:
-                if k == 0:
-                    take_bank(key, [P, PASS])
-                one_pass(banks[key][:], b, k, ("P", 2 * c + k), slice(0, PASS))
+        def f_tile(b, k):
+            col = PAIR * k + P * (b % 2)
+            return ("F", b // 2), slice(col, col + P)
 
-        def first_part(b, c, u):
-            cols = slice(PAIR * u, PAIR * u + PAIR)
-            one_pass(banks[("sum", b, c)][:, cols], b, 1, ("P", 2 * c + 1), cols, closes=(u == 1))
+        def p_place(c, t, k):
+            return ("P", 2 * c + k), slice(P * t, P * t + P)
 
-        def direct(b, c, passes=(0, 1)):
-            key = ("direct", b, c)
-            f_words, f_scales = codes[("F", b // 2)]
-            for k in passes:
-                if k == 0:
-                    take_bank(key, [P, 4, P])
-                words, scales = codes[("P", 2 * c + k)]
-                tile_b = slice(PAIR * k + P * (b % 2), PAIR * k + P * (b % 2) + P)
-                for t in range(4):
-                    nc.tensor.matmul_mx(
-                        out=banks[key][:, t, :],
-                        lhsT=words[:, P * t : P * t + P].bitcast(FP8X4),
-                        lhsT_scale=scales[:, P * t : P * t + P],
-                        rhs=f_words[:, tile_b].bitcast(FP8X4),
-                        rhs_scale=f_scales[:, tile_b],
-                        start=(k == 0 and t == 0),
-                        stop=(k == 1 and t == 3),
-                    )
+        def sum_f(b, c, k):
+            key = ("sum_f", b, c)
+            if k == 0:
+                take_bank(key, [P, PASS])
+            one_pass(banks[key][:], f_tile(b, k), (("P", 2 * c + k), slice(0, PASS)), k == 0, k == 1)
 
-        def direct_gain(b, c):
-            key = ("direct", b, c)
-            group, col = place("h", b // 2, c)
-            col = col + P * (b % 2)
-            dst = grouped[group][:, 4 * col : 4 * col + PASS].rearrange("p (r t) -> p r t", t=4)
-            factor = g_all[:, P * b : P * b + P].unsqueeze(2).to_broadcast([P, P, 4])
-            nc.vector.tensor_tensor(out=dst, in0=banks[key][:].rearrange("p t r -> p r t"), in1=factor, op=MULT)
-            give_bank(key)
-
-        def direct_wide(pair, c, u, passes=(0, 1)):
-            key = ("wide", pair, c, u)
-            f_words, f_scales = codes[("F", pair)]
-            for k in passes:
-                if k == 0:
-                    take_bank(key, [P, 2, PAIR])
-                words, scales = codes[("P", 2 * c + k)]
-                cols = slice(PAIR * k, PAIR * k + PAIR)
-                for x in range(2):
-                    place_t = slice(P * (2 * u + x), P * (2 * u + x) + P)
-                    nc.tensor.matmul_mx(
-                        out=banks[key][:, x, :],
-                        lhsT=words[:, place_t].bitcast(FP8X4),
-                        lhsT_scale=scales[:, place_t],
-                        rhs=f_words[:, cols].bitcast(FP8X4),
-                        rhs_scale=f_scales[:, cols],
-                        start=(k == 0 and x == 0),
-                        stop=(k == 1 and x == 1),
-                    )
-
-        paired = {}
-
-        def wide_gain(pair, c, u):
-            key = ("wide", pair, c, u)
-            if u == 0:
-                paired[(pair, c)] = keep.tile([P, 4 * PAIR], BF16, name="paired%d%d" % (pair, c), align_bytes=64)
-            dst = paired[(pair, c)][:, PASS * u : PASS * u + PASS].rearrange("p (n x) -> p n x", x=2)
-            factor = g_all[:, PAIR * pair : PAIR * pair + PAIR].unsqueeze(2).to_broadcast([P, PAIR, 2])
-            nc.vector.tensor_tensor(out=dst, in0=banks[key][:].rearrange("p x n -> p n x"), in1=factor, op=MULT)
-            give_bank(key)
-
-        def join(pair, c, on_vector=False):
-            group, col = place("h", pair, c)
-            dst = grouped[group][:].bitcast(F32)[:, 2 * col : 2 * col + 2 * PAIR].rearrange("p (n u) -> p n u", u=2)
-            src = paired[(pair, c)][:].bitcast(F32).rearrange("p (u n) -> p n u", u=2)
-            if on_vector:
-                nc.vector.tensor_copy(out=dst, in_=src)
-            else:
-                nc.scalar.copy(out=dst, in_=src)
-
-        def gain(b, c, on_vector=False):
-            key = ("sum", b, c)
+        def gain_f(b, c):
+            key = ("sum_f", b, c)
             tile = keep.tile([P, PASS], BF16, name="h_wide%d%d" % (b, c), align_bytes=64)
             wide[("h", b // 2, c, b % 2)] = tile
             dst = tile[:].rearrange("p (u q x) -> p u q x", u=2, x=2)
             src = banks[key][:].rearrange("p (u x q) -> p u q x", u=2, x=2)
-            if on_vector:
-                nc.vector.tensor_scalar(out=dst, in0=src, scalar1=g_col[:, b : b + 1], scalar2=None, op0=MULT)
-            else:
-                nc.scalar.activation(out=dst, in_=src, func=COPY, scale=g_col[:, b : b + 1])
+            nc.scalar.activation(out=dst, in_=src, func=COPY, scale=g_col[:, b : b + 1])
             give_bank(key)
 
-        def second(parts):
-            take_bank(parts, [P, len(parts), PAIR])
-            if parts[0][1] < 2:
-                cols = slice(PAIR * parts[0][1], PAIR * parts[-1][1] + PAIR)
+        def sum_p(pair, c, u, k):
+            key = ("sum_p", pair, c, u)
+            if k == 0:
+                take_bank(key, [P, 2, PAIR])
+            moving = (("F", pair), slice(PAIR * k, PAIR * k + PAIR))
+            for x in range(2):
+                one_pass(banks[key][:, x, :], p_place(c, 2 * u + x, k), moving, (k, x) == (0, 0), (k, x) == (1, 1))
+
+        halves = {}
+
+        def gain_p(pair, c, u):
+            key = ("sum_p", pair, c, u)
+            if u == 0:
+                halves[(pair, c)] = keep.tile([P, 4 * PAIR], BF16, name="halves%d%d" % (pair, c), align_bytes=64)
+            dst = halves[(pair, c)][:, PASS * u : PASS * u + PASS].rearrange("p (n x) -> p n x", x=2)
+            factor = g_free[pair].unsqueeze(2).to_broadcast([P, PAIR, 2])
+            nc.vector.tensor_tensor(out=dst, in0=banks[key][:].rearrange("p x n -> p n x"), in1=factor, op=MULT)
+            give_bank(key)
+
+        def join(pair, c):
+            dst = unit_words("h", pair, c).rearrange("p (n u) -> p n u", u=2)
+            nc.scalar.copy(out=dst, in_=halves[(pair, c)][:].bitcast(F32).rearrange("p (u n) -> p n u", u=2))
+
+        def sum_p4(b, c):
+            key = ("sum_p4", b, c)
+            take_bank(key, [P, 4, P])
+            for k in range(2):
+                for t in range(4):
+                    one_pass(banks[key][:, t, :], p_place(c, t, k), f_tile(b, k), (k, t) == (0, 0), (k, t) == (1, 3))
+
+        def gain_p4(b, c):
+            key = ("sum_p4", b, c)
+            group, col = place("h", b // 2, c)
+            col = col + P * (b % 2)
+            dst = grouped[group][:, 4 * col : 4 * col + PASS].rearrange("p (r t) -> p r t", t=4)
+            factor = g_free[b // 2][:, P * (b % 2) : P * (b % 2) + P].unsqueeze(2).to_broadcast([P, P, 4])
+            nc.vector.tensor_tensor(out=dst, in0=banks[key][:].rearrange("p t r -> p r t"), in1=factor, op=MULT)
+            give_bank(key)
+
+        def product(piece):
+            b, tiles, col, width = piece
+            take_bank(piece, [P, tiles, width])
+            for j in range(tiles):
                 for k in range(2):
-                    one_pass(banks[parts][:].rearrange("p j n -> p (j n)"), parts[0][0], k, ("h", k), cols)
-                return
-            for j, (b, h_pair) in enumerate(parts):
-                for k in range(2):
-                    one_pass(banks[parts][:, j, :], b, k, ("h", h_pair), slice(PAIR * k, PAIR * k + PAIR))
+                    group, first = place("h", col // PAIR, k)
+                    one_pass(banks[piece][:, j, :], f_tile(b + j, k), (group, slice(first, first + width)), k == 0, k == 1)
 
-        def finish_shared(parts):
-            b, h_pair = parts[0]
-            scaled = keep.tile([P, 2, PAIR], F32, name="scaled_%d_%d" % parts[0])
-            result = keep.tile([P, 2, PAIR], F32, name="res_%d_%d" % parts[0])
-            if parts[1][0] == b:
-                cols = slice(PAIR * h_pair, PAIR * h_pair + PASS)
-                flat = "p j n -> p (j n)"
-                src = banks[parts][:].rearrange(flat)
-                nc.scalar.activation(out=scaled[:].rearrange(flat), in_=src, func=COPY, scale=g_col[:, b : b + 1])
-                noise = q_tiles[b // 2][:, b % 2, cols].rearrange("p (j n) -> p j n", j=2)
-                dst = out[P * b : P * b + P, cols].rearrange("p (j n) -> p j n", j=2)
-            else:
-                cols = slice(PAIR * h_pair, PAIR * h_pair + PAIR)
-                for j in range(2):
-                    factor = g_col[:, b + j : b + j + 1]
-                    nc.scalar.activation(out=scaled[:, j, :], in_=banks[parts][:, j, :], func=COPY, scale=factor)
-                noise = q_tiles[b // 2][:, :, cols]
-                dst = out[P * b : P * b + 2 * P, cols].rearrange("(j p) n -> p j n", p=P)
-            give_bank(parts)
-            nc.gpsimd.tensor_tensor(out=result[:], in0=scaled[:], in1=noise, op=ADD)
-            pending[parts] = (dst, result)
+        def out_view(piece):
+            b, tiles, col, width = piece
+            return out[P * b : P * b + P * tiles, col : col + width].rearrange("(j p) n -> p j n", p=P)
 
-        pending = {}
-
-        def store(parts):
-            dst, result = pending[parts]
-            nc.scalar.dma_start(out=dst, in_=result[:])
-
-        def finish(parts, queue=nc.sync):
-            result = keep.tile([P, len(parts), PAIR], F32, name="res_%d_%d" % parts[0])
-            b, h_pair = parts[0]
-            if len(parts) == 2 and parts[1][0] == b:
-                cols = slice(PAIR * h_pair, PAIR * h_pair + PASS)
-                steps = [(b, cols, result[:].rearrange("p j n -> p (j n)"), banks[parts][:].rearrange("p j n -> p (j n)"))]
-                dst = out[P * b : P * b + P, cols].rearrange("p (j n) -> p j n", j=2)
-            else:
-                cols = slice(PAIR * h_pair, PAIR * h_pair + PAIR)
-                steps = [(b + j, cols, result[:, j, :], banks[parts][:, j, :]) for j in range(len(parts))]
-                dst = out[P * b : P * b + len(parts) * P, cols].rearrange("(j p) n -> p j n", p=P)
-            for row_tile, cols, res, src in steps:
+        def finish(piece, queue=nc.sync):
+            b, tiles, col, width = piece
+            result = keep.tile([P, tiles, width], F32, name="res_%d_%d" % (b, col))
+            for j in range(tiles):
                 nc.vector.scalar_tensor_tensor(
-                    out=res,
-                    in0=src,
-                    scalar=g_col[:, row_tile : row_tile + 1],
-                    in1=q_tiles[row_tile // 2][:, row_tile % 2, cols],
+                    out=result[:, j, :],
+                    in0=banks[piece][:, j, :],
+                    scalar=g_col[:, b + j : b + j + 1],
+                    in1=q_tiles[(b + j) // 2][:, (b + j) % 2, col : col + width],
                     op0=MULT,
                     op1=ADD,
                 )
-            give_bank(parts)
-            queue.dma_start(out=dst, in_=result[:])
+            give_bank(piece)
+            queue.dma_start(out=out_view(piece), in_=result[:])
 
-
-        def widen_unit(kind, pair, k, tiles=(0, 1)):
-            for e in tiles:
-                widen(kind, pair, k, e, on_scalar=(e == 1 and (kind, pair, k) in SHARED))
+        def finish_shared(piece):
+            b, tiles, col, width = piece
+            scaled = keep.tile([P, tiles, width], F32, name="scaled")
+            nc.scalar.activation(out=scaled[:, 0, :], in_=banks[piece][:, 0, :], func=COPY, scale=g_col[:, b : b + 1])
+            give_bank(piece)
+            result = keep.tile([P, tiles, width], F32, name="res_shared")
+            noise = q_tiles[b // 2][:, b % 2, col : col + width]
+            nc.gpsimd.tensor_tensor(out=result[:, 0, :], in0=scaled[:, 0, :], in1=noise, op=ADD)
+            return result
 
         head = [(kind, pair, k) for kind in ["P", "F"] for pair in range(2) for k in range(2)]
         f_banks = [("F", pair, k) for k in range(2) for pair in range(2)]
@@ -352,138 +296,139 @@ def tile_kalman_predicted_covariance_d2_kernel(tc, P_bytes, P_scale, F_bytes, F_
         for k in range(2):
             to_empty.extend([("P", 0, k), ("P", 1, k), f_banks[k]])
         to_empty.extend(f_banks[2:])
-        widen_unit("P", 0, 0, (0,))
-        widen_unit("P", 0, 1, (0,))
-        for n, unit in enumerate(head):
-            if unit[:2] != ("P", 0):
-                if unit == ("P", 1, 1):
-                    copy_spread()
-                widen_unit(*unit, (0,))
-            widen_unit(*unit, (1,))
-            if n == 0:
-                turn(*unit, (0,))
-                spread_matmuls()
-                turn(*unit, (1,))
-            else:
-                turn(*unit)
+        for k in range(2):
+            widen("P", 0, k, (0,))
+        widen("P", 0, 0, (1,))
+        turn("P", 0, 0, (0,))
+        spread_matmuls()
+        turn("P", 0, 0, (1,))
+        widen("P", 0, 1, (1,))
+        turn("P", 0, 1)
+        for n in range(2, len(head)):
+            if head[n] == ("P", 1, 1):
+                copy_spread()
+            widen(*head[n])
+            turn(*head[n])
             if n >= EMPTY_LAG:
                 empty(*to_empty[n - EMPTY_LAG])
+
         quantise(("P", 0))
-        quantise_part("F", 0, 0)
+        quantise_unit("F", 0, 0)
         for pair in (2, 3):
-            widen_unit("P", pair, 0)
+            widen("P", pair, 0)
         for unit in to_empty[len(head) - EMPTY_LAG :]:
             empty(*unit)
         for b in (0, 1):
-            first(b, 0, (0,))
+            sum_f(b, 0, 0)
         for pair in (2, 3):
             turn("P", pair, 0)
-        widen_unit("P", 2, 1)
+        widen("P", 2, 1)
         turn("P", 2, 1)
-        quantise_part("F", 1, 0)
-        widen_unit("P", 3, 1)
+        quantise_unit("F", 1, 0)
+        widen("P", 3, 1)
         for b in (2, 3):
-            first(b, 0, (0,))
+            sum_f(b, 0, 0)
         turn("P", 3, 1)
+
         for pair in (2, 3):
             empty("P", pair, 0)
         quantise(("P", 1))
         for pair in (0, 1):
-            quantise_part("F", pair, 1)
+            quantise_unit("F", pair, 1)
         for b in range(4):
-            first(b, 0, (1,))
+            sum_f(b, 0, 1)
         for pair in (2, 3):
             empty("P", pair, 1)
         quantise(("P", 2))
-        widen_unit("F", 2, 0, (0,))
-        for b in range(4):
-            direct_wide(b // 2, 1, b % 2, (0,))
+        widen("F", 2, 0, (0,))
+        for pair in range(2):
+            for u in range(2):
+                sum_p(pair, 1, u, 0)
         quantise(("P", 3))
-        widen_unit("F", 2, 0, (1,))
+        widen("F", 2, 0, (1,))
         for b in range(4):
-            gain(b, 0)
+            gain_f(b, 0)
         for u in range(2):
-            direct_wide(0, 1, u, (1,))
+            sum_p(0, 1, u, 1)
 
         for unit in [("F", 2, 1), ("F", 3, 0), ("F", 3, 1)]:
-            widen_unit(*unit)
+            widen(*unit)
         for unit in [("F", 2, 0), ("F", 2, 1), ("h", 0, 0)]:
             turn(*unit)
         for u in range(2):
-            direct_wide(1, 1, u, (1,))
+            sum_p(1, 1, u, 1)
         turn("h", 1, 0)
-        third = [(b, half) for half in range(2) for b in (4, 5)]
-        wide_gain(0, 1, 0)
+        gain_p(0, 1, 0)
         turn("F", 3, 0)
         empty("F", 2, 0)
         turn("F", 3, 1)
-        wide_gain(0, 1, 1)
-        quantise_part("F", 2, 0)
-        join(0, 1, on_vector=True)
+        gain_p(0, 1, 1)
+
+        third = [(b, c) for c in range(2) for b in (4, 5)]
+        quantise_unit("F", 2, 0)
         empty("F", 2, 1)
         empty("h", 0, 0)
-        for b, half in third[:2]:
-            first(b, half, (0,))
-        quantise_part("F", 2, 1)
+        for b, c in third[:2]:
+            sum_f(b, c, 0)
+        quantise_unit("F", 2, 1)
         empty("F", 3, 0)
-        wide_gain(1, 1, 0)
-        for b, half in third[2:]:
-            first(b, half, (0,))
-        for b, half in third:
-            first(b, half, (1,))
-        empty("F", 3, 1)
-        wide_gain(1, 1, 1)
-        empty("h", 1, 0)
-        join(1, 1)
-        quantise(("F", 3))
-        quantise(("h", 0))
-        quantise(("h", 1))
-
-        left = [((b, 0), (b, 1)) for b in range(8)]
-        thirds = [((2 * j, 2), (2 * j + 1, 2)) for j in range(4)]
-        last = [((2 * j, 3), (2 * j + 1, 3)) for j in range(3)] + [((6, 3),), ((7, 3),)]
-        shared = [left[b] for b in (5,)]
+        gain_p(1, 1, 0)
+        for b, c in third[2:]:
+            sum_f(b, c, 0)
         for b, c in third:
-            gain(b, c)
+            sum_f(b, c, 1)
+        empty("F", 3, 1)
+        gain_p(1, 1, 1)
+        empty("h", 1, 0)
+        for pair in range(2):
+            join(pair, 1)
+        for group in [("F", 3), ("h", 0), ("h", 1)]:
+            quantise(group)
+
+        left = [(b, 1, 0, PASS) for b in range(8)]
+        for b, c in third:
+            gain_f(b, c)
         for u in range(2):
-            direct_wide(3, 0, u)
-            wide_gain(3, 0, u)
+            for k in range(2):
+                sum_p(3, 0, u, k)
+            gain_p(3, 0, u)
         join(3, 0)
-        for b in range(3):
-            second(left[b])
-            finish(left[b])
-        quantise_part("h", 3, 0)
+        for piece in left[:EARLY_TILES]:
+            product(piece)
+            finish(piece)
+        quantise_unit("h", 3, 0)
         for k in range(2):
             turn("h", 2, k)
         for k in range(2):
             empty("h", 2, k)
-        halves = [((3, 0),), ((3, 1),)]
-        for parts in halves:
-            second(parts)
-        for parts in halves:
-            finish(parts)
-        for b in range(4, 7):
-            second(left[b])
-            if b == 4:
+
+        split = [(EARLY_TILES, 1, PAIR * j, PAIR) for j in range(2)]
+        for piece in split:
+            product(piece)
+        for piece in split:
+            finish(piece)
+        for b in range(EARLY_TILES + 1, 7):
+            product(left[b])
+            if b == EARLY_TILES + 1:
                 quantise(("h", 2))
-            if left[b] in shared:
-                finish_shared(left[b])
+            if b == SHARED_TILE:
+                shared_result = finish_shared(left[b])
             else:
                 finish(left[b])
-        direct(6, 1)
-        second(left[7])
-        direct_gain(6, 1)
-        direct(7, 1)
+        sum_p4(6, 1)
+        product(left[7])
+        gain_p4(6, 1)
+        sum_p4(7, 1)
         finish(left[7])
-        for parts in shared:
-            store(parts)
-        rest = thirds + last
-        for n, parts in enumerate(rest):
-            second(parts)
-            if n == 0:
-                direct_gain(7, 1)
-            if n > 0:
-                finish(rest[n - 1], nc.scalar if n % 2 == 1 else nc.sync)
+        nc.scalar.dma_start(out=out_view(left[SHARED_TILE]), in_=shared_result[:])
+
+        rest = [(2 * j, 2, PAIR * pair, PAIR) for pair in (2, 3) for j in range(4)]
+        rest = rest[:-1] + [(b, 1, N - PAIR, PAIR) for b in (6, 7)]
+        product(rest[0])
+        gain_p4(7, 1)
+        for n in range(1, len(rest)):
+            product(rest[n])
+            finish(rest[n - 1], nc.scalar if n % 2 == 1 else nc.sync)
             if n == 1:
-                quantise_part("h", 3, 1)
+                quantise_unit("h", 3, 1)
         finish(rest[-1], nc.scalar)

@@ -121,6 +121,12 @@ def tile_kalman_predicted_covariance_d2_kernel(tc, P_bytes, P_scale, F_bytes, F_
             nc.tensor.matmul(banks["spread"][:, 0:64], lhsT=row_0, rhs=f_row, start=True, stop=True)
             nc.tensor.matmul(banks["spread"][:, 64:72], lhsT=g_rows, rhs=unit_cols[:], start=True, stop=True)
 
+        def warm_up(width):
+            take_bank("warm", [P, width, P])
+            moving = ident[:].unsqueeze(1).to_broadcast([P, width, P])
+            nc.tensor.matmul(banks["warm"][:], lhsT=ident[:], rhs=moving, start=True, stop=True)
+            give_bank("warm")
+
         def copy_spread():
             nc.vector.tensor_copy(out=spread[:], in_=banks["spread"][:, 0:72])
             give_bank("spread")
@@ -296,6 +302,8 @@ def tile_kalman_predicted_covariance_d2_kernel(tc, P_bytes, P_scale, F_bytes, F_
         for k in range(2):
             to_empty.extend([("P", 0, k), ("P", 1, k), f_banks[k]])
         to_empty.extend(f_banks[2:])
+        for n in range(2):
+            warm_up(2)
         for k in range(2):
             widen("P", 0, k, (0,))
         widen("P", 0, 0, (1,))
@@ -309,6 +317,8 @@ def tile_kalman_predicted_covariance_d2_kernel(tc, P_bytes, P_scale, F_bytes, F_
                 copy_spread()
             widen(*head[n])
             turn(*head[n])
+            if n in (2, 4, 6):
+                warm_up(1)
             if n >= EMPTY_LAG:
                 empty(*to_empty[n - EMPTY_LAG])
 

@@ -1,7 +1,6 @@
 from contextlib import ExitStack
 
 import concourse.mybir as mybir
-from concourse.masks import make_identity
 
 N = 1024
 P = 128
@@ -38,7 +37,17 @@ def tile_kalman_predicted_covariance_d2_kernel(tc, P_bytes, P_scale, F_bytes, F_
         f_row = small[:, 0:64]
         g_rows = small[:, 64:P].bitcast(BF16)
         ident = keep.tile([P, P], F32, name="ident")
-        make_identity(nc, ident[:])
+        zeros = keep.tile([P, P], F32, name="zeros")
+        nc.gpsimd.memset(zeros[:], 0.0)
+        nc.gpsimd.affine_select(
+            out=ident[:],
+            in_=zeros[:],
+            compare_op=mybir.AluOpType.not_equal,
+            fill=1.0,
+            base=0,
+            pattern=[[-1, P]],
+            channel_multiplier=1,
+        )
 
         p_rows = P_bytes.rearrange("(c p u e) j -> p c u e j", c=2, u=2, e=2)
         f_rows = F_bytes.rearrange("(h e p) j -> p h e j", h=4, e=2)
@@ -123,8 +132,8 @@ def tile_kalman_predicted_covariance_d2_kernel(tc, P_bytes, P_scale, F_bytes, F_
 
         def warm_up(width):
             take_bank("warm", [P, width, P])
-            moving = ident[:].unsqueeze(1).to_broadcast([P, width, P])
-            nc.tensor.matmul(banks["warm"][:], lhsT=ident[:], rhs=moving, start=True, stop=True)
+            moving = zeros[:].unsqueeze(1).to_broadcast([P, width, P])
+            nc.tensor.matmul(banks["warm"][:], lhsT=zeros[:], rhs=moving, start=True, stop=True)
             give_bank("warm")
 
         def copy_spread():

@@ -316,8 +316,8 @@ def tile_kalman_predicted_covariance_d2_kernel(tc, P_bytes, P_scale, F_bytes, F_
         for k in range(2):
             widen("P", 0, k, (0,))
         widen("P", 0, 0, (1,))
-        turn("P", 0, 0, (0,))
         spread_matmuls()
+        turn("P", 0, 0, (0,))
         turn("P", 0, 0, (1,))
         widen("P", 0, 1, (1,))
         turn("P", 0, 1)

@@ -426,28 +426,30 @@ def tile_kalman_predicted_covariance_d2_kernel(tc, P_bytes, P_scale, F_bytes, F_
             product(piece)
         for piece in split:
             finish(piece)
-        for b in range(EARLY_TILES + 1, 7):
-            product(left[b])
-            if b == EARLY_TILES + 1:
-                quantise(("h", 2))
-            if b == SHARED_TILE:
-                shared_result = finish_shared(left[b])
-            else:
-                finish(left[b])
-        sum_p4(6, 1)
-        product(left[7])
-        gain_p4(6, 1)
-        sum_p4(7, 1)
-        finish(left[7])
-        nc.scalar.dma_start(out=out_view(left[SHARED_TILE]), in_=shared_result[:])
-
         rest = [(2 * j, 2, PAIR * pair, PAIR) for pair in (2, 3) for j in range(4)]
         rest = rest[:-1] + [(b, 1, N - PAIR, PAIR) for b in (6, 7)]
+        product(left[4])
+        quantise(("h", 2))
+        finish(left[4])
+        product(left[SHARED_TILE])
+        shared_result = finish_shared(left[SHARED_TILE])
+        sum_p4(6, 1)
         product(rest[0])
+        gain_p4(6, 1)
+        product(rest[1])
+        finish(rest[0])
+        product(rest[2])
+        finish(rest[1])
+        nc.scalar.dma_start(out=out_view(left[SHARED_TILE]), in_=shared_result[:])
+        sum_p4(7, 1)
+        finish(rest[2])
+
+        last = [left[6], left[7]] + rest[3:]
+        product(last[0])
         gain_p4(7, 1)
-        for n in range(1, len(rest)):
-            product(rest[n])
-            finish(rest[n - 1], nc.scalar if n % 2 == 1 else nc.sync)
+        for n in range(1, len(last)):
+            product(last[n])
+            finish(last[n - 1], nc.scalar if n % 2 == 1 else nc.sync)
             if n == 1:
                 quantise_unit("h", 3, 1)
-        finish(rest[-1], nc.scalar)
+        finish(last[-1], nc.sync)

from contextlib import ExitStack

import concourse.mybir as mybir

N = 1024
P = 128
PASS = 512
PAIR = 256
FLOPS = 2 * 2 * N * N * N

F32 = mybir.dt.float32
BF16 = mybir.dt.bfloat16
U32 = mybir.dt.uint32
U8 = mybir.dt.uint8
FP8 = mybir.dt.float8_e4m3fn
FP8X4 = mybir.dt.float8_e4m3fn_x4
MULT = mybir.AluOpType.mult
ADD = mybir.AluOpType.add
COPY = mybir.ActivationFunctionType.Copy

LOADS = [("P", 0), ("P", 1), ("F", 0), ("F", 1), ("P", 2), ("P", 3), ("F", 2), ("F", 3)]
ON_SCALAR = [("P", 0, 0), ("P", 1, 0), ("P", 1, 1), ("F", 0, 0), ("P", 2, 0), ("F", 3, 1)]
EMPTY_LAG = 4
EARLY_TILES = 3
SHARED_TILE = 5


def tile_kalman_predicted_covariance_d2_kernel(tc, P_bytes, P_scale, F_bytes, F_scale, g, Q, out):
    nc = tc.nc
    with ExitStack() as ctx:
        keep = ctx.enter_context(tc.tile_pool(name="keep", bufs=1))
        psum = ctx.enter_context(tc.psum_pool(name="psum", bufs=1))
        ctx.enter_context(tc.manual_schedule())

        small = keep.tile([P, P], F32, name="small")
        nc.gpsimd.memset(small[:], 0.0)
        f_row = small[:, 0:64]
        g_rows = small[:, 64:P].bitcast(BF16)
        ident = keep.tile([P, P], F32, name="ident")
        zeros = keep.tile([P, P], F32, name="zeros")
        nc.gpsimd.memset(zeros[:], 0.0)
        nc.gpsimd.affine_select(
            out=ident[:],
            in_=zeros[:],
            compare_op=mybir.AluOpType.not_equal,
            fill=1.0,
            base=0,
            pattern=[[-1, P]],
            channel_multiplier=1,
        )

        p_rows = P_bytes.rearrange("(c p u e) j -> p c u e j", c=2, u=2, e=2)
        f_rows = F_bytes.rearrange("(h e p) j -> p h e j", h=4, e=2)
        p_scale_rows = P_scale.rearrange("(c p t) b -> p c (t b)", c=2, t=4)
        p_scale = {}

        def load_p_scales(queue, c):
            part = keep.tile([P, 32], F32, name="p_scale%d" % c)
            queue.dma_start(out=part[:], in_=p_scale_rows[:, c, :])
            for u in range(2):
                p_scale[2 * c + u] = part[:, 16 * u : 16 * u + 16]

        load_p_scales(nc.scalar, 0)
        nc.scalar.dma_start(out=f_row[0:1, :], in_=F_scale.rearrange("(o b) c -> o (b c)", o=1))
        nc.scalar.dma_start(out=g_rows[0:8, :], in_=g.rearrange("(b p) -> b p", p=P))

        raw = {}
        for kind, pair in LOADS:
            if (kind, pair) == ("P", 2):
                load_p_scales(nc.sync, 1)
            part = keep.tile([P, 2, N], U8, name="bytes_%s%d" % (kind, pair))
            rows = p_rows[:, pair // 2, pair % 2] if kind == "P" else f_rows[:, pair]
            if (kind, pair) == LOADS[0]:
                for e in range(2):
                    nc.sync.dma_start(out=part[:, e, :], in_=rows[:, e, :])
            else:
                nc.sync.dma_start(out=part[:], in_=rows)
            raw[(kind, pair)] = part

        g_first = keep.tile([P, PASS], BF16, name="g_first")
        nc.sync.dma_start(out=g_first[:], in_=g[0:PASS].partition_broadcast(P))
        q_rows = Q.rearrange("(b p) n -> p b n", p=P)
        q_tiles = []
        for pair in range(4):
            part = keep.tile([P, 2, N], BF16, name="q%d" % pair)
            nc.sync.dma_start(out=part[:], in_=q_rows[:, 2 * pair : 2 * pair + 2, :])
            q_tiles.append(part)
        g_last = keep.tile([P, PAIR], BF16, name="g_last")
        nc.sync.dma_start(out=g_last[:], in_=g[N - PAIR : N].partition_broadcast(P))
        g_free = {0: g_first[:, 0:PAIR], 1: g_first[:, PAIR:PASS], 3: g_last[:]}

        unit_cols = keep.tile([P, 8], BF16, name="unit_cols")
        nc.scalar.activation(out=unit_cols[:], in_=ident[:, 0:8], func=COPY)

        spread = keep.tile([P, 72], F32, name="spread")
        g_col = spread[:, 64:72]

        grouped = {}
        codes = {}
        for kind in ["P", "F", "h"]:
            for n in range(4):
                name = "%s%d" % (kind, n)
                words = keep.tile([P, PASS], U32, name="codes_" + name, align_bytes=256)
                scales = keep.tile([P, PASS], U8, name="scales_" + name, align_bytes=256)
                codes[(kind, n)] = (words, scales)
                grouped[(kind, n)] = keep.tile([P, 4 * PASS], BF16, name="grouped_" + name, align_bytes=64)

        def place(kind, pair, k):
            if kind == "P" or (kind == "h" and pair < 2):
                return (kind, 2 * (pair // 2) + k), PAIR * (pair % 2)
            return (kind, pair), PAIR * k

        free = list(range(8))
        taken = {}
        banks = {}

        def take_bank(key, shape):
            i = free[0]
            free.remove(i)
            taken[key] = i
            bank = psum.tile(shape, F32, name="bank%d" % i, tag="bank%d" % i)
            banks[key] = bank

        def give_bank(key):
            free.append(taken[key])

        def spread_matmuls():
            take_bank("spread", [P, PASS])
            row_0 = ident[:, 0:1].to_broadcast([P, P])
            nc.tensor.matmul(banks["spread"][:, 0:64], lhsT=row_0, rhs=f_row, start=True, stop=True)
            nc.tensor.matmul(banks["spread"][:, 64:72], lhsT=g_rows, rhs=unit_cols[:], start=True, stop=True)

        def warm_up(width):
            take_bank("warm", [P, width, P])
            moving = zeros[:].unsqueeze(1).to_broadcast([P, width, P])
            nc.tensor.matmul(banks["warm"][:], lhsT=zeros[:], rhs=moving, start=True, stop=True)
            give_bank("warm")

        def copy_spread():
            nc.vector.tensor_copy(out=spread[:], in_=banks["spread"][:, 0:72])
            give_bank("spread")

        wide = {}

        def in_order(kind, pair, k, e):
            return e == 1 and (kind, pair, k) in ON_SCALAR

        def widen(kind, pair, k, tiles=(0, 1)):
            for e in tiles:
                tile = keep.tile([P, PASS], BF16, name="wide_%s%d%d%d" % (kind, pair, k, e), align_bytes=64)
                wide[(kind, pair, k, e)] = tile
                by_u = tile[:].rearrange("p (u c q x) -> p c q u x", u=2, c=4, x=2)
                for c in range(4):
                    block = 4 * k + c
                    src = raw[(kind, pair)][:, e, P * block : P * block + P].bitcast(FP8)
                    if kind == "P":
                        col = p_scale[pair][:, 8 * e + block : 8 * e + block + 1]
                    else:
                        col = spread[:, 16 * pair + 8 * e + block : 16 * pair + 8 * e + block + 1]
                    if in_order(kind, pair, k, e):
                        nc.scalar.activation(out=tile[:, P * c : P * c + P], in_=src, func=COPY, scale=col)
                    else:
                        nc.vector.tensor_scalar(out=by_u[:, c], in0=src, scalar1=col, scalar2=None, op0=MULT)

        def turn(kind, pair, k, tiles=(0, 1)):
            unit = (kind, pair, k)
            if 0 in tiles:
                take_bank(unit, [P, 2, 2, P])
            for e in tiles:
                words = wide[(kind, pair, k, e)][:].bitcast(F32)
                for u in range(2):
                    if in_order(kind, pair, k, e):
                        src = words[:, u : 2 * P : 2]
                    else:
                        src = words[:, P * u : P * u + P]
                    nc.tensor.transpose(banks[unit][:, e, u, :], src, ident[:])

        def unit_words(kind, pair, k):
            group, col = place(kind, pair, k)
            return grouped[group][:].bitcast(F32)[:, 2 * col : 2 * col + 2 * PAIR]

        def empty(kind, pair, k):
            unit = (kind, pair, k)
            dst = unit_words(kind, pair, k).rearrange("p (e r u) -> p e r u", e=2, u=2)
            nc.scalar.copy(out=dst, in_=banks[unit][:].rearrange("p e u r -> p e r u"))
            give_bank(unit)

        def quantise(group, cols=slice(0, PASS)):
            words, scales = codes[group]
            values = grouped[group][:, 4 * cols.start : 4 * cols.stop]
            nc.vector.quantize_mx(out=words[:, cols].bitcast(FP8X4), scales=scales[:, cols], in_=values)

        def quantise_unit(kind, pair, k):
            group, col = place(kind, pair, k)
            quantise(group, slice(col, col + PAIR))

        def one_pass(dst, stationary, moving, start, stop):
            lhs_words, lhs_scales = codes[stationary[0]]
            rhs_words, rhs_scales = codes[moving[0]]
            nc.tensor.matmul_mx(
                out=dst,
                lhsT=lhs_words[:, stationary[1]].bitcast(FP8X4),
                lhsT_scale=lhs_scales[:, stationary[1]],
                rhs=rhs_words[:, moving[1]].bitcast(FP8X4),
                rhs_scale=rhs_scales[:, moving[1]],
                start=start,
                stop=stop,
            )

        def f_tile(b, k):
            col = PAIR * k + P * (b % 2)
            return ("F", b // 2), slice(col, col + P)

        def p_place(c, t, k):
            return ("P", 2 * c + k), slice(P * t, P * t + P)

        def sum_f(b, c, k):
            key = ("sum_f", b, c)
            if k == 0:
                take_bank(key, [P, PASS])
            one_pass(banks[key][:], f_tile(b, k), (("P", 2 * c + k), slice(0, PASS)), k == 0, k == 1)

        def gain_f(b, c):
            key = ("sum_f", b, c)
            tile = keep.tile([P, PASS], BF16, name="h_wide%d%d" % (b, c), align_bytes=64)
            wide[("h", b // 2, c, b % 2)] = tile
            dst = tile[:].rearrange("p (u q x) -> p u q x", u=2, x=2)
            src = banks[key][:].rearrange("p (u x q) -> p u q x", u=2, x=2)
            nc.scalar.activation(out=dst, in_=src, func=COPY, scale=g_col[:, b : b + 1])
            give_bank(key)

        def sum_p(pair, c, u, k):
            key = ("sum_p", pair, c, u)
            if k == 0:
                take_bank(key, [P, 2, PAIR])
            moving = (("F", pair), slice(PAIR * k, PAIR * k + PAIR))
            for x in range(2):
                one_pass(banks[key][:, x, :], p_place(c, 2 * u + x, k), moving, (k, x) == (0, 0), (k, x) == (1, 1))

        halves = {}

        def gain_p(pair, c, u):
            key = ("sum_p", pair, c, u)
            if u == 0:
                halves[(pair, c)] = keep.tile([P, 4 * PAIR], BF16, name="halves%d%d" % (pair, c), align_bytes=64)
            dst = halves[(pair, c)][:, PASS * u : PASS * u + PASS].rearrange("p (n x) -> p n x", x=2)
            factor = g_free[pair].unsqueeze(2).to_broadcast([P, PAIR, 2])
            nc.vector.tensor_tensor(out=dst, in0=banks[key][:].rearrange("p x n -> p n x"), in1=factor, op=MULT)
            give_bank(key)

        def join(pair, c):
            dst = unit_words("h", pair, c).rearrange("p (n u) -> p n u", u=2)
            nc.scalar.copy(out=dst, in_=halves[(pair, c)][:].bitcast(F32).rearrange("p (u n) -> p n u", u=2))

        def sum_p4(b, c):
            key = ("sum_p4", b, c)
            take_bank(key, [P, 4, P])
            for k in range(2):
                for t in range(4):
                    one_pass(banks[key][:, t, :], p_place(c, t, k), f_tile(b, k), (k, t) == (0, 0), (k, t) == (1, 3))

        def gain_p4(b, c):
            key = ("sum_p4", b, c)
            group, col = place("h", b // 2, c)
            col = col + P * (b % 2)
            dst = grouped[group][:, 4 * col : 4 * col + PASS].rearrange("p (r t) -> p r t", t=4)
            factor = g_free[b // 2][:, P * (b % 2) : P * (b % 2) + P].unsqueeze(2).to_broadcast([P, P, 4])
            nc.vector.tensor_tensor(out=dst, in0=banks[key][:].rearrange("p t r -> p r t"), in1=factor, op=MULT)
            give_bank(key)

        def product(piece):
            b, tiles, col, width = piece
            take_bank(piece, [P, tiles, width])
            for j in range(tiles):
                for k in range(2):
                    group, first = place("h", col // PAIR, k)
                    one_pass(banks[piece][:, j, :], f_tile(b + j, k), (group, slice(first, first + width)), k == 0, k == 1)

        def out_view(piece):
            b, tiles, col, width = piece
            return out[P * b : P * b + P * tiles, col : col + width].rearrange("(j p) n -> p j n", p=P)

        def finish(piece, queue=nc.sync):
            b, tiles, col, width = piece
            result = keep.tile([P, tiles, width], F32, name="res_%d_%d" % (b, col))
            for j in range(tiles):
                nc.vector.scalar_tensor_tensor(
                    out=result[:, j, :],
                    in0=banks[piece][:, j, :],
                    scalar=g_col[:, b + j : b + j + 1],
                    in1=q_tiles[(b + j) // 2][:, (b + j) % 2, col : col + width],
                    op0=MULT,
                    op1=ADD,
                )
            give_bank(piece)
            queue.dma_start(out=out_view(piece), in_=result[:])

        def finish_shared(piece):
            b, tiles, col, width = piece
            scaled = keep.tile([P, tiles, width], F32, name="scaled")
            nc.scalar.activation(out=scaled[:, 0, :], in_=banks[piece][:, 0, :], func=COPY, scale=g_col[:, b : b + 1])
            give_bank(piece)
            result = keep.tile([P, tiles, width], F32, name="res_shared")
            noise = q_tiles[b // 2][:, b % 2, col : col + width]
            nc.gpsimd.tensor_tensor(out=result[:, 0, :], in0=scaled[:, 0, :], in1=noise, op=ADD)
            return result

        head = [(kind, pair, k) for kind in ["P", "F"] for pair in range(2) for k in range(2)]
        f_banks = [("F", pair, k) for k in range(2) for pair in range(2)]
        to_empty = []
        for k in range(2):
            to_empty.extend([("P", 0, k), ("P", 1, k), f_banks[k]])
        to_empty.extend(f_banks[2:])
        for n in range(2):
            warm_up(2)
        for k in range(2):
            widen("P", 0, k, (0,))
        widen("P", 0, 0, (1,))
        spread_matmuls()
        turn("P", 0, 0, (0,))
        turn("P", 0, 0, (1,))
        widen("P", 0, 1, (1,))
        turn("P", 0, 1)
        for n in range(2, len(head)):
            if head[n] == ("P", 1, 1):
                copy_spread()
            widen(*head[n])
            turn(*head[n])
            if n in (2, 4, 6):
                warm_up(1)
            if n >= EMPTY_LAG:
                empty(*to_empty[n - EMPTY_LAG])

        quantise(("P", 0))
        quantise_unit("F", 0, 0)
        for pair in (2, 3):
            widen("P", pair, 0)
        for unit in to_empty[len(head) - EMPTY_LAG :]:
            empty(*unit)
        for b in (0, 1):
            sum_f(b, 0, 0)
        for pair in (2, 3):
            turn("P", pair, 0)
        widen("P", 2, 1)
        turn("P", 2, 1)
        quantise_unit("F", 1, 0)
        widen("P", 3, 1)
        for b in (2, 3):
            sum_f(b, 0, 0)
        turn("P", 3, 1)

        for pair in (2, 3):
            empty("P", pair, 0)
        quantise(("P", 1))
        for pair in (0, 1):
            quantise_unit("F", pair, 1)
        for b in range(4):
            sum_f(b, 0, 1)
        for pair in (2, 3):
            empty("P", pair, 1)
        quantise(("P", 2))
        widen("F", 2, 0, (0,))
        for pair in range(2):
            for u in range(2):
                sum_p(pair, 1, u, 0)
        quantise(("P", 3))
        widen("F", 2, 0, (1,))
        for b in range(4):
            gain_f(b, 0)
        for u in range(2):
            sum_p(0, 1, u, 1)

        for unit in [("F", 2, 1), ("F", 3, 0), ("F", 3, 1)]:
            widen(*unit)
        for unit in [("F", 2, 0), ("F", 2, 1), ("h", 0, 0)]:
            turn(*unit)
        for u in range(2):
            sum_p(1, 1, u, 1)
        turn("h", 1, 0)
        gain_p(0, 1, 0)
        turn("F", 3, 0)
        empty("F", 2, 0)
        turn("F", 3, 1)
        gain_p(0, 1, 1)

        third = [(b, c) for c in range(2) for b in (4, 5)]
        quantise_unit("F", 2, 0)
        empty("F", 2, 1)
        empty("h", 0, 0)
        for b, c in third[:2]:
            sum_f(b, c, 0)
        quantise_unit("F", 2, 1)
        empty("F", 3, 0)
        gain_p(1, 1, 0)
        for b, c in third[2:]:
            sum_f(b, c, 0)
        for b, c in third:
            sum_f(b, c, 1)
        empty("F", 3, 1)
        gain_p(1, 1, 1)
        empty("h", 1, 0)
        for pair in range(2):
            join(pair, 1)
        for group in [("F", 3), ("h", 0), ("h", 1)]:
            quantise(group)

        left = [(b, 1, 0, PASS) for b in range(8)]
        for b, c in third:
            gain_f(b, c)
        for u in range(2):
            for k in range(2):
                sum_p(3, 0, u, k)
            gain_p(3, 0, u)
        join(3, 0)
        for piece in left[:EARLY_TILES]:
            product(piece)
            finish(piece)
        quantise_unit("h", 3, 0)
        for k in range(2):
            turn("h", 2, k)
        for k in range(2):
            empty("h", 2, k)

        split = [(EARLY_TILES, 1, PAIR * j, PAIR) for j in range(2)]
        for piece in split:
            product(piece)
        for piece in split:
            finish(piece)
        rest = [(2 * j, 2, PAIR * pair, PAIR) for pair in (2, 3) for j in range(4)]
        rest = rest[:-1] + [(b, 1, N - PAIR, PAIR) for b in (6, 7)]
        product(left[4])
        quantise(("h", 2))
        finish(left[4])
        product(left[SHARED_TILE])
        shared_result = finish_shared(left[SHARED_TILE])
        sum_p4(6, 1)
        product(rest[0])
        gain_p4(6, 1)
        product(rest[1])
        finish(rest[0])
        product(rest[2])
        finish(rest[1])
        nc.scalar.dma_start(out=out_view(left[SHARED_TILE]), in_=shared_result[:])
        sum_p4(7, 1)
        finish(rest[2])

        last = [left[6], left[7]] + rest[3:]
        product(last[0])
        gain_p4(7, 1)
        for n in range(1, len(last)):
            product(last[n])
            finish(last[n - 1], nc.scalar if n % 2 == 1 else nc.sync)
            if n == 1:
                quantise_unit("h", 3, 1)
        finish(last[-1], nc.sync)
